import numpy as np
import ml_dtypes


def mxq(x, axis, fmt="e4m3"):
    dtype, down = {"e4m3": (ml_dtypes.float8_e4m3fn, 7), "e5m2": (ml_dtypes.float8_e5m2, 14)}[fmt]
    v = np.moveaxis(np.asarray(x, np.float32).astype(ml_dtypes.bfloat16).astype(np.float64), axis, -1)
    blocks = v.reshape(v.shape[:-1] + (-1, 32))
    amax = np.abs(blocks).max(-1, keepdims=True)
    byte = np.maximum(np.where(amax > 0, np.frexp(amax)[1] - 1 + 127, 0) - down, 1)
    scale = np.exp2(byte - 127.0)
    codes = (blocks / scale).astype(np.float32).astype(dtype).astype(np.float64)
    return np.moveaxis((codes * scale).reshape(v.shape), -1, axis)


WIDE = False


def mx_kscale(k):
    if not WIDE:
        return np.ones(k)
    levels = np.array([18, -18])
    if k % 512:
        return np.exp2(np.random.permutation(np.resize(levels, k // 32))).repeat(32)
    a = np.empty((k // 512, 16))
    for p in range(k // 512):
        a[p, :8] = np.random.permutation(np.resize(levels, 8))
        for g in range(8):
            far = levels[np.abs(levels - a[p, g]) >= 10]
            a[p, g + 8] = far[np.random.randint(len(far))]
    return np.exp2(a.ravel()).repeat(32)


def f64(x):
    return np.asarray(x).astype(np.float64)


def striped(idx):
    return np.tile(np.asarray(idx).reshape(-1, 16).T, (8, 1)).astype(np.uint16)


def unstriped(offs):
    return offs[:16].T.reshape(-1).astype(np.int64)

def planes(y):
    n, m = y.shape
    v = y.astype(np.float32).astype(ml_dtypes.bfloat16).astype(np.float64).reshape(n // 32, 32, m)
    top = np.abs(v).max(1)
    byte = np.clip(np.where(top > 0, np.frexp(top)[1] - 1 + 127 - 7, 1), 1, 254)
    codes = (v * np.exp2(127.0 - byte)[:, None, :]).reshape(n, m).astype(np.float32).astype(ml_dtypes.float8_e4m3fn).view(np.uint8)
    words = codes.reshape(n // 512, 128, 4, m).transpose(0, 1, 3, 2)
    return np.ascontiguousarray(words), np.ascontiguousarray(byte.astype(np.uint8).reshape(n // 512, 16, m))


def setup_inputs():
    n = np.random.standard_normal
    uni = np.random.uniform
    idx = np.random.permutation(2048)[:512]
    f_r = mx_kscale(512)
    return {
        "xT": (n((512, 512)) * f_r[None, :]).astype(np.float32),
        "G": (n((512, 512)) / np.sqrt(512) / f_r[:, None]).astype(np.float32),
        "acc": np.tile(uni(0.5, 2.0, 2048), (128, 1)).astype(np.float32),
        "offs": striped(idx),
    }


def reference(xT, G, acc, offs):
    idx = unstriped(offs)
    acc_i = f64(acc)[:1][:, idx]
    dw = mxq(f64(xT), 1, "e4m3") @ mxq(f64(G), 0, "e5m2")
    dt = dw.T
    q = (np.square(dt)).sum(-1, keepdims=True)
    qr = q.T
    na = acc_i + qr / 512.0
    up = dw / (np.sqrt(na) + 0.001)
    out_0 = np.zeros((512, 2048))
    out_0[:, idx] = up
    nac = na.T
    out_1 = nac.T
    return (out_0, out_1,) + planes(out_0)

@@ -1,0 +1,226 @@
+import math
+from contextlib import ExitStack
+
+import concourse.mybir as mybir
+from concourse.masks import make_identity
+
+F32 = mybir.dt.float32
+BF16 = mybir.dt.bfloat16
+I32 = mybir.dt.int32
+U32 = mybir.dt.uint32
+U16 = mybir.dt.uint16
+U8 = mybir.dt.uint8
+E4M3 = mybir.dt.float8_e4m3fn_x4
+E5M2 = mybir.dt.float8_e5m2_x4
+ACT = mybir.ActivationFunctionType
+ALU = mybir.AluOpType
+
+P = 128
+LANES = 4
+D = 512
+R = 512
+SLOTS = 512
+TABLE = 2048
+HALF = SLOTS // 2
+CHUNK = 512
+EPS = 0.001
+
+FLOPS = 2 * D * R * SLOTS
+BYTES = 4 * (D * R + R * SLOTS + TABLE) + 2 * P * SLOTS // 16 + 4 * (D * TABLE + SLOTS) + D * TABLE + 16 * TABLE
+
+
+def tile_attend_grwada_pl_kernel(tc, xT, G, acc, offs, out_0, out_1, out_2, out_3):
+    nc = tc.nc
+    with ExitStack() as ctx:
+        sb = ctx.enter_context(tc.tile_pool(name="sb", bufs=1))
+        ps = ctx.enter_context(tc.psum_pool(name="ps", bufs=1))
+
+        def bank(b, name):
+            return ps.tile([P, 512], F32, name=name, tag="bank%d" % b)
+
+        x_rows = xT.rearrange("(m t) r -> m t r", t=LANES)
+        x_raw = []
+        for t in range(LANES):
+            raw = sb.tile([P, R], F32, name="x_raw%d" % t)
+            nc.sync.dma_start(raw[:], x_rows[:, t, :])
+            x_raw.append(raw)
+        offsets = sb.tile([P, SLOTS // 16], U16, name="offsets")
+        nc.sync.dma_start(offsets[:], offs)
+        g_rows = G.rearrange("(p j) i -> p j i", j=LANES)
+        g_raw = []
+        for h in range(2):
+            raw = sb.tile([P, LANES, HALF], F32, name="g_raw%d" % h)
+            nc.sync.dma_start(raw[:], g_rows[:, :, h * HALF:(h + 1) * HALF])
+            g_raw.append(raw)
+
+        warm = sb.tile([P, 1], F32, name="warm")
+        nc.gpsimd.memset(warm[:], 1.0)
+        warm_out = sb.tile([P, 1], F32, name="warm_out")
+        nc.scalar.activation(warm_out[:], warm[:], ACT.Sqrt)
+        acc_win = sb.tile([P, TABLE], F32, name="acc_win")
+        nc.vector.memset(acc_win[:], 0.0)
+        nc.scalar.dma_start(acc_win[0:1, :], acc[0:1, :])
+        ident = sb.tile([P, P], F32, name="ident")
+        make_identity(nc, ident[:])
+        q_pad = sb.tile([P, P], F32, name="q_pad")
+        nc.gpsimd.memset(q_pad[:], 0.0)
+        win = [sb.tile([P, TABLE], F32, name="win0")]
+        nc.vector.memset(win[0][:], 0.0)
+
+        acc_g = sb.tile([P, SLOTS], F32, name="acc_g")
+        nc.vector.tensor_copy(acc_g[:], acc_win[:].indirect(offsets[:]))
+
+        x_codes = sb.tile([P, D], U32, name="x_codes", align_bytes=64)
+        x_scales = sb.tile([P, D], U8, name="x_scales", align_bytes=64)
+        x_banks = (0, 1, 7, 5)
+        for t in range(LANES):
+            xb = sb.tile([P, 2, P, 2], BF16, name="xb%d" % t)
+            nc.scalar.copy(xb[:], x_raw[t][:].rearrange("m (p u e) -> m u p e", u=2, e=2))
+            words = xb[:].rearrange("m u p e -> m (u p e)").bitcast(F32)
+            xt = bank(x_banks[t], "xt%d" % t)
+            for u in range(2):
+                nc.tensor.transpose(xt[:, u * P:(u + 1) * P], words[:, u * P:(u + 1) * P], ident[:])
+            xg = sb.tile([P, LANES * P], BF16, name="xg%d" % t, align_bytes=64)
+            nc.scalar.copy(
+                xg[:].bitcast(F32).rearrange("p (m u) -> p m u", u=2),
+                xt[:, 0:2 * P].rearrange("p (u m) -> p m u", u=2))
+            cols = slice(t * P, (t + 1) * P)
+            nc.vector.quantize_mx(out=x_codes[:, cols].bitcast(E4M3), scales=x_scales[:, cols], in_=xg[:])
+
+        acc_t = bank(6, "acc_t")
+        for c in range(4):
+            nc.tensor.transpose(acc_t[:, c * P:(c + 1) * P], acc_g[:, c * P:(c + 1) * P], ident[:])
+        acc_pad = sb.tile([P, P], F32, name="acc_pad")
+        nc.scalar.copy(acc_pad[:].rearrange("p (k c) -> p k c", c=4),
+                       acc_t[:].rearrange("p (c k) -> p k c", c=4)[:, 0:P // 4, :])
+
+        dw_sb = []
+        dw_ps = []
+        for h in range(2):
+            gg = sb.tile([P, HALF * LANES], BF16, name="gg%d" % h, align_bytes=64,
+                         tag="late_w1" if h else "gg0")
+            nc.vector.tensor_copy(
+                gg[:].rearrange("p (c i j) -> p c j i", i=4, j=LANES),
+                g_raw[h][:].rearrange("p j (c i) -> p c j i", i=4))
+            g_codes = sb.tile([P, HALF], U32, name="g_codes%d" % h, align_bytes=64)
+            g_scales = sb.tile([P, HALF], U8, name="g_scales%d" % h, align_bytes=64)
+            nc.vector.quantize_mx(out=g_codes[:].bitcast(E5M2), scales=g_scales[:], in_=gg[:])
+            for k in range(2):
+                c = 2 * h + k
+                cols = slice(k * P, (k + 1) * P)
+                dw = bank(2 + c, "dw%d" % c)
+                nc.tensor.matmul_mx(
+                    out=dw[:], lhsT=g_codes[:, cols].bitcast(E5M2), lhsT_scale=g_scales[:, cols],
+                    rhs=x_codes[:].bitcast(E4M3), rhs_scale=x_scales[:], start=True, stop=True)
+                dw_ps.append(dw)
+
+        def late_window(t):
+            w = sb.tile([P, TABLE], F32, name="win%d" % t, tag="late_w%d" % t, align_bytes=64)
+            nc.gpsimd.memset(w[:], 0.0)
+            win.append(w)
+
+        late_window(1)
+
+        r_ps = bank(6, "r_ps")
+        r_row = sb.tile([P, SLOTS], F32, name="r_row")
+        up_ps = [bank(0, "up_ps0"), bank(1, "up_ps1")]
+        by_c = {}
+
+        def turn(t, c):
+            nc.tensor.transpose(up_ps[t][:, c * P:(c + 1) * P], by_c[c][:, t * P:(t + 1) * P], ident[:])
+
+        def scatter_half(t, h, tag):
+            half = slice(h * HALF, (h + 1) * HALF)
+            src = sb.tile([P, HALF], F32, name="up_half%d%d" % (t, h), tag=tag)
+            nc.scalar.copy(src[:], up_ps[t][:, half])
+            return lambda: nc.vector.tensor_tensor(
+                win[t][:].indirect(offsets[:, h * HALF // 16:(h + 1) * HALF // 16]),
+                src[:], r_row[:, half], ALU.mult)
+
+        for h in range(2):
+            half = slice(h * HALF, (h + 1) * HALF)
+            root = sb.tile([P, 2], F32, name="root%d" % h, tag="root%d" % h)
+            for k in (0, 1):
+                c = 2 * h + k
+                by_c[c] = sb.tile([P, D], F32, name="dw_sb%d" % c)
+                squares = sb.tile([P, D], BF16, name="squares%d" % c)
+                nc.scalar.activation(squares[:], dw_ps[c][:], ACT.Square, scale=math.sqrt(1.0 / D),
+                                     accum_out=q_pad[:, c:c + 1])
+                if c < 3:
+                    nc.vector.tensor_copy(by_c[c][:], dw_ps[c][:])
+            for k in (0, 1):
+                c = 2 * h + k
+                nc.scalar.activation(root[:, k:k + 1], q_pad[:, c:c + 1], ACT.Sqrt, bias=acc_pad[:, c:c + 1])
+            denom = sb.tile([P, 2], F32, name="denom%d" % h, tag="late_w%d" % (2 + h), align_bytes=64)
+            nc.scalar.activation(denom[:], root[:], ACT.Identity, bias=EPS)
+            rinv = sb.tile([P, 2], F32, name="rinv%d" % h)
+            nc.vector.reciprocal(rinv[:], denom[:])
+            if h == 1:
+                scatter_half(1, 0, "root1")()
+                nc.scalar.copy(by_c[3][:], dw_ps[3][:])
+            for k in (0, 1):
+                turn(0, 2 * h + k)
+            scatter = scatter_half(0, h, "up_half0%d" % h)
+            for k in (0, 1):
+                c = 2 * h + k
+                nc.tensor.transpose(r_ps[:, c * P:(c + 1) * P], rinv[:, k:k + 1].to_broadcast([P, P]), ident[:])
+            nc.scalar.copy(r_row[:, half], r_ps[:, half])
+            scatter()
+            for k in (0, 1):
+                turn(1, 2 * h + k)
+        scatter_half(1, 1, "up_half11")()
+
+        late_window(2)
+        late_window(3)
+
+        up_ps.append(bank(2, "up_ps2"))
+        up_ps.append(bank(3, "up_ps3"))
+        up_sb = {}
+        for t in range(2, LANES):
+            for c in range(4):
+                turn(t, c)
+            up_sb[t] = sb.tile([P, SLOTS], F32, name="up_sb%d" % t)
+            nc.scalar.copy(up_sb[t][:], up_ps[t][:])
+
+        na_ps = bank(7, "na_ps")
+        nc.tensor.matmul(na_ps[:, 0:P], q_pad[:], ident[:], start=True, stop=False, is_transpose=True)
+        nc.tensor.matmul(na_ps[:, 0:P], acc_pad[:], ident[:], start=False, stop=True, is_transpose=True)
+        na_rows = sb.tile([32, P], F32, name="na_rows")
+        nc.scalar.copy(na_rows[:], na_ps[0:32, 0:P])
+        nc.sync.dma_start(out_1.rearrange("o (c i) -> (o c) i", c=4), na_rows[0:4, :])
+
+        out_rows = out_0.rearrange("(m t) c -> m t c", t=LANES)
+        chunks = TABLE // CHUNK
+        pairs = [sb.tile([P, 2, CHUNK, 2], BF16, name="pairs%d" % k) for k in range(chunks)]
+
+        def round_lane(engine_copy, t, k):
+            engine_copy(pairs[k][:, t // 2, :, t % 2], win[t][:, k * CHUNK:(k + 1) * CHUNK])
+
+        for t in range(LANES):
+            if t > 1:
+                nc.vector.tensor_tensor(win[t][:].indirect(offsets[:]), up_sb[t][:], r_row[:], ALU.mult)
+            nc.sync.dma_start(out_rows[:, t, :], win[t][:])
+            if t < LANES - 1:
+                for k in range(t // 2, chunks):
+                    round_lane(nc.scalar.copy, t, k)
+
+        words_out = out_2[0].rearrange("p c l -> p (c l)").bitcast(I32)
+        y_scales = sb.tile([P, TABLE], U8, name="y_scales", align_bytes=64)
+        last = LANES - 1
+        round_lane(nc.vector.tensor_copy, last - 1, 0)
+        round_lane(nc.vector.tensor_copy, last, 0)
+        for k in range(1, chunks):
+            round_lane(nc.scalar.copy, last, k)
+        for k in range(chunks):
+            cols = slice(k * CHUNK, (k + 1) * CHUNK)
+            grouped = sb.tile([P, CHUNK * LANES], BF16, name="grouped%d" % k, align_bytes=64)
+            weave = nc.scalar.copy if k == chunks - 1 else nc.vector.tensor_copy
+            weave(grouped[:].bitcast(F32).rearrange("p (c u) -> p c u", u=2),
+                  pairs[k][:].rearrange("p u c e -> p (u c e)").bitcast(F32).rearrange("p (u c) -> p c u", u=2))
+            y_codes = sb.tile([P, CHUNK], U32, name="y_codes%d" % k, align_bytes=64)
+            nc.vector.quantize_mx(out=y_codes[:].bitcast(E4M3), scales=y_scales[:, cols], in_=grouped[:])
+            nc.sync.dma_start(words_out[:, cols], y_codes[:].bitcast(I32))
+        scales_out = out_3[0].bitcast(I32)
+        for q in range(4):
+            queue = nc.scalar if q % 2 else nc.sync
+            queue.dma_start(scales_out[4 * q:4 * q + 4, :], y_scales[32 * q:32 * q + 4, :].bitcast(I32))

@@ -64,8 +64,10 @@ def tile_attend_grwada_pl_kernel(tc, xT, G, acc, offs, out_0, out_1, out_2, out_
         make_identity(nc, ident[:])
         q_pad = sb.tile([P, P], F32, name="q_pad")
         nc.gpsimd.memset(q_pad[:], 0.0)
-        win = [sb.tile([P, TABLE], F32, name="win0")]
-        nc.vector.memset(win[0][:], 0.0)
+        win = {}
+        for t in (0, 1, 3):
+            win[t] = sb.tile([P, TABLE], F32, name="win%d" % t)
+            nc.vector.memset(win[t][:], 0.0)
 
         acc_g = sb.tile([P, SLOTS], F32, name="acc_g")
         nc.vector.tensor_copy(acc_g[:], acc_win[:].indirect(offsets[:]))
@@ -98,8 +100,9 @@ def tile_attend_grwada_pl_kernel(tc, xT, G, acc, offs, out_0, out_1, out_2, out_
         dw_ps = []
         for h in range(2):
             gg = sb.tile([P, HALF * LANES], BF16, name="gg%d" % h, align_bytes=64,
-                         tag="late_w1" if h else "gg0")
-            nc.vector.tensor_copy(
+                         tag="late_w2" if h else "gg0")
+            weave_g = nc.scalar.copy if h else nc.vector.tensor_copy
+            weave_g(
                 gg[:].rearrange("p (c i j) -> p c j i", i=4, j=LANES),
                 g_raw[h][:].rearrange("p j (c i) -> p c j i", i=4))
             g_codes = sb.tile([P, HALF], U32, name="g_codes%d" % h, align_bytes=64)
@@ -117,9 +120,9 @@ def tile_attend_grwada_pl_kernel(tc, xT, G, acc, offs, out_0, out_1, out_2, out_
         def late_window(t):
             w = sb.tile([P, TABLE], F32, name="win%d" % t, tag="late_w%d" % t, align_bytes=64)
             nc.gpsimd.memset(w[:], 0.0)
-            win.append(w)
+            win[t] = w
 
-        late_window(1)
+        late_window(2)
 
         r_ps = bank(6, "r_ps")
         r_row = sb.tile([P, SLOTS], F32, name="r_row")
@@ -151,7 +154,7 @@ def tile_attend_grwada_pl_kernel(tc, xT, G, acc, offs, out_0, out_1, out_2, out_
             for k in (0, 1):
                 c = 2 * h + k
                 nc.scalar.activation(root[:, k:k + 1], q_pad[:, c:c + 1], ACT.Sqrt, bias=acc_pad[:, c:c + 1])
-            denom = sb.tile([P, 2], F32, name="denom%d" % h, tag="late_w%d" % (2 + h), align_bytes=64)
+            denom = sb.tile([P, 2], F32, name="denom%d" % h)
             nc.scalar.activation(denom[:], root[:], ACT.Identity, bias=EPS)
             rinv = sb.tile([P, 2], F32, name="rinv%d" % h)
             nc.vector.reciprocal(rinv[:], denom[:])
@@ -169,9 +172,6 @@ def tile_attend_grwada_pl_kernel(tc, xT, G, acc, offs, out_0, out_1, out_2, out_
             for k in (0, 1):
                 turn(1, 2 * h + k)
         scatter_half(1, 1, "up_half11")()
-
-        late_window(2)
-        late_window(3)
 
         up_ps.append(bank(2, "up_ps2"))
         up_ps.append(bank(3, "up_ps3"))

@@ -24,6 +24,7 @@ TABLE = 2048
 HALF = SLOTS // 2
 CHUNK = 512
 EPS = 0.001
+COL = P - 4
 
 FLOPS = 2 * D * R * SLOTS
 BYTES = 4 * (D * R + R * SLOTS + TABLE) + 2 * P * SLOTS // 16 + 4 * (D * TABLE + SLOTS) + D * TABLE + 16 * TABLE
@@ -39,13 +40,17 @@ def tile_attend_grwada_pl_kernel(tc, xT, G, acc, offs, out_0, out_1, out_2, out_
             return ps.tile([P, 512], F32, name=name, tag="bank%d" % b)
 
         x_rows = xT.rearrange("(m t) r -> m t r", t=LANES)
+        offsets = sb.tile([P, SLOTS // 16], U16, name="offsets")
+        nc.sync.dma_start(offsets[:], offs)
+        acc_win = sb.tile([P, TABLE], F32, name="acc_win")
+        nc.scalar.dma_start(acc_win[P - 1:P, :], acc[0:1, :])
+        nc.vector.memset(acc_win[0:96, :], 0.0)
+        nc.vector.memset(acc_win[96:P - 1, :], 0.0)
         x_raw = []
         for t in range(LANES):
             raw = sb.tile([P, R], F32, name="x_raw%d" % t)
             nc.sync.dma_start(raw[:], x_rows[:, t, :])
             x_raw.append(raw)
-        offsets = sb.tile([P, SLOTS // 16], U16, name="offsets")
-        nc.sync.dma_start(offsets[:], offs)
         g_rows = G.rearrange("(p j) i -> p j i", j=LANES)
         g_raw = []
         for h in range(2):
@@ -57,17 +62,11 @@ def tile_attend_grwada_pl_kernel(tc, xT, G, acc, offs, out_0, out_1, out_2, out_
         nc.gpsimd.memset(warm[:], 1.0)
         warm_out = sb.tile([P, 1], F32, name="warm_out")
         nc.scalar.activation(warm_out[:], warm[:], ACT.Sqrt)
-        acc_win = sb.tile([P, TABLE], F32, name="acc_win")
-        nc.vector.memset(acc_win[:], 0.0)
-        nc.scalar.dma_start(acc_win[0:1, :], acc[0:1, :])
         ident = sb.tile([P, P], F32, name="ident")
         make_identity(nc, ident[:])
         q_pad = sb.tile([P, P], F32, name="q_pad")
         nc.gpsimd.memset(q_pad[:], 0.0)
         win = {}
-        for t in (0, 1, 3):
-            win[t] = sb.tile([P, TABLE], F32, name="win%d" % t)
-            nc.vector.memset(win[t][:], 0.0)
 
         acc_g = sb.tile([P, SLOTS], F32, name="acc_g")
         nc.vector.tensor_copy(acc_g[:], acc_win[:].indirect(offsets[:]))
@@ -75,10 +74,13 @@ def tile_attend_grwada_pl_kernel(tc, xT, G, acc, offs, out_0, out_1, out_2, out_
         x_codes = sb.tile([P, D], U32, name="x_codes", align_bytes=64)
         x_scales = sb.tile([P, D], U8, name="x_scales", align_bytes=64)
         x_banks = (0, 1, 7, 5)
+        xb = {}
+        for t in (2, 3, 0, 1):
+            xb[t] = sb.tile([P, 2, P, 2], BF16, name="xb%d" % t)
+            engine_copy = nc.vector.tensor_copy if t >= 2 else nc.scalar.copy
+            engine_copy(xb[t][:], x_raw[t][:].rearrange("m (p u e) -> m u p e", u=2, e=2))
         for t in range(LANES):
-            xb = sb.tile([P, 2, P, 2], BF16, name="xb%d" % t)
-            nc.scalar.copy(xb[:], x_raw[t][:].rearrange("m (p u e) -> m u p e", u=2, e=2))
-            words = xb[:].rearrange("m u p e -> m (u p e)").bitcast(F32)
+            words = xb[t][:].rearrange("m u p e -> m (u p e)").bitcast(F32)
             xt = bank(x_banks[t], "xt%d" % t)
             for u in range(2):
                 nc.tensor.transpose(xt[:, u * P:(u + 1) * P], words[:, u * P:(u + 1) * P], ident[:])
@@ -94,18 +96,18 @@ def tile_attend_grwada_pl_kernel(tc, xT, G, acc, offs, out_0, out_1, out_2, out_
             nc.tensor.transpose(acc_t[:, c * P:(c + 1) * P], acc_g[:, c * P:(c + 1) * P], ident[:])
         acc_pad = sb.tile([P, P], F32, name="acc_pad")
         nc.scalar.copy(acc_pad[:].rearrange("p (k c) -> p k c", c=4),
-                       acc_t[:].rearrange("p (c k) -> p k c", c=4)[:, 0:P // 4, :])
+                       acc_t[:].rearrange("p (c k) -> p k c", c=4)[:, P - P // 4:P, :])
 
         dw_sb = []
         dw_ps = []
         for h in range(2):
             gg = sb.tile([P, HALF * LANES], BF16, name="gg%d" % h, align_bytes=64,
-                         tag="late_w2" if h else "gg0")
-            weave_g = nc.scalar.copy if h else nc.vector.tensor_copy
-            weave_g(
+                         tag="late_w0" if h else "gg0")
+            nc.vector.tensor_copy(
                 gg[:].rearrange("p (c i j) -> p c j i", i=4, j=LANES),
                 g_raw[h][:].rearrange("p j (c i) -> p c j i", i=4))
-            g_codes = sb.tile([P, HALF], U32, name="g_codes%d" % h, align_bytes=64)
+            g_codes = sb.tile([P, HALF], U32, name="g_codes%d" % h, align_bytes=64,
+                              tag="late_w1" if h else "g_codes0")
             g_scales = sb.tile([P, HALF], U8, name="g_scales%d" % h, align_bytes=64)
             nc.vector.quantize_mx(out=g_codes[:].bitcast(E5M2), scales=g_scales[:], in_=gg[:])
             for k in range(2):
@@ -122,7 +124,8 @@ def tile_attend_grwada_pl_kernel(tc, xT, G, acc, offs, out_0, out_1, out_2, out_
             nc.gpsimd.memset(w[:], 0.0)
             win[t] = w
 
-        late_window(2)
+        late_window(0)
+        late_window(1)
 
         r_ps = bank(6, "r_ps")
         r_row = sb.tile([P, SLOTS], F32, name="r_row")
@@ -145,18 +148,20 @@ def tile_attend_grwada_pl_kernel(tc, xT, G, acc, offs, out_0, out_1, out_2, out_
             root = sb.tile([P, 2], F32, name="root%d" % h, tag="root%d" % h)
             for k in (0, 1):
                 c = 2 * h + k
-                by_c[c] = sb.tile([P, D], F32, name="dw_sb%d" % c)
-                squares = sb.tile([P, D], BF16, name="squares%d" % c)
+                by_c[c] = sb.tile([P, D], F32, name="dw_sb%d" % c, tag="dw_sb%d" % c)
+                squares = sb.tile([P, D], BF16, name="squares%d" % c,
+                                  tag={2: "root0", 3: "rinv0"}.get(c, "squares%d" % c))
                 nc.scalar.activation(squares[:], dw_ps[c][:], ACT.Square, scale=math.sqrt(1.0 / D),
-                                     accum_out=q_pad[:, c:c + 1])
+                                     accum_out=q_pad[:, COL + c:COL + c + 1])
                 if c < 3:
                     nc.vector.tensor_copy(by_c[c][:], dw_ps[c][:])
             for k in (0, 1):
                 c = 2 * h + k
-                nc.scalar.activation(root[:, k:k + 1], q_pad[:, c:c + 1], ACT.Sqrt, bias=acc_pad[:, c:c + 1])
-            denom = sb.tile([P, 2], F32, name="denom%d" % h)
+                nc.scalar.activation(root[:, k:k + 1], q_pad[:, COL + c:COL + c + 1], ACT.Sqrt,
+                                     bias=acc_pad[:, COL + c:COL + c + 1])
+            denom = sb.tile([P, 2], F32, name="denom%d" % h, tag="late_w%d" % (2 + h), align_bytes=64)
             nc.scalar.activation(denom[:], root[:], ACT.Identity, bias=EPS)
-            rinv = sb.tile([P, 2], F32, name="rinv%d" % h)
+            rinv = sb.tile([P, 2], F32, name="rinv%d" % h, tag="rinv%d" % h)
             nc.vector.reciprocal(rinv[:], denom[:])
             if h == 1:
                 scatter_half(1, 0, "root1")()
@@ -173,6 +178,8 @@ def tile_attend_grwada_pl_kernel(tc, xT, G, acc, offs, out_0, out_1, out_2, out_
                 turn(1, 2 * h + k)
         scatter_half(1, 1, "up_half11")()
 
+        late_window(2)
+        late_window(3)
         up_ps.append(bank(2, "up_ps2"))
         up_ps.append(bank(3, "up_ps3"))
         up_sb = {}
@@ -185,13 +192,13 @@ def tile_attend_grwada_pl_kernel(tc, xT, G, acc, offs, out_0, out_1, out_2, out_
         na_ps = bank(7, "na_ps")
         nc.tensor.matmul(na_ps[:, 0:P], q_pad[:], ident[:], start=True, stop=False, is_transpose=True)
         nc.tensor.matmul(na_ps[:, 0:P], acc_pad[:], ident[:], start=False, stop=True, is_transpose=True)
-        na_rows = sb.tile([32, P], F32, name="na_rows")
-        nc.scalar.copy(na_rows[:], na_ps[0:32, 0:P])
-        nc.sync.dma_start(out_1.rearrange("o (c i) -> (o c) i", c=4), na_rows[0:4, :])
+        na_rows = sb.tile([P, P], F32, name="na_rows")
+        nc.scalar.copy(na_rows[:], na_ps[:, 0:P])
+        nc.sync.dma_start(out_1.rearrange("o (c i) -> (o c) i", c=4), na_rows[COL:P, :])
 
         out_rows = out_0.rearrange("(m t) c -> m t c", t=LANES)
         chunks = TABLE // CHUNK
-        pairs = [sb.tile([P, 2, CHUNK, 2], BF16, name="pairs%d" % k) for k in range(chunks)]
+        pairs = [sb.tile([P, 2, CHUNK, 2], BF16, name="pairs%d" % k, tag="dw_sb%d" % k) for k in range(chunks)]
 
         def round_lane(engine_copy, t, k):
             engine_copy(pairs[k][:, t // 2, :, t % 2], win[t][:, k * CHUNK:(k + 1) * CHUNK])
@@ -201,25 +208,33 @@ def tile_attend_grwada_pl_kernel(tc, xT, G, acc, offs, out_0, out_1, out_2, out_
                 nc.vector.tensor_tensor(win[t][:].indirect(offsets[:]), up_sb[t][:], r_row[:], ALU.mult)
             nc.sync.dma_start(out_rows[:, t, :], win[t][:])
             if t < LANES - 1:
-                for k in range(t // 2, chunks):
+                for k in range(2 * (t // 2), chunks):
                     round_lane(nc.scalar.copy, t, k)
 
         words_out = out_2[0].rearrange("p c l -> p (c l)").bitcast(I32)
         y_scales = sb.tile([P, TABLE], U8, name="y_scales", align_bytes=64)
         last = LANES - 1
-        round_lane(nc.vector.tensor_copy, last - 1, 0)
-        round_lane(nc.vector.tensor_copy, last, 0)
-        for k in range(1, chunks):
+        for k in range(chunks // 2):
+            round_lane(nc.vector.tensor_copy, last - 1, k)
+            round_lane(nc.vector.tensor_copy, last, k)
+        for k in range(chunks // 2, chunks):
             round_lane(nc.scalar.copy, last, k)
+
+        width = CHUNK // 2
         for k in range(chunks):
-            cols = slice(k * CHUNK, (k + 1) * CHUNK)
-            grouped = sb.tile([P, CHUNK * LANES], BF16, name="grouped%d" % k, align_bytes=64)
-            weave = nc.scalar.copy if k == chunks - 1 else nc.vector.tensor_copy
-            weave(grouped[:].bitcast(F32).rearrange("p (c u) -> p c u", u=2),
-                  pairs[k][:].rearrange("p u c e -> p (u c e)").bitcast(F32).rearrange("p (u c) -> p c u", u=2))
+            words = pairs[k][:].rearrange("p u c e -> p (u c e)").bitcast(F32).rearrange("p (u c) -> p c u", u=2)
+            grouped = []
+            for j in range(2):
+                engine_copy = nc.scalar.copy if 2 * k + j > chunks else nc.vector.tensor_copy
+                grouped.append(sb.tile([P, width * LANES], BF16, name="grouped%d%d" % (k, j), align_bytes=64))
+                engine_copy(grouped[j][:].bitcast(F32).rearrange("p (c u) -> p c u", u=2),
+                            words[:, j * width:(j + 1) * width, :])
             y_codes = sb.tile([P, CHUNK], U32, name="y_codes%d" % k, align_bytes=64)
-            nc.vector.quantize_mx(out=y_codes[:].bitcast(E4M3), scales=y_scales[:, cols], in_=grouped[:])
-            nc.sync.dma_start(words_out[:, cols], y_codes[:].bitcast(I32))
+            for j in range(2):
+                first = k * CHUNK + j * width
+                nc.vector.quantize_mx(out=y_codes[:, j * width:(j + 1) * width].bitcast(E4M3),
+                                      scales=y_scales[:, first:first + width], in_=grouped[j][:])
+            nc.sync.dma_start(words_out[:, k * CHUNK:(k + 1) * CHUNK], y_codes[:].bitcast(I32))
         scales_out = out_3[0].bitcast(I32)
         for q in range(4):
             queue = nc.scalar if q % 2 else nc.sync

@@ -1,4 +1,3 @@
-import math
 from contextlib import ExitStack
 
 import concourse.mybir as mybir
@@ -25,6 +24,9 @@ HALF = SLOTS // 2
 CHUNK = 512
 EPS = 0.001
 COL = P - 4
+VECTOR_COLS = 1280
+VECTOR_PIECES = ((0, 512), (512, 1024), (1024, 1280))
+SCALAR_PIECES = ((1280, 1792), (1792, 2048))
 
 FLOPS = 2 * D * R * SLOTS
 BYTES = 4 * (D * R + R * SLOTS + TABLE) + 2 * P * SLOTS // 16 + 4 * (D * TABLE + SLOTS) + D * TABLE + 16 * TABLE
@@ -44,8 +46,7 @@ def tile_attend_grwada_pl_kernel(tc, xT, G, acc, offs, out_0, out_1, out_2, out_
         nc.sync.dma_start(offsets[:], offs)
         acc_win = sb.tile([P, TABLE], F32, name="acc_win")
         nc.scalar.dma_start(acc_win[P - 1:P, :], acc[0:1, :])
-        nc.vector.memset(acc_win[0:96, :], 0.0)
-        nc.vector.memset(acc_win[96:P - 1, :], 0.0)
+        nc.vector.memset(acc_win[0:P - 1, :], 0.0)
         x_raw = []
         for t in range(LANES):
             raw = sb.tile([P, R], F32, name="x_raw%d" % t)
@@ -58,22 +59,22 @@ def tile_attend_grwada_pl_kernel(tc, xT, G, acc, offs, out_0, out_1, out_2, out_
             nc.sync.dma_start(raw[:], g_rows[:, :, h * HALF:(h + 1) * HALF])
             g_raw.append(raw)
 
-        warm = sb.tile([P, 1], F32, name="warm")
-        nc.gpsimd.memset(warm[:], 1.0)
-        warm_out = sb.tile([P, 1], F32, name="warm_out")
-        nc.scalar.activation(warm_out[:], warm[:], ACT.Sqrt)
+        inv_d = sb.tile([P, 1], F32, name="inv_d")
+        nc.gpsimd.memset(inv_d[:], 1.0 / D)
+        root_inv_d = sb.tile([P, 1], F32, name="root_inv_d")
+        nc.scalar.activation(root_inv_d[:], inv_d[:], ACT.Sqrt)
         ident = sb.tile([P, P], F32, name="ident")
         make_identity(nc, ident[:])
         q_pad = sb.tile([P, P], F32, name="q_pad")
         nc.gpsimd.memset(q_pad[:], 0.0)
-        win = {}
+        win = {0: sb.tile([P, TABLE], F32, name="win0")}
+        nc.vector.memset(win[0][:], 0.0)
 
         acc_g = sb.tile([P, SLOTS], F32, name="acc_g")
         nc.vector.tensor_copy(acc_g[:], acc_win[:].indirect(offsets[:]))
 
         x_codes = sb.tile([P, D], U32, name="x_codes", align_bytes=64)
         x_scales = sb.tile([P, D], U8, name="x_scales", align_bytes=64)
-        x_banks = (0, 1, 7, 5)
         xb = {}
         for t in (2, 3, 0, 1):
             xb[t] = sb.tile([P, 2, P, 2], BF16, name="xb%d" % t)
@@ -81,7 +82,7 @@ def tile_attend_grwada_pl_kernel(tc, xT, G, acc, offs, out_0, out_1, out_2, out_
             engine_copy(xb[t][:], x_raw[t][:].rearrange("m (p u e) -> m u p e", u=2, e=2))
         for t in range(LANES):
             words = xb[t][:].rearrange("m u p e -> m (u p e)").bitcast(F32)
-            xt = bank(x_banks[t], "xt%d" % t)
+            xt = bank(t, "xt%d" % t)
             for u in range(2):
                 nc.tensor.transpose(xt[:, u * P:(u + 1) * P], words[:, u * P:(u + 1) * P], ident[:])
             xg = sb.tile([P, LANES * P], BF16, name="xg%d" % t, align_bytes=64)
@@ -91,150 +92,141 @@ def tile_attend_grwada_pl_kernel(tc, xT, G, acc, offs, out_0, out_1, out_2, out_
             cols = slice(t * P, (t + 1) * P)
             nc.vector.quantize_mx(out=x_codes[:, cols].bitcast(E4M3), scales=x_scales[:, cols], in_=xg[:])
 
-        acc_t = bank(6, "acc_t")
+        acc_t = bank(4, "acc_t")
         for c in range(4):
             nc.tensor.transpose(acc_t[:, c * P:(c + 1) * P], acc_g[:, c * P:(c + 1) * P], ident[:])
         acc_pad = sb.tile([P, P], F32, name="acc_pad")
         nc.scalar.copy(acc_pad[:].rearrange("p (k c) -> p k c", c=4),
                        acc_t[:].rearrange("p (c k) -> p k c", c=4)[:, P - P // 4:P, :])
 
-        dw_sb = []
         dw_ps = []
         for h in range(2):
             gg = sb.tile([P, HALF * LANES], BF16, name="gg%d" % h, align_bytes=64,
-                         tag="late_w0" if h else "gg0")
+                         tag="late_w1" if h else "gg0")
             nc.vector.tensor_copy(
                 gg[:].rearrange("p (c i j) -> p c j i", i=4, j=LANES),
                 g_raw[h][:].rearrange("p j (c i) -> p c j i", i=4))
             g_codes = sb.tile([P, HALF], U32, name="g_codes%d" % h, align_bytes=64,
-                              tag="late_w1" if h else "g_codes0")
-            g_scales = sb.tile([P, HALF], U8, name="g_scales%d" % h, align_bytes=64)
+                              tag="late_w2" if h else "g_codes0")
+            g_scales = sb.tile([P, HALF], U8, name="g_scales%d" % h, align_bytes=64,
+                               tag="late_w3" if h else "g_scales0")
             nc.vector.quantize_mx(out=g_codes[:].bitcast(E5M2), scales=g_scales[:], in_=gg[:])
             for k in range(2):
                 c = 2 * h + k
                 cols = slice(k * P, (k + 1) * P)
-                dw = bank(2 + c, "dw%d" % c)
+                dw = bank((5 + c) % 8, "dw%d" % c)
                 nc.tensor.matmul_mx(
                     out=dw[:], lhsT=g_codes[:, cols].bitcast(E5M2), lhsT_scale=g_scales[:, cols],
                     rhs=x_codes[:].bitcast(E4M3), rhs_scale=x_scales[:], start=True, stop=True)
                 dw_ps.append(dw)
 
-        def late_window(t):
-            w = sb.tile([P, TABLE], F32, name="win%d" % t, tag="late_w%d" % t, align_bytes=64)
-            nc.gpsimd.memset(w[:], 0.0)
-            win[t] = w
+        for t in range(1, LANES):
+            win[t] = sb.tile([P, TABLE], F32, name="win%d" % t, tag="late_w%d" % t, align_bytes=64)
+            nc.gpsimd.memset(win[t][:], 0.0)
 
-        late_window(0)
-        late_window(1)
-
-        r_ps = bank(6, "r_ps")
         r_row = sb.tile([P, SLOTS], F32, name="r_row")
-        up_ps = [bank(0, "up_ps0"), bank(1, "up_ps1")]
         by_c = {}
+        late_ps = {2: bank(3, "late_ps2"), 3: bank(4, "late_ps3")}
 
-        def turn(t, c):
-            nc.tensor.transpose(up_ps[t][:, c * P:(c + 1) * P], by_c[c][:, t * P:(t + 1) * P], ident[:])
-
-        def scatter_half(t, h, tag):
-            half = slice(h * HALF, (h + 1) * HALF)
-            src = sb.tile([P, HALF], F32, name="up_half%d%d" % (t, h), tag=tag)
-            nc.scalar.copy(src[:], up_ps[t][:, half])
-            return lambda: nc.vector.tensor_tensor(
-                win[t][:].indirect(offsets[:, h * HALF // 16:(h + 1) * HALF // 16]),
-                src[:], r_row[:, half], ALU.mult)
+        def listed(t, h):
+            return win[t][:].indirect(offsets[:, h * HALF // 16:(h + 1) * HALF // 16])
 
         for h in range(2):
             half = slice(h * HALF, (h + 1) * HALF)
-            root = sb.tile([P, 2], F32, name="root%d" % h, tag="root%d" % h)
+            root = sb.tile([P, 2], F32, name="root%d" % h)
+            early_ps = bank(1 + h, "early_ps%d" % h)
             for k in (0, 1):
                 c = 2 * h + k
                 by_c[c] = sb.tile([P, D], F32, name="dw_sb%d" % c, tag="dw_sb%d" % c)
-                squares = sb.tile([P, D], BF16, name="squares%d" % c,
-                                  tag={2: "root0", 3: "rinv0"}.get(c, "squares%d" % c))
-                nc.scalar.activation(squares[:], dw_ps[c][:], ACT.Square, scale=math.sqrt(1.0 / D),
+                squares = sb.tile([P, D], BF16, name="squares%d" % c)
+                nc.scalar.activation(squares[:], dw_ps[c][:], ACT.Square, scale=root_inv_d[:],
                                      accum_out=q_pad[:, COL + c:COL + c + 1])
-                if c < 3:
-                    nc.vector.tensor_copy(by_c[c][:], dw_ps[c][:])
+                nc.vector.tensor_copy(by_c[c][:], dw_ps[c][:])
+                for t in (0, 1):
+                    nc.tensor.transpose(early_ps[:, t * HALF + k * P:t * HALF + (k + 1) * P],
+                                        by_c[c][:, t * P:(t + 1) * P], ident[:])
             for k in (0, 1):
                 c = 2 * h + k
                 nc.scalar.activation(root[:, k:k + 1], q_pad[:, COL + c:COL + c + 1], ACT.Sqrt,
                                      bias=acc_pad[:, COL + c:COL + c + 1])
-            denom = sb.tile([P, 2], F32, name="denom%d" % h, tag="late_w%d" % (2 + h), align_bytes=64)
+            denom = sb.tile([P, 2], F32, name="denom%d" % h)
             nc.scalar.activation(denom[:], root[:], ACT.Identity, bias=EPS)
-            rinv = sb.tile([P, 2], F32, name="rinv%d" % h, tag="rinv%d" % h)
+            rinv = sb.tile([P, 2], F32, name="rinv%d" % h)
             nc.vector.reciprocal(rinv[:], denom[:])
-            if h == 1:
-                scatter_half(1, 0, "root1")()
-                nc.scalar.copy(by_c[3][:], dw_ps[3][:])
+            r_ps = bank(5 + h, "r_ps%d" % h)
             for k in (0, 1):
-                turn(0, 2 * h + k)
-            scatter = scatter_half(0, h, "up_half0%d" % h)
-            for k in (0, 1):
-                c = 2 * h + k
-                nc.tensor.transpose(r_ps[:, c * P:(c + 1) * P], rinv[:, k:k + 1].to_broadcast([P, P]), ident[:])
-            nc.scalar.copy(r_row[:, half], r_ps[:, half])
-            scatter()
-            for k in (0, 1):
-                turn(1, 2 * h + k)
-        scatter_half(1, 1, "up_half11")()
+                nc.tensor.transpose(r_ps[:, k * P:(k + 1) * P], rinv[:, k:k + 1].to_broadcast([P, P]), ident[:])
+            dw0 = sb.tile([P, HALF], F32, name="dw0_%d" % h)
+            nc.scalar.copy(dw0[:], early_ps[:, 0:HALF])
+            nc.scalar.copy(r_row[:, half], r_ps[:, 0:HALF])
+            up1 = sb.tile([P, HALF], F32, name="up1_%d" % h)
+            nc.vector.tensor_tensor(up1[:], early_ps[:, HALF:2 * HALF], r_row[:, half], ALU.mult)
+            nc.vector.tensor_tensor(listed(0, h), dw0[:], r_row[:, half], ALU.mult)
+            nc.scalar.activation(listed(1, h), up1[:], ACT.Copy)
 
-        late_window(2)
-        late_window(3)
-        up_ps.append(bank(2, "up_ps2"))
-        up_ps.append(bank(3, "up_ps3"))
-        up_sb = {}
-        for t in range(2, LANES):
+        out_rows = out_0.rearrange("(m t) c -> m t c", t=LANES)
+        for t in (0, 1):
+            nc.sync.dma_start(out_rows[:, t, :], win[t][:])
+
+        for t in (2, 3):
             for c in range(4):
-                turn(t, c)
-            up_sb[t] = sb.tile([P, SLOTS], F32, name="up_sb%d" % t)
-            nc.scalar.copy(up_sb[t][:], up_ps[t][:])
+                nc.tensor.transpose(late_ps[t][:, c * P:(c + 1) * P], by_c[c][:, t * P:(t + 1) * P], ident[:])
+        up3 = sb.tile([P, SLOTS], F32, name="up3", tag="after_scalar")
+        nc.vector.tensor_tensor(up3[:], late_ps[3][:], r_row[:], ALU.mult)
+        dw2 = sb.tile([P, SLOTS], F32, name="dw2", tag="after_vector")
+        nc.scalar.copy(dw2[:], late_ps[2][:])
+        nc.vector.tensor_tensor(win[2][:].indirect(offsets[:]), dw2[:], r_row[:], ALU.mult)
+        for h in range(2):
+            nc.scalar.activation(listed(3, h), up3[:, h * HALF:(h + 1) * HALF], ACT.Copy)
+        for t in (2, 3):
+            nc.sync.dma_start(out_rows[:, t, :], win[t][:])
 
         na_ps = bank(7, "na_ps")
         nc.tensor.matmul(na_ps[:, 0:P], q_pad[:], ident[:], start=True, stop=False, is_transpose=True)
         nc.tensor.matmul(na_ps[:, 0:P], acc_pad[:], ident[:], start=False, stop=True, is_transpose=True)
         na_rows = sb.tile([P, P], F32, name="na_rows")
-        nc.scalar.copy(na_rows[:], na_ps[:, 0:P])
+        nc.vector.tensor_copy(na_rows[:], na_ps[:, 0:P])
         nc.sync.dma_start(out_1.rearrange("o (c i) -> (o c) i", c=4), na_rows[COL:P, :])
-
-        out_rows = out_0.rearrange("(m t) c -> m t c", t=LANES)
-        chunks = TABLE // CHUNK
-        pairs = [sb.tile([P, 2, CHUNK, 2], BF16, name="pairs%d" % k, tag="dw_sb%d" % k) for k in range(chunks)]
-
-        def round_lane(engine_copy, t, k):
-            engine_copy(pairs[k][:, t // 2, :, t % 2], win[t][:, k * CHUNK:(k + 1) * CHUNK])
-
-        for t in range(LANES):
-            if t > 1:
-                nc.vector.tensor_tensor(win[t][:].indirect(offsets[:]), up_sb[t][:], r_row[:], ALU.mult)
-            nc.sync.dma_start(out_rows[:, t, :], win[t][:])
-            if t < LANES - 1:
-                for k in range(2 * (t // 2), chunks):
-                    round_lane(nc.scalar.copy, t, k)
 
         words_out = out_2[0].rearrange("p c l -> p (c l)").bitcast(I32)
         y_scales = sb.tile([P, TABLE], U8, name="y_scales", align_bytes=64)
-        last = LANES - 1
-        for k in range(chunks // 2):
-            round_lane(nc.vector.tensor_copy, last - 1, k)
-            round_lane(nc.vector.tensor_copy, last, k)
-        for k in range(chunks // 2, chunks):
-            round_lane(nc.scalar.copy, last, k)
+        pairs = {"vector": sb.tile([P, 2, VECTOR_COLS, 2], BF16, name="pairs_v", tag="after_vector"),
+                 "scalar": sb.tile([P, 2, TABLE - VECTOR_COLS, 2], BF16, name="pairs_s", tag="after_scalar")}
+        grouped = {}
 
-        width = CHUNK // 2
-        for k in range(chunks):
-            words = pairs[k][:].rearrange("p u c e -> p (u c e)").bitcast(F32).rearrange("p (u c) -> p c u", u=2)
-            grouped = []
-            for j in range(2):
-                engine_copy = nc.scalar.copy if 2 * k + j > chunks else nc.vector.tensor_copy
-                grouped.append(sb.tile([P, width * LANES], BF16, name="grouped%d%d" % (k, j), align_bytes=64))
-                engine_copy(grouped[j][:].bitcast(F32).rearrange("p (c u) -> p c u", u=2),
-                            words[:, j * width:(j + 1) * width, :])
-            y_codes = sb.tile([P, CHUNK], U32, name="y_codes%d" % k, align_bytes=64)
-            for j in range(2):
-                first = k * CHUNK + j * width
-                nc.vector.quantize_mx(out=y_codes[:, j * width:(j + 1) * width].bitcast(E4M3),
-                                      scales=y_scales[:, first:first + width], in_=grouped[j][:])
-            nc.sync.dma_start(words_out[:, k * CHUNK:(k + 1) * CHUNK], y_codes[:].bitcast(I32))
+        def round_lane(who, a, b, t):
+            first = 0 if who == "vector" else VECTOR_COLS
+            engine_copy = nc.vector.tensor_copy if who == "vector" else nc.scalar.copy
+            engine_copy(pairs[who][:, t // 2, a - first:b - first, t % 2], win[t][:, a:b])
+
+        def weave(who, a, b):
+            first = 0 if who == "vector" else VECTOR_COLS
+            engine_copy = nc.vector.tensor_copy if who == "vector" else nc.scalar.copy
+            words = pairs[who][:].rearrange("p u c e -> p (u c e)").bitcast(F32).rearrange("p (u c) -> p c u", u=2)
+            grouped[a] = sb.tile([P, (b - a) * LANES], BF16, name="grouped%d" % a, align_bytes=64)
+            engine_copy(grouped[a][:].bitcast(F32).rearrange("p (c u) -> p c u", u=2), words[:, a - first:b - first, :])
+
+        def quantise(a, b):
+            y_codes = sb.tile([P, b - a], U32, name="y_codes%d" % a, align_bytes=64)
+            nc.vector.quantize_mx(out=y_codes[:].bitcast(E4M3), scales=y_scales[:, a:b], in_=grouped[a][:])
+            nc.sync.dma_start(words_out[:, a:b], y_codes[:].bitcast(I32))
+
+        scalar_pieces = SCALAR_PIECES
+        for a, b in scalar_pieces:
+            for t in range(LANES):
+                round_lane("scalar", a, b, t)
+            weave("scalar", a, b)
+        waiting = []
+        for n, (a, b) in enumerate(VECTOR_PIECES):
+            for t in range(LANES):
+                round_lane("vector", a, b, t)
+                if t == 0 and waiting:
+                    quantise(*waiting.pop(0))
+            weave("vector", a, b)
+            waiting.append((a, b))
+        quantise(*scalar_pieces[0])
+        quantise(*waiting.pop(0))
+        quantise(*scalar_pieces[1])
         scales_out = out_3[0].bitcast(I32)
         for q in range(4):
             queue = nc.scalar if q % 2 else nc.sync

@@ -24,9 +24,8 @@ HALF = SLOTS // 2
 CHUNK = 512
 EPS = 0.001
 COL = P - 4
-VECTOR_COLS = 1280
-VECTOR_PIECES = ((0, 512), (512, 1024), (1024, 1280))
-SCALAR_PIECES = ((1280, 1792), (1792, 2048))
+VECTOR_PIECES = ((0, 512), (512, 1024), (1024, 1088))
+SCALAR_PIECES = ((1536, 2048), (1280, 1536), (1088, 1280))
 
 FLOPS = 2 * D * R * SLOTS
 BYTES = 4 * (D * R + R * SLOTS + TABLE) + 2 * P * SLOTS // 16 + 4 * (D * TABLE + SLOTS) + D * TABLE + 16 * TABLE
@@ -43,15 +42,16 @@ def tile_attend_grwada_pl_kernel(tc, xT, G, acc, offs, out_0, out_1, out_2, out_
 
         x_rows = xT.rearrange("(m t) r -> m t r", t=LANES)
         offsets = sb.tile([P, SLOTS // 16], U16, name="offsets")
-        nc.sync.dma_start(offsets[:], offs)
         acc_win = sb.tile([P, TABLE], F32, name="acc_win")
-        nc.scalar.dma_start(acc_win[P - 1:P, :], acc[0:1, :])
         nc.vector.memset(acc_win[0:P - 1, :], 0.0)
         x_raw = []
         for t in range(LANES):
             raw = sb.tile([P, R], F32, name="x_raw%d" % t)
             nc.sync.dma_start(raw[:], x_rows[:, t, :])
             x_raw.append(raw)
+            if t == 0:
+                nc.sync.dma_start(acc_win[P - 1:P, :], acc[0:1, :])
+                nc.sync.dma_start(offsets[:], offs)
         g_rows = G.rearrange("(p j) i -> p j i", j=LANES)
         g_raw = []
         for h in range(2):
@@ -68,7 +68,7 @@ def tile_attend_grwada_pl_kernel(tc, xT, G, acc, offs, out_0, out_1, out_2, out_
         q_pad = sb.tile([P, P], F32, name="q_pad")
         nc.gpsimd.memset(q_pad[:], 0.0)
         win = {0: sb.tile([P, TABLE], F32, name="win0")}
-        nc.vector.memset(win[0][:], 0.0)
+        nc.gpsimd.memset(win[0][:], 0.0)
 
         acc_g = sb.tile([P, SLOTS], F32, name="acc_g")
         nc.vector.tensor_copy(acc_g[:], acc_win[:].indirect(offsets[:]))
@@ -77,7 +77,7 @@ def tile_attend_grwada_pl_kernel(tc, xT, G, acc, offs, out_0, out_1, out_2, out_
         x_scales = sb.tile([P, D], U8, name="x_scales", align_bytes=64)
         xb = {}
         for t in (2, 3, 0, 1):
-            xb[t] = sb.tile([P, 2, P, 2], BF16, name="xb%d" % t)
+            xb[t] = sb.tile([P, 2, P, 2], BF16, name="xb%d" % t, tag="xb%d" % t, align_bytes=64)
             engine_copy = nc.vector.tensor_copy if t >= 2 else nc.scalar.copy
             engine_copy(xb[t][:], x_raw[t][:].rearrange("m (p u e) -> m u p e", u=2, e=2))
         for t in range(LANES):
@@ -85,14 +85,15 @@ def tile_attend_grwada_pl_kernel(tc, xT, G, acc, offs, out_0, out_1, out_2, out_
             xt = bank(t, "xt%d" % t)
             for u in range(2):
                 nc.tensor.transpose(xt[:, u * P:(u + 1) * P], words[:, u * P:(u + 1) * P], ident[:])
-            xg = sb.tile([P, LANES * P], BF16, name="xg%d" % t, align_bytes=64)
+            xg = sb.tile([P, LANES * P], BF16, name="xg%d" % t, align_bytes=64,
+                         tag="late_w1" if t == 3 else "xg%d" % t)
             nc.scalar.copy(
                 xg[:].bitcast(F32).rearrange("p (m u) -> p m u", u=2),
                 xt[:, 0:2 * P].rearrange("p (u m) -> p m u", u=2))
             cols = slice(t * P, (t + 1) * P)
             nc.vector.quantize_mx(out=x_codes[:, cols].bitcast(E4M3), scales=x_scales[:, cols], in_=xg[:])
 
-        acc_t = bank(4, "acc_t")
+        acc_t = bank(2, "acc_t")
         for c in range(4):
             nc.tensor.transpose(acc_t[:, c * P:(c + 1) * P], acc_g[:, c * P:(c + 1) * P], ident[:])
         acc_pad = sb.tile([P, P], F32, name="acc_pad")
@@ -100,133 +101,181 @@ def tile_attend_grwada_pl_kernel(tc, xT, G, acc, offs, out_0, out_1, out_2, out_
                        acc_t[:].rearrange("p (c k) -> p k c", c=4)[:, P - P // 4:P, :])
 
         dw_ps = []
-        for h in range(2):
-            gg = sb.tile([P, HALF * LANES], BF16, name="gg%d" % h, align_bytes=64,
-                         tag="late_w1" if h else "gg0")
-            nc.vector.tensor_copy(
-                gg[:].rearrange("p (c i j) -> p c j i", i=4, j=LANES),
-                g_raw[h][:].rearrange("p j (c i) -> p c j i", i=4))
-            g_codes = sb.tile([P, HALF], U32, name="g_codes%d" % h, align_bytes=64,
-                              tag="late_w2" if h else "g_codes0")
-            g_scales = sb.tile([P, HALF], U8, name="g_scales%d" % h, align_bytes=64,
-                               tag="late_w3" if h else "g_scales0")
-            nc.vector.quantize_mx(out=g_codes[:].bitcast(E5M2), scales=g_scales[:], in_=gg[:])
-            for k in range(2):
-                c = 2 * h + k
-                cols = slice(k * P, (k + 1) * P)
+        gg = []
+        g_codes = sb.tile([P, SLOTS], U32, name="g_codes", align_bytes=64, tag="late_w3")
+        g_scales = sb.tile([P, SLOTS], U8, name="g_scales", align_bytes=64, tag="late_w2")
+        for c in range(4):
+            h, k = divmod(c, 2)
+            if c < 2:
+                gg.append(sb.tile([P, P * LANES], BF16, name="gg%d" % c, align_bytes=64, tag=("xg2", "xb3")[c])[:])
+            elif c == 2:
+                late_gg = sb.tile([P, 2 * P * LANES], BF16, name="late_gg", align_bytes=64, tag="late_w1")
+                gg.extend([late_gg[:, :P * LANES], late_gg[:, P * LANES:]])
+            engine_copy = nc.scalar.copy if c == 1 else nc.vector.tensor_copy
+            engine_copy(gg[c].rearrange("p (c i j) -> p c j i", i=4, j=LANES),
+                        g_raw[h][:, :, k * P:(k + 1) * P].rearrange("p j (c i) -> p c j i", i=4))
+            if k == 0:
+                continue
+            for c in (2 * h, 2 * h + 1):
+                cols = slice(c * P, (c + 1) * P)
+                nc.vector.quantize_mx(out=g_codes[:, cols].bitcast(E5M2), scales=g_scales[:, cols], in_=gg[c])
                 dw = bank((5 + c) % 8, "dw%d" % c)
                 nc.tensor.matmul_mx(
                     out=dw[:], lhsT=g_codes[:, cols].bitcast(E5M2), lhsT_scale=g_scales[:, cols],
                     rhs=x_codes[:].bitcast(E4M3), rhs_scale=x_scales[:], start=True, stop=True)
                 dw_ps.append(dw)
+        lane0_ps = bank(1, "lane0_ps")
+        nc.tensor.matmul_mx(
+            out=lane0_ps[:], lhsT=x_codes[:, 0:P].bitcast(E4M3), lhsT_scale=x_scales[:, 0:P],
+            rhs=g_codes[:].bitcast(E5M2), rhs_scale=g_scales[:], start=True, stop=True)
 
-        for t in range(1, LANES):
+        for t in (1, 2, 3):
             win[t] = sb.tile([P, TABLE], F32, name="win%d" % t, tag="late_w%d" % t, align_bytes=64)
             nc.gpsimd.memset(win[t][:], 0.0)
 
+        first_ps = [bank(2 + h, "first_ps%d" % h) for h in range(2)]
+        by_slot = {}
+
+        def turned(t, h):
+            if t < 3:
+                return first_ps[h][:, (t - 1) * HALF:t * HALF]
+            return lane3_ps[:, h * HALF:(h + 1) * HALF]
+
+        def turn(t, c):
+            h, k = divmod(c, 2)
+            nc.tensor.transpose(turned(t, h)[:, k * P:(k + 1) * P], by_slot[c][:, (t - 1) * P:t * P], ident[:])
+
+        def copy_and_turn(c, engine_copy):
+            by_slot[c] = sb.tile([P, D - P], F32, name="dw_by_slot%d" % c, tag="root" if c == 3 else "dw_by_slot%d" % c)
+            engine_copy(by_slot[c][:], dw_ps[c][:, P:])
+            for t in (1, 2):
+                turn(t, c)
+
+        for c in range(4):
+            squares = sb.tile([P, D], BF16, name="squares%d" % c)
+            nc.scalar.activation(squares[:], dw_ps[c][:], ACT.Square, scale=root_inv_d[:],
+                                 accum_out=q_pad[:, COL + c:COL + c + 1])
+            if c < 3:
+                copy_and_turn(c, nc.vector.tensor_copy)
+        root = sb.tile([P, 4], F32, name="root", tag="root")
+        for c in range(4):
+            nc.scalar.activation(root[:, c:c + 1], q_pad[:, COL + c:COL + c + 1], ACT.Sqrt,
+                                 bias=acc_pad[:, COL + c:COL + c + 1])
+        denom = sb.tile([P, 4], F32, name="denom")
+        nc.scalar.activation(denom[:], root[:], ACT.Identity, bias=EPS)
+        rinv = sb.tile([P, 4], F32, name="rinv")
+        nc.vector.reciprocal(rinv[:], denom[:])
+
+        src = {t: sb.tile([P, SLOTS], F32, name="src%d" % t) for t in (0, 3)}
+        nc.vector.tensor_copy(src[0][:], lane0_ps[:])
+        raw2 = sb.tile([P, HALF], F32, name="raw2", tag="raw2")
+        nc.vector.tensor_copy(raw2[:], turned(2, 0))
+
+        scaled = {}
         r_row = sb.tile([P, SLOTS], F32, name="r_row")
-        by_c = {}
-        late_ps = {2: bank(3, "late_ps2"), 3: bank(4, "late_ps3")}
-
-        def listed(t, h):
-            return win[t][:].indirect(offsets[:, h * HALF // 16:(h + 1) * HALF // 16])
-
+        r_ps = [bank(5 + h, "r_ps%d" % h) for h in range(2)]
+        for c in range(4):
+            h, k = divmod(c, 2)
+            nc.tensor.transpose(r_ps[h][:, k * P:(k + 1) * P], rinv[:, c:c + 1].to_broadcast([P, P]), ident[:])
+        copy_and_turn(3, nc.scalar.copy)
         for h in range(2):
             half = slice(h * HALF, (h + 1) * HALF)
-            root = sb.tile([P, 2], F32, name="root%d" % h)
-            early_ps = bank(1 + h, "early_ps%d" % h)
-            for k in (0, 1):
-                c = 2 * h + k
-                by_c[c] = sb.tile([P, D], F32, name="dw_sb%d" % c, tag="dw_sb%d" % c)
-                squares = sb.tile([P, D], BF16, name="squares%d" % c)
-                nc.scalar.activation(squares[:], dw_ps[c][:], ACT.Square, scale=root_inv_d[:],
-                                     accum_out=q_pad[:, COL + c:COL + c + 1])
-                nc.vector.tensor_copy(by_c[c][:], dw_ps[c][:])
-                for t in (0, 1):
-                    nc.tensor.transpose(early_ps[:, t * HALF + k * P:t * HALF + (k + 1) * P],
-                                        by_c[c][:, t * P:(t + 1) * P], ident[:])
-            for k in (0, 1):
-                c = 2 * h + k
-                nc.scalar.activation(root[:, k:k + 1], q_pad[:, COL + c:COL + c + 1], ACT.Sqrt,
-                                     bias=acc_pad[:, COL + c:COL + c + 1])
-            denom = sb.tile([P, 2], F32, name="denom%d" % h)
-            nc.scalar.activation(denom[:], root[:], ACT.Identity, bias=EPS)
-            rinv = sb.tile([P, 2], F32, name="rinv%d" % h)
-            nc.vector.reciprocal(rinv[:], denom[:])
-            r_ps = bank(5 + h, "r_ps%d" % h)
-            for k in (0, 1):
-                nc.tensor.transpose(r_ps[:, k * P:(k + 1) * P], rinv[:, k:k + 1].to_broadcast([P, P]), ident[:])
-            dw0 = sb.tile([P, HALF], F32, name="dw0_%d" % h)
-            nc.scalar.copy(dw0[:], early_ps[:, 0:HALF])
-            nc.scalar.copy(r_row[:, half], r_ps[:, 0:HALF])
-            up1 = sb.tile([P, HALF], F32, name="up1_%d" % h)
-            nc.vector.tensor_tensor(up1[:], early_ps[:, HALF:2 * HALF], r_row[:, half], ALU.mult)
-            nc.vector.tensor_tensor(listed(0, h), dw0[:], r_row[:, half], ALU.mult)
-            nc.scalar.activation(listed(1, h), up1[:], ACT.Copy)
-
-        out_rows = out_0.rearrange("(m t) c -> m t c", t=LANES)
-        for t in (0, 1):
-            nc.sync.dma_start(out_rows[:, t, :], win[t][:])
-
-        for t in (2, 3):
-            for c in range(4):
-                nc.tensor.transpose(late_ps[t][:, c * P:(c + 1) * P], by_c[c][:, t * P:(t + 1) * P], ident[:])
-        up3 = sb.tile([P, SLOTS], F32, name="up3", tag="after_scalar")
-        nc.vector.tensor_tensor(up3[:], late_ps[3][:], r_row[:], ALU.mult)
-        dw2 = sb.tile([P, SLOTS], F32, name="dw2", tag="after_vector")
-        nc.scalar.copy(dw2[:], late_ps[2][:])
-        nc.vector.tensor_tensor(win[2][:].indirect(offsets[:]), dw2[:], r_row[:], ALU.mult)
+            engine_copy = nc.vector.tensor_copy if h else nc.scalar.copy
+            engine_copy(r_row[:, half], r_ps[h][:, 0:HALF])
         for h in range(2):
-            nc.scalar.activation(listed(3, h), up3[:, h * HALF:(h + 1) * HALF], ACT.Copy)
-        for t in (2, 3):
-            nc.sync.dma_start(out_rows[:, t, :], win[t][:])
+            half = slice(h * HALF, (h + 1) * HALF)
+            scaled[1, h] = sb.tile([P, HALF], F32, name="scaled1%d" % h)
+            nc.vector.tensor_tensor(scaled[1, h][:], turned(1, h), r_row[:, half], ALU.mult)
+        scaled[2, 1] = sb.tile([P, HALF], F32, name="scaled21")
+        nc.vector.tensor_tensor(scaled[2, 1][:], turned(2, 1), r_row[:, HALF:], ALU.mult)
+        lane3_ps = bank(5, "lane3_ps")
+        for c in range(4):
+            turn(3, c)
 
-        na_ps = bank(7, "na_ps")
+        na_ps = bank(4, "na_ps")
         nc.tensor.matmul(na_ps[:, 0:P], q_pad[:], ident[:], start=True, stop=False, is_transpose=True)
         nc.tensor.matmul(na_ps[:, 0:P], acc_pad[:], ident[:], start=False, stop=True, is_transpose=True)
         na_rows = sb.tile([P, P], F32, name="na_rows")
         nc.vector.tensor_copy(na_rows[:], na_ps[:, 0:P])
         nc.sync.dma_start(out_1.rearrange("o (c i) -> (o c) i", c=4), na_rows[COL:P, :])
 
+        out_rows = out_0.rearrange("(m t) c -> m t c", t=LANES)
+
+        def listed(t, h):
+            return win[t][:].indirect(offsets[:, h * HALF // 16:(h + 1) * HALF // 16])
+
+        def scalar_scatter(t, h):
+            values = src[3][:, h * HALF:(h + 1) * HALF] if t == 3 else scaled[t, h][:]
+            nc.scalar.activation(listed(t, h), values, ACT.Copy)
+
+        def store(t):
+            nc.sync.dma_start(out_rows[:, t, :], win[t][:])
+
+        pairs = {}
+        for a, b in SCALAR_PIECES:
+            pairs[a] = sb.tile([P, 2, b - a, 2], BF16, name="pairs%d" % a)[:]
+
+        def round_lane(engine_copy, a, b, t):
+            engine_copy(pairs[a][:, t // 2, :, t % 2], win[t][:, a:b])
+
+        scalar_scatter(1, 0)
+        scalar_scatter(1, 1)
+        store(1)
+        nc.vector.tensor_tensor(win[0][:].indirect(offsets[:]), src[0][:], r_row[:], ALU.mult)
+        store(0)
+        scalar_scatter(2, 1)
+        nc.vector.tensor_tensor(src[3][:], lane3_ps[:], r_row[:], ALU.mult)
+        for t in (0, 1):
+            for a, b in SCALAR_PIECES:
+                round_lane(nc.vector.tensor_copy, a, b, t)
+        nc.vector.tensor_tensor(listed(2, 0), raw2[:], r_row[:, :HALF], ALU.mult)
+        store(2)
+        scalar_scatter(3, 0)
+        scalar_scatter(3, 1)
+        store(3)
+
+
         words_out = out_2[0].rearrange("p c l -> p (c l)").bitcast(I32)
         y_scales = sb.tile([P, TABLE], U8, name="y_scales", align_bytes=64)
-        pairs = {"vector": sb.tile([P, 2, VECTOR_COLS, 2], BF16, name="pairs_v", tag="after_vector"),
-                 "scalar": sb.tile([P, 2, TABLE - VECTOR_COLS, 2], BF16, name="pairs_s", tag="after_scalar")}
-        grouped = {}
+        grouped = [sb.tile([P, CHUNK * LANES], BF16, name="grouped%d" % k, align_bytes=64) for k in range(4)]
+        y_codes = [sb.tile([P, CHUNK], U32, name="y_codes%d" % k, align_bytes=64) for k in range(4)]
 
-        def round_lane(who, a, b, t):
-            first = 0 if who == "vector" else VECTOR_COLS
-            engine_copy = nc.vector.tensor_copy if who == "vector" else nc.scalar.copy
-            engine_copy(pairs[who][:, t // 2, a - first:b - first, t % 2], win[t][:, a:b])
-
-        def weave(who, a, b):
-            first = 0 if who == "vector" else VECTOR_COLS
-            engine_copy = nc.vector.tensor_copy if who == "vector" else nc.scalar.copy
-            words = pairs[who][:].rearrange("p u c e -> p (u c e)").bitcast(F32).rearrange("p (u c) -> p c u", u=2)
-            grouped[a] = sb.tile([P, (b - a) * LANES], BF16, name="grouped%d" % a, align_bytes=64)
-            engine_copy(grouped[a][:].bitcast(F32).rearrange("p (c u) -> p c u", u=2), words[:, a - first:b - first, :])
+        def finish(engine_copy, a, b):
+            for t in (2, 3):
+                round_lane(engine_copy, a, b, t)
+            words = pairs[a].bitcast(F32).rearrange("p u c e -> p c (u e)")
+            k, first = divmod(a, CHUNK)
+            dst = grouped[k][:].bitcast(F32).rearrange("p (c u) -> p c u", u=2)
+            engine_copy(dst[:, first:first + b - a, :], words)
 
         def quantise(a, b):
-            y_codes = sb.tile([P, b - a], U32, name="y_codes%d" % a, align_bytes=64)
-            nc.vector.quantize_mx(out=y_codes[:].bitcast(E4M3), scales=y_scales[:, a:b], in_=grouped[a][:])
-            nc.sync.dma_start(words_out[:, a:b], y_codes[:].bitcast(I32))
+            k, first = divmod(a, CHUNK)
+            nc.vector.quantize_mx(out=y_codes[k][:, first:first + b - a].bitcast(E4M3), scales=y_scales[:, a:b],
+                                  in_=grouped[k][:, first * LANES:(first + b - a) * LANES])
 
-        scalar_pieces = SCALAR_PIECES
-        for a, b in scalar_pieces:
-            for t in range(LANES):
-                round_lane("scalar", a, b, t)
-            weave("scalar", a, b)
-        waiting = []
-        for n, (a, b) in enumerate(VECTOR_PIECES):
-            for t in range(LANES):
-                round_lane("vector", a, b, t)
-                if t == 0 and waiting:
-                    quantise(*waiting.pop(0))
-            weave("vector", a, b)
-            waiting.append((a, b))
-        quantise(*scalar_pieces[0])
-        quantise(*waiting.pop(0))
-        quantise(*scalar_pieces[1])
+        def store_codes(k):
+            nc.sync.dma_start(words_out[:, k * CHUNK:(k + 1) * CHUNK], y_codes[k][:].bitcast(I32))
+
+        vector_cols = VECTOR_PIECES[-1][1]
+        vector_pairs = sb.tile([P, 2, vector_cols, 2], BF16, name="vector_pairs", tag="raw2")
+        for t in (0, 1):
+            nc.vector.tensor_copy(vector_pairs[:, 0, :, t], win[t][:, 0:vector_cols])
+        for a, b in VECTOR_PIECES:
+            pairs[a] = vector_pairs[:, :, a:b, :]
+        for a, b in SCALAR_PIECES:
+            finish(nc.scalar.copy, a, b)
+        finish(nc.vector.tensor_copy, *VECTOR_PIECES[0])
+        finish(nc.vector.tensor_copy, *VECTOR_PIECES[1])
+        quantise(0, 512)
+        store_codes(0)
+        quantise(1536, 2048)
+        store_codes(3)
+        finish(nc.vector.tensor_copy, *VECTOR_PIECES[2])
+        quantise(512, 1024)
+        store_codes(1)
+        quantise(1280, 1536)
+        quantise(1024, 1280)
+        store_codes(2)
         scales_out = out_3[0].bitcast(I32)
         for q in range(4):
             queue = nc.scalar if q % 2 else nc.sync

@@ -24,8 +24,9 @@ HALF = SLOTS // 2
 CHUNK = 512
 EPS = 0.001
 COL = P - 4
-VECTOR_PIECES = ((0, 512), (512, 1024), (1024, 1088))
-SCALAR_PIECES = ((1536, 2048), (1280, 1536), (1088, 1280))
+VECTOR_COLS = 1024
+SCALAR_PIECES = ((1536, 2048), (1280, 1536), (1152, 1280), (VECTOR_COLS, 1152))
+QUANTISED = ((0, 512), (512, 1024), (1536, 2048), (1280, 1536), (1152, 1280), (1024, 1152))
 
 FLOPS = 2 * D * R * SLOTS
 BYTES = 4 * (D * R + R * SLOTS + TABLE) + 2 * P * SLOTS // 16 + 4 * (D * TABLE + SLOTS) + D * TABLE + 16 * TABLE
@@ -67,8 +68,7 @@ def tile_attend_grwada_pl_kernel(tc, xT, G, acc, offs, out_0, out_1, out_2, out_
         make_identity(nc, ident[:])
         q_pad = sb.tile([P, P], F32, name="q_pad")
         nc.gpsimd.memset(q_pad[:], 0.0)
-        win = {0: sb.tile([P, TABLE], F32, name="win0")}
-        nc.gpsimd.memset(win[0][:], 0.0)
+        win = {}
 
         acc_g = sb.tile([P, SLOTS], F32, name="acc_g")
         nc.vector.tensor_copy(acc_g[:], acc_win[:].indirect(offsets[:]))
@@ -80,6 +80,12 @@ def tile_attend_grwada_pl_kernel(tc, xT, G, acc, offs, out_0, out_1, out_2, out_
             xb[t] = sb.tile([P, 2, P, 2], BF16, name="xb%d" % t, tag="xb%d" % t, align_bytes=64)
             engine_copy = nc.vector.tensor_copy if t >= 2 else nc.scalar.copy
             engine_copy(xb[t][:], x_raw[t][:].rearrange("m (p u e) -> m u p e", u=2, e=2))
+        x_grouped = []
+
+        def quantise_x(t):
+            cols = slice(t * P, (t + 1) * P)
+            nc.vector.quantize_mx(out=x_codes[:, cols].bitcast(E4M3), scales=x_scales[:, cols], in_=x_grouped[t][:])
+
         for t in range(LANES):
             words = xb[t][:].rearrange("m u p e -> m (u p e)").bitcast(F32)
             xt = bank(t, "xt%d" % t)
@@ -90,8 +96,9 @@ def tile_attend_grwada_pl_kernel(tc, xT, G, acc, offs, out_0, out_1, out_2, out_
             nc.scalar.copy(
                 xg[:].bitcast(F32).rearrange("p (m u) -> p m u", u=2),
                 xt[:, 0:2 * P].rearrange("p (u m) -> p m u", u=2))
-            cols = slice(t * P, (t + 1) * P)
-            nc.vector.quantize_mx(out=x_codes[:, cols].bitcast(E4M3), scales=x_scales[:, cols], in_=xg[:])
+            x_grouped.append(xg)
+            if t < LANES - 1:
+                quantise_x(t)
 
         acc_t = bank(2, "acc_t")
         for c in range(4):
@@ -100,104 +107,110 @@ def tile_attend_grwada_pl_kernel(tc, xT, G, acc, offs, out_0, out_1, out_2, out_
         nc.scalar.copy(acc_pad[:].rearrange("p (k c) -> p k c", c=4),
                        acc_t[:].rearrange("p (c k) -> p k c", c=4)[:, P - P // 4:P, :])
 
-        dw_ps = []
-        gg = []
-        g_codes = sb.tile([P, SLOTS], U32, name="g_codes", align_bytes=64, tag="late_w3")
-        g_scales = sb.tile([P, SLOTS], U8, name="g_scales", align_bytes=64, tag="late_w2")
-        for c in range(4):
+        g_codes = sb.tile([P, SLOTS], U32, name="g_codes", align_bytes=64)
+        g_scales = sb.tile([P, SLOTS], U8, name="g_scales", align_bytes=64)
+        dw_ps = [bank((5 + c) % 8, "dw%d" % c) for c in range(3)]
+
+        def weave_g(c, engine_copy, dst):
             h, k = divmod(c, 2)
-            if c < 2:
-                gg.append(sb.tile([P, P * LANES], BF16, name="gg%d" % c, align_bytes=64, tag=("xg2", "xb3")[c])[:])
-            elif c == 2:
-                late_gg = sb.tile([P, 2 * P * LANES], BF16, name="late_gg", align_bytes=64, tag="late_w1")
-                gg.extend([late_gg[:, :P * LANES], late_gg[:, P * LANES:]])
-            engine_copy = nc.scalar.copy if c == 1 else nc.vector.tensor_copy
-            engine_copy(gg[c].rearrange("p (c i j) -> p c j i", i=4, j=LANES),
+            engine_copy(dst.rearrange("p (c i j) -> p c j i", i=4, j=LANES),
                         g_raw[h][:, :, k * P:(k + 1) * P].rearrange("p j (c i) -> p c j i", i=4))
-            if k == 0:
-                continue
-            for c in (2 * h, 2 * h + 1):
-                cols = slice(c * P, (c + 1) * P)
-                nc.vector.quantize_mx(out=g_codes[:, cols].bitcast(E5M2), scales=g_scales[:, cols], in_=gg[c])
-                dw = bank((5 + c) % 8, "dw%d" % c)
-                nc.tensor.matmul_mx(
-                    out=dw[:], lhsT=g_codes[:, cols].bitcast(E5M2), lhsT_scale=g_scales[:, cols],
-                    rhs=x_codes[:].bitcast(E4M3), rhs_scale=x_scales[:], start=True, stop=True)
-                dw_ps.append(dw)
+
+        def quantise_g(c, woven):
+            cols = slice(c * P, (c + 1) * P)
+            nc.vector.quantize_mx(out=g_codes[:, cols].bitcast(E5M2), scales=g_scales[:, cols], in_=woven)
+
+        def product(c, first, end):
+            cols = slice(c * P, (c + 1) * P)
+            nc.tensor.matmul_mx(
+                out=dw_ps[c][:, first:end], lhsT=g_codes[:, cols].bitcast(E5M2), lhsT_scale=g_scales[:, cols],
+                rhs=x_codes[:, first:end].bitcast(E4M3), rhs_scale=x_scales[:, first:end], start=True, stop=True)
+
+        gg0 = sb.tile([P, P * LANES], BF16, name="gg0", align_bytes=64, tag="xg2")
+        weave_g(0, nc.vector.tensor_copy, gg0[:])
+        gg1 = sb.tile([P, P * LANES], BF16, name="gg1", align_bytes=64, tag="xb3")
+        weave_g(1, nc.scalar.copy, gg1[:])
+        quantise_g(0, gg0[:])
+        product(0, 0, D // 2)
+        quantise_x(LANES - 1)
+        product(0, D // 2, D)
+        quantise_g(1, gg1[:])
+        product(1, 0, D)
+        late_gg = sb.tile([P, 2 * P * LANES], BF16, name="late_gg", align_bytes=64, tag="late_w1")
+        weave_g(2, nc.vector.tensor_copy, late_gg[:, :P * LANES])
+        weave_g(3, nc.vector.tensor_copy, late_gg[:, P * LANES:])
+        dw_ps.append(bank(0, "dw3"))
+        for c in (2, 3):
+            quantise_g(c, late_gg[:, (c - 2) * P * LANES:(c - 1) * P * LANES])
+            product(c, 0, D)
         lane0_ps = bank(1, "lane0_ps")
         nc.tensor.matmul_mx(
             out=lane0_ps[:], lhsT=x_codes[:, 0:P].bitcast(E4M3), lhsT_scale=x_scales[:, 0:P],
             rhs=g_codes[:].bitcast(E5M2), rhs_scale=g_scales[:], start=True, stop=True)
 
-        for t in (1, 2, 3):
-            win[t] = sb.tile([P, TABLE], F32, name="win%d" % t, tag="late_w%d" % t, align_bytes=64)
-            nc.gpsimd.memset(win[t][:], 0.0)
 
         first_ps = [bank(2 + h, "first_ps%d" % h) for h in range(2)]
+        lane3_ps = bank(4, "lane3_ps")
         by_slot = {}
 
         def turned(t, h):
-            if t < 3:
-                return first_ps[h][:, (t - 1) * HALF:t * HALF]
-            return lane3_ps[:, h * HALF:(h + 1) * HALF]
+            if t == 3:
+                return lane3_ps[:, h * HALF:(h + 1) * HALF]
+            if (t, h) == (2, 1):
+                return last_ps[:, :HALF]
+            return first_ps[h][:, (t - 1) * HALF:t * HALF]
 
         def turn(t, c):
             h, k = divmod(c, 2)
             nc.tensor.transpose(turned(t, h)[:, k * P:(k + 1) * P], by_slot[c][:, (t - 1) * P:t * P], ident[:])
 
         def copy_and_turn(c, engine_copy):
-            by_slot[c] = sb.tile([P, D - P], F32, name="dw_by_slot%d" % c, tag="root" if c == 3 else "dw_by_slot%d" % c)
+            by_slot[c] = sb.tile([P, D - P], F32, name="dw_by_slot%d" % c, tag="denom" if c == 3 else "dw_by_slot%d" % c)
             engine_copy(by_slot[c][:], dw_ps[c][:, P:])
-            for t in (1, 2):
+            for t in (1, 3, 2) if c < 2 else (1, 3):
                 turn(t, c)
 
         for c in range(4):
-            squares = sb.tile([P, D], BF16, name="squares%d" % c)
+            squares = sb.tile([P, D], BF16, name="squares%d" % c, align_bytes=64,
+                              tag=("squares0", "late_w0", "late_w3", "late_w2")[c])
             nc.scalar.activation(squares[:], dw_ps[c][:], ACT.Square, scale=root_inv_d[:],
                                  accum_out=q_pad[:, COL + c:COL + c + 1])
             if c < 3:
                 copy_and_turn(c, nc.vector.tensor_copy)
-        root = sb.tile([P, 4], F32, name="root", tag="root")
+        for t in (1, 0, 3, 2):
+            win[t] = sb.tile([P, TABLE], F32, name="win%d" % t, tag="late_w%d" % t, align_bytes=64)
+            nc.gpsimd.memset(win[t][:], 0.0)
+        root = sb.tile([P, 4], F32, name="root", tag="raw2")
         for c in range(4):
             nc.scalar.activation(root[:, c:c + 1], q_pad[:, COL + c:COL + c + 1], ACT.Sqrt,
                                  bias=acc_pad[:, COL + c:COL + c + 1])
-        denom = sb.tile([P, 4], F32, name="denom")
+        denom = sb.tile([P, 4], F32, name="denom", tag="denom")
         nc.scalar.activation(denom[:], root[:], ACT.Identity, bias=EPS)
         rinv = sb.tile([P, 4], F32, name="rinv")
         nc.vector.reciprocal(rinv[:], denom[:])
 
-        src = {t: sb.tile([P, SLOTS], F32, name="src%d" % t) for t in (0, 3)}
+        src = {t: sb.tile([P, SLOTS], F32, name="src%d" % t, tag="src%d" % t) for t in (0, 3)}
         nc.vector.tensor_copy(src[0][:], lane0_ps[:])
-        raw2 = sb.tile([P, HALF], F32, name="raw2", tag="raw2")
-        nc.vector.tensor_copy(raw2[:], turned(2, 0))
 
         scaled = {}
-        r_row = sb.tile([P, SLOTS], F32, name="r_row")
+        r_row = sb.tile([P, SLOTS], F32, name="r_row", tag="r_row")
         r_ps = [bank(5 + h, "r_ps%d" % h) for h in range(2)]
         for c in range(4):
             h, k = divmod(c, 2)
             nc.tensor.transpose(r_ps[h][:, k * P:(k + 1) * P], rinv[:, c:c + 1].to_broadcast([P, P]), ident[:])
-        copy_and_turn(3, nc.scalar.copy)
+        copy_and_turn(3, nc.vector.tensor_copy)
+        raw_first = sb.tile([P, 2 * HALF], F32, name="raw_first", tag="raw2")
+        nc.scalar.copy(raw_first[:], first_ps[0][:])
         for h in range(2):
-            half = slice(h * HALF, (h + 1) * HALF)
-            engine_copy = nc.vector.tensor_copy if h else nc.scalar.copy
-            engine_copy(r_row[:, half], r_ps[h][:, 0:HALF])
-        for h in range(2):
-            half = slice(h * HALF, (h + 1) * HALF)
             scaled[1, h] = sb.tile([P, HALF], F32, name="scaled1%d" % h)
-            nc.vector.tensor_tensor(scaled[1, h][:], turned(1, h), r_row[:, half], ALU.mult)
-        scaled[2, 1] = sb.tile([P, HALF], F32, name="scaled21")
-        nc.vector.tensor_tensor(scaled[2, 1][:], turned(2, 1), r_row[:, HALF:], ALU.mult)
-        lane3_ps = bank(5, "lane3_ps")
-        for c in range(4):
-            turn(3, c)
-
-        na_ps = bank(4, "na_ps")
-        nc.tensor.matmul(na_ps[:, 0:P], q_pad[:], ident[:], start=True, stop=False, is_transpose=True)
-        nc.tensor.matmul(na_ps[:, 0:P], acc_pad[:], ident[:], start=False, stop=True, is_transpose=True)
-        na_rows = sb.tile([P, P], F32, name="na_rows")
-        nc.vector.tensor_copy(na_rows[:], na_ps[:, 0:P])
-        nc.sync.dma_start(out_1.rearrange("o (c i) -> (o c) i", c=4), na_rows[COL:P, :])
+        nc.vector.tensor_tensor(scaled[1, 0][:], r_ps[0][:, :HALF], raw_first[:, :HALF], ALU.mult)
+        nc.vector.tensor_copy(r_row[:, :HALF], r_ps[0][:, :HALF])
+        nc.scalar.copy(r_row[:, HALF:], r_ps[1][:, :HALF])
+        nc.vector.tensor_tensor(scaled[1, 1][:], turned(1, 1), r_row[:, HALF:], ALU.mult)
+        nc.vector.tensor_tensor(src[3][:], lane3_ps[:], r_row[:], ALU.mult)
+        last_ps = bank(5, "last_ps")
+        for c in (2, 3):
+            turn(2, c)
 
         out_rows = out_0.rearrange("(m t) c -> m t c", t=LANES)
 
@@ -211,70 +224,81 @@ def tile_attend_grwada_pl_kernel(tc, xT, G, acc, offs, out_0, out_1, out_2, out_
         def store(t):
             nc.sync.dma_start(out_rows[:, t, :], win[t][:])
 
-        pairs = {}
-        for a, b in SCALAR_PIECES:
-            pairs[a] = sb.tile([P, 2, b - a, 2], BF16, name="pairs%d" % a)[:]
-
-        def round_lane(engine_copy, a, b, t):
-            engine_copy(pairs[a][:, t // 2, :, t % 2], win[t][:, a:b])
-
         scalar_scatter(1, 0)
         scalar_scatter(1, 1)
         store(1)
         nc.vector.tensor_tensor(win[0][:].indirect(offsets[:]), src[0][:], r_row[:], ALU.mult)
         store(0)
-        scalar_scatter(2, 1)
-        nc.vector.tensor_tensor(src[3][:], lane3_ps[:], r_row[:], ALU.mult)
-        for t in (0, 1):
-            for a, b in SCALAR_PIECES:
-                round_lane(nc.vector.tensor_copy, a, b, t)
-        nc.vector.tensor_tensor(listed(2, 0), raw2[:], r_row[:, :HALF], ALU.mult)
-        store(2)
         scalar_scatter(3, 0)
         scalar_scatter(3, 1)
         store(3)
+        nc.vector.tensor_tensor(listed(2, 0), raw_first[:, HALF:], r_row[:, :HALF], ALU.mult)
+        scaled[2, 1] = sb.tile([P, HALF], F32, name="scaled21", tag="src0")
+        nc.vector.tensor_tensor(scaled[2, 1][:], turned(2, 1), r_row[:, HALF:], ALU.mult)
+        scalar_scatter(2, 1)
+        store(2)
+        na_ps = bank(6, "na_ps")
+        nc.tensor.matmul(na_ps[:, 0:P], q_pad[:], ident[:], start=True, stop=False, is_transpose=True)
+        nc.tensor.matmul(na_ps[:, 0:P], acc_pad[:], ident[:], start=False, stop=True, is_transpose=True)
+        na_rows = sb.tile([P, P], F32, name="na_rows", tag="src0")
+        nc.scalar.copy(na_rows[:], na_ps[:, 0:P])
+        nc.sync.dma_start(out_1.rearrange("o (c i) -> (o c) i", c=4), na_rows[COL:P, :])
+
+        scalar_pairs = sb.tile([P, 2, TABLE - VECTOR_COLS, 2], BF16, name="scalar_pairs", tag="raw2")
+        vector_pairs = sb.tile([P, 2, VECTOR_COLS, 2], BF16, name="vector_pairs", tag="r_row")
+        for t in (0, 1):
+            nc.vector.tensor_copy(scalar_pairs[:, 0, :, t], win[t][:, VECTOR_COLS:])
+        for t in (0, 1):
+            nc.vector.tensor_copy(vector_pairs[:, 0, :, t], win[t][:, :VECTOR_COLS])
 
 
         words_out = out_2[0].rearrange("p c l -> p (c l)").bitcast(I32)
         y_scales = sb.tile([P, TABLE], U8, name="y_scales", align_bytes=64)
-        grouped = [sb.tile([P, CHUNK * LANES], BF16, name="grouped%d" % k, align_bytes=64) for k in range(4)]
-        y_codes = [sb.tile([P, CHUNK], U32, name="y_codes%d" % k, align_bytes=64) for k in range(4)]
+        grouped = {}
+        y_codes = {k: sb.tile([P, CHUNK], U32, name="y_codes%d" % k, align_bytes=64) for k in range(2)}
 
-        def finish(engine_copy, a, b):
-            for t in (2, 3):
-                round_lane(engine_copy, a, b, t)
-            words = pairs[a].bitcast(F32).rearrange("p u c e -> p c (u e)")
-            k, first = divmod(a, CHUNK)
-            dst = grouped[k][:].bitcast(F32).rearrange("p (c u) -> p c u", u=2)
-            engine_copy(dst[:, first:first + b - a, :], words)
+        def round_lane(engine_copy, pairs, a, b, t):
+            engine_copy(pairs[:, 1, :, t % 2], win[t][:, a:b])
+
+        def weave(engine_copy, pairs, a, b):
+            base, end = [piece for piece in QUANTISED if piece[0] <= a < piece[1]][0]
+            if base not in grouped:
+                grouped[base] = sb.tile([P, (end - base) * LANES], BF16, name="grouped%d" % base, align_bytes=64,
+                                        tag="grouped%d" % base)
+            engine_copy(grouped[base][:, (a - base) * LANES:(b - base) * LANES].bitcast(F32).rearrange("p (c u) -> p c u", u=2),
+                        pairs.bitcast(F32).rearrange("p u c e -> p c (u e)"))
 
         def quantise(a, b):
             k, first = divmod(a, CHUNK)
             nc.vector.quantize_mx(out=y_codes[k][:, first:first + b - a].bitcast(E4M3), scales=y_scales[:, a:b],
-                                  in_=grouped[k][:, first * LANES:(first + b - a) * LANES])
+                                  in_=grouped[a][:])
 
         def store_codes(k):
             nc.sync.dma_start(words_out[:, k * CHUNK:(k + 1) * CHUNK], y_codes[k][:].bitcast(I32))
 
-        vector_cols = VECTOR_PIECES[-1][1]
-        vector_pairs = sb.tile([P, 2, vector_cols, 2], BF16, name="vector_pairs", tag="raw2")
-        for t in (0, 1):
-            nc.vector.tensor_copy(vector_pairs[:, 0, :, t], win[t][:, 0:vector_cols])
-        for a, b in VECTOR_PIECES:
-            pairs[a] = vector_pairs[:, :, a:b, :]
-        for a, b in SCALAR_PIECES:
-            finish(nc.scalar.copy, a, b)
-        finish(nc.vector.tensor_copy, *VECTOR_PIECES[0])
-        finish(nc.vector.tensor_copy, *VECTOR_PIECES[1])
-        quantise(0, 512)
+        for a, b in ((3 * CHUNK, TABLE), (VECTOR_COLS, 3 * CHUNK)):
+            for t in (3, 2):
+                round_lane(nc.scalar.copy, scalar_pairs[:, :, a - VECTOR_COLS:b - VECTOR_COLS, :], a, b, t)
+            for c, d in SCALAR_PIECES:
+                if a <= c < b:
+                    weave(nc.scalar.copy, scalar_pairs[:, :, c - VECTOR_COLS:d - VECTOR_COLS, :], c, d)
+        first, second = vector_pairs[:, :, :CHUNK, :], vector_pairs[:, :, CHUNK:, :]
+        round_lane(nc.vector.tensor_copy, first, 0, CHUNK, 3)
+        round_lane(nc.vector.tensor_copy, first, 0, CHUNK, 2)
+        round_lane(nc.vector.tensor_copy, second, CHUNK, VECTOR_COLS, 3)
+        weave(nc.vector.tensor_copy, first, 0, CHUNK)
+        round_lane(nc.vector.tensor_copy, second, CHUNK, VECTOR_COLS, 2)
+        quantise(0, CHUNK)
         store_codes(0)
-        quantise(1536, 2048)
+        weave(nc.vector.tensor_copy, second[:, :, :CHUNK, :], CHUNK, 2 * CHUNK)
+        y_codes[3] = sb.tile([P, CHUNK], U32, name="y_codes3", align_bytes=64, tag="grouped0")
+        quantise(3 * CHUNK, TABLE)
         store_codes(3)
-        finish(nc.vector.tensor_copy, *VECTOR_PIECES[2])
-        quantise(512, 1024)
+        quantise(CHUNK, 2 * CHUNK)
         store_codes(1)
-        quantise(1280, 1536)
-        quantise(1024, 1280)
+        y_codes[2] = sb.tile([P, CHUNK], U32, name="y_codes2", align_bytes=64, tag="grouped%d" % (3 * CHUNK))
+        for a, b in QUANTISED[3:]:
+            quantise(a, b)
         store_codes(2)
         scales_out = out_3[0].bitcast(I32)
         for q in range(4):

@@ -19,14 +19,15 @@ LANES = 4
 D = 512
 R = 512
 SLOTS = 512
-TABLE = 2048
+BLOCKS = SLOTS // P
 HALF = SLOTS // 2
+TABLE = 2048
 CHUNK = 512
 EPS = 0.001
-COL = P - 4
-VECTOR_COLS = 1024
-SCALAR_PIECES = ((1536, 2048), (1280, 1536), (1152, 1280), (VECTOR_COLS, 1152))
-QUANTISED = ((0, 512), (512, 1024), (1536, 2048), (1280, 1536), (1152, 1280), (1024, 1152))
+BANK = 512
+STAT = P - BLOCKS
+VECTOR_COLS = 2 * CHUNK
+LAST_PIECES = ((1280, 1536), (1152, 1280), (1024, 1152))
 
 FLOPS = 2 * D * R * SLOTS
 BYTES = 4 * (D * R + R * SLOTS + TABLE) + 2 * P * SLOTS // 16 + 4 * (D * TABLE + SLOTS) + D * TABLE + 16 * TABLE
@@ -39,26 +40,26 @@ def tile_attend_grwada_pl_kernel(tc, xT, G, acc, offs, out_0, out_1, out_2, out_
         ps = ctx.enter_context(tc.psum_pool(name="ps", bufs=1))
 
         def bank(b, name):
-            return ps.tile([P, 512], F32, name=name, tag="bank%d" % b)
+            return ps.tile([P, BANK], F32, name=name, tag="bank%d" % b)
 
         x_rows = xT.rearrange("(m t) r -> m t r", t=LANES)
         offsets = sb.tile([P, SLOTS // 16], U16, name="offsets")
-        acc_win = sb.tile([P, TABLE], F32, name="acc_win")
-        nc.vector.memset(acc_win[0:P - 1, :], 0.0)
+        acc_table = sb.tile([P, TABLE], F32, name="acc_table")
+        nc.vector.memset(acc_table[0:P - 1, :], 0.0)
         x_raw = []
         for t in range(LANES):
-            raw = sb.tile([P, R], F32, name="x_raw%d" % t)
-            nc.sync.dma_start(raw[:], x_rows[:, t, :])
-            x_raw.append(raw)
+            x_lane = sb.tile([P, R], F32, name="x_raw%d" % t)
+            nc.sync.dma_start(x_lane[:], x_rows[:, t, :])
+            x_raw.append(x_lane)
             if t == 0:
-                nc.sync.dma_start(acc_win[P - 1:P, :], acc[0:1, :])
+                nc.sync.dma_start(acc_table[P - 1:P, :], acc[0:1, :])
                 nc.sync.dma_start(offsets[:], offs)
         g_rows = G.rearrange("(p j) i -> p j i", j=LANES)
         g_raw = []
         for h in range(2):
-            raw = sb.tile([P, LANES, HALF], F32, name="g_raw%d" % h)
-            nc.sync.dma_start(raw[:], g_rows[:, :, h * HALF:(h + 1) * HALF])
-            g_raw.append(raw)
+            g_half = sb.tile([P, LANES, HALF], F32, name="g_raw%d" % h)
+            nc.sync.dma_start(g_half[:], g_rows[:, :, h * HALF:(h + 1) * HALF])
+            g_raw.append(g_half)
 
         inv_d = sb.tile([P, 1], F32, name="inv_d")
         nc.gpsimd.memset(inv_d[:], 1.0 / D)
@@ -66,55 +67,53 @@ def tile_attend_grwada_pl_kernel(tc, xT, G, acc, offs, out_0, out_1, out_2, out_
         nc.scalar.activation(root_inv_d[:], inv_d[:], ACT.Sqrt)
         ident = sb.tile([P, P], F32, name="ident")
         make_identity(nc, ident[:])
-        q_pad = sb.tile([P, P], F32, name="q_pad")
-        nc.gpsimd.memset(q_pad[:], 0.0)
-        win = {}
+        mean_squares = sb.tile([P, P], F32, name="mean_squares")
+        nc.gpsimd.memset(mean_squares[:], 0.0)
 
-        acc_g = sb.tile([P, SLOTS], F32, name="acc_g")
-        nc.vector.tensor_copy(acc_g[:], acc_win[:].indirect(offsets[:]))
+        acc_listed = sb.tile([P, SLOTS], F32, name="acc_listed")
+        nc.vector.tensor_copy(acc_listed[:], acc_table[:].indirect(offsets[:]))
 
-        x_codes = sb.tile([P, D], U32, name="x_codes", align_bytes=64)
+        x_codes = sb.tile([P, D], U32, name="x_codes", align_bytes=64, tag="window0")
         x_scales = sb.tile([P, D], U8, name="x_scales", align_bytes=64)
-        xb = {}
+        x_cast = {}
         for t in (2, 3, 0, 1):
-            xb[t] = sb.tile([P, 2, P, 2], BF16, name="xb%d" % t, tag="xb%d" % t, align_bytes=64)
+            x_cast[t] = sb.tile([P, 2, P, 2], BF16, name="x_cast%d" % t, tag="x_cast%d" % t, align_bytes=64)
             engine_copy = nc.vector.tensor_copy if t >= 2 else nc.scalar.copy
-            engine_copy(xb[t][:], x_raw[t][:].rearrange("m (p u e) -> m u p e", u=2, e=2))
-        x_grouped = []
+            engine_copy(x_cast[t][:], x_raw[t][:].rearrange("m (p u e) -> m u p e", u=2, e=2))
+        x_woven = []
 
         def quantise_x(t):
             cols = slice(t * P, (t + 1) * P)
-            nc.vector.quantize_mx(out=x_codes[:, cols].bitcast(E4M3), scales=x_scales[:, cols], in_=x_grouped[t][:])
+            nc.vector.quantize_mx(out=x_codes[:, cols].bitcast(E4M3), scales=x_scales[:, cols], in_=x_woven[t][:])
 
         for t in range(LANES):
-            words = xb[t][:].rearrange("m u p e -> m (u p e)").bitcast(F32)
-            xt = bank(t, "xt%d" % t)
+            x_words = x_cast[t][:].rearrange("m u p e -> m (u p e)").bitcast(F32)
+            x_ps = bank(t, "x_ps%d" % t)
             for u in range(2):
-                nc.tensor.transpose(xt[:, u * P:(u + 1) * P], words[:, u * P:(u + 1) * P], ident[:])
-            xg = sb.tile([P, LANES * P], BF16, name="xg%d" % t, align_bytes=64,
-                         tag="late_w1" if t == 3 else "xg%d" % t)
+                nc.tensor.transpose(x_ps[:, u * P:(u + 1) * P], x_words[:, u * P:(u + 1) * P], ident[:])
+            x_woven.append(sb.tile([P, LANES * P], BF16, name="x_woven%d" % t, align_bytes=64,
+                                   tag="window1" if t == LANES - 1 else "x_woven%d" % t))
             nc.scalar.copy(
-                xg[:].bitcast(F32).rearrange("p (m u) -> p m u", u=2),
-                xt[:, 0:2 * P].rearrange("p (u m) -> p m u", u=2))
-            x_grouped.append(xg)
+                x_woven[t][:].bitcast(F32).rearrange("p (m u) -> p m u", u=2),
+                x_ps[:, 0:2 * P].rearrange("p (u m) -> p m u", u=2))
             if t < LANES - 1:
                 quantise_x(t)
 
-        acc_t = bank(2, "acc_t")
-        for c in range(4):
-            nc.tensor.transpose(acc_t[:, c * P:(c + 1) * P], acc_g[:, c * P:(c + 1) * P], ident[:])
-        acc_pad = sb.tile([P, P], F32, name="acc_pad")
-        nc.scalar.copy(acc_pad[:].rearrange("p (k c) -> p k c", c=4),
-                       acc_t[:].rearrange("p (c k) -> p k c", c=4)[:, P - P // 4:P, :])
+        acc_ps = bank(2, "acc_ps")
+        for c in range(BLOCKS):
+            nc.tensor.transpose(acc_ps[:, c * P:(c + 1) * P], acc_listed[:, c * P:(c + 1) * P], ident[:])
+        acc_cols = sb.tile([P, P], F32, name="acc_cols")
+        nc.scalar.copy(acc_cols[:].rearrange("p (m c) -> p m c", c=BLOCKS),
+                       acc_ps[:].rearrange("p (c m) -> p m c", c=BLOCKS)[:, P - P // BLOCKS:P, :])
 
-        g_codes = sb.tile([P, SLOTS], U32, name="g_codes", align_bytes=64)
-        g_scales = sb.tile([P, SLOTS], U8, name="g_scales", align_bytes=64)
-        dw_ps = [bank((5 + c) % 8, "dw%d" % c) for c in range(3)]
+        g_codes = sb.tile([P, SLOTS], U32, name="g_codes", align_bytes=64, tag="window3")
+        g_scales = sb.tile([P, SLOTS], U8, name="g_scales", align_bytes=64, tag="window2")
+        dw_ps = [bank(5 + c, "dw_ps%d" % c) for c in range(BLOCKS - 1)]
 
-        def weave_g(c, engine_copy, dst):
-            h, k = divmod(c, 2)
-            engine_copy(dst.rearrange("p (c i j) -> p c j i", i=4, j=LANES),
-                        g_raw[h][:, :, k * P:(k + 1) * P].rearrange("p j (c i) -> p c j i", i=4))
+        def weave_g(c, engine_copy, woven):
+            h, in_half = divmod(c, 2)
+            engine_copy(woven.rearrange("p (g i j) -> p g j i", i=4, j=LANES),
+                        g_raw[h][:, :, in_half * P:(in_half + 1) * P].rearrange("p j (g i) -> p g j i", i=4))
 
         def quantise_g(c, woven):
             cols = slice(c * P, (c + 1) * P)
@@ -126,180 +125,187 @@ def tile_attend_grwada_pl_kernel(tc, xT, G, acc, offs, out_0, out_1, out_2, out_
                 out=dw_ps[c][:, first:end], lhsT=g_codes[:, cols].bitcast(E5M2), lhsT_scale=g_scales[:, cols],
                 rhs=x_codes[:, first:end].bitcast(E4M3), rhs_scale=x_scales[:, first:end], start=True, stop=True)
 
-        gg0 = sb.tile([P, P * LANES], BF16, name="gg0", align_bytes=64, tag="xg2")
-        weave_g(0, nc.vector.tensor_copy, gg0[:])
-        gg1 = sb.tile([P, P * LANES], BF16, name="gg1", align_bytes=64, tag="xb3")
-        weave_g(1, nc.scalar.copy, gg1[:])
-        quantise_g(0, gg0[:])
+        g_woven0 = sb.tile([P, P * LANES], BF16, name="g_woven0", align_bytes=64, tag="x_woven2")
+        weave_g(0, nc.vector.tensor_copy, g_woven0[:])
+        g_woven1 = sb.tile([P, P * LANES], BF16, name="g_woven1", align_bytes=64, tag="x_cast3")
+        weave_g(1, nc.scalar.copy, g_woven1[:])
+        quantise_g(0, g_woven0[:])
         product(0, 0, D // 2)
         quantise_x(LANES - 1)
         product(0, D // 2, D)
-        quantise_g(1, gg1[:])
+        quantise_g(1, g_woven1[:])
         product(1, 0, D)
-        late_gg = sb.tile([P, 2 * P * LANES], BF16, name="late_gg", align_bytes=64, tag="late_w1")
-        weave_g(2, nc.vector.tensor_copy, late_gg[:, :P * LANES])
-        weave_g(3, nc.vector.tensor_copy, late_gg[:, P * LANES:])
-        dw_ps.append(bank(0, "dw3"))
+        g_woven23 = sb.tile([P, 2 * P * LANES], BF16, name="g_woven23", align_bytes=64, tag="window1")
         for c in (2, 3):
-            quantise_g(c, late_gg[:, (c - 2) * P * LANES:(c - 1) * P * LANES])
+            weave_g(c, nc.vector.tensor_copy, g_woven23[:, (c - 2) * P * LANES:(c - 1) * P * LANES])
+        dw_ps.append(bank(0, "dw_ps3"))
+        for c in (2, 3):
+            quantise_g(c, g_woven23[:, (c - 2) * P * LANES:(c - 1) * P * LANES])
             product(c, 0, D)
         lane0_ps = bank(1, "lane0_ps")
         nc.tensor.matmul_mx(
             out=lane0_ps[:], lhsT=x_codes[:, 0:P].bitcast(E4M3), lhsT_scale=x_scales[:, 0:P],
             rhs=g_codes[:].bitcast(E5M2), rhs_scale=g_scales[:], start=True, stop=True)
 
-
-        first_ps = [bank(2 + h, "first_ps%d" % h) for h in range(2)]
+        half_ps = [bank(2 + h, "half_ps%d" % h) for h in range(2)]
         lane3_ps = bank(4, "lane3_ps")
-        by_slot = {}
+        dw_rows = {}
 
         def turned(t, h):
             if t == 3:
                 return lane3_ps[:, h * HALF:(h + 1) * HALF]
             if (t, h) == (2, 1):
-                return last_ps[:, :HALF]
-            return first_ps[h][:, (t - 1) * HALF:t * HALF]
+                return lane2_late_ps[:, :HALF]
+            return half_ps[h][:, (t - 1) * HALF:t * HALF]
 
         def turn(t, c):
-            h, k = divmod(c, 2)
-            nc.tensor.transpose(turned(t, h)[:, k * P:(k + 1) * P], by_slot[c][:, (t - 1) * P:t * P], ident[:])
+            h, in_half = divmod(c, 2)
+            nc.tensor.transpose(turned(t, h)[:, in_half * P:(in_half + 1) * P],
+                                dw_rows[c][:, (t - 1) * P:t * P], ident[:])
 
-        def copy_and_turn(c, engine_copy):
-            by_slot[c] = sb.tile([P, D - P], F32, name="dw_by_slot%d" % c, tag="denom" if c == 3 else "dw_by_slot%d" % c)
-            engine_copy(by_slot[c][:], dw_ps[c][:, P:])
+        def copy_and_turn(c):
+            dw_rows[c] = sb.tile([P, D - P], F32, name="dw_rows%d" % c)
+            nc.vector.tensor_copy(dw_rows[c][:], dw_ps[c][:, P:])
             for t in (1, 3, 2) if c < 2 else (1, 3):
                 turn(t, c)
 
-        for c in range(4):
-            squares = sb.tile([P, D], BF16, name="squares%d" % c, align_bytes=64,
-                              tag=("squares0", "late_w0", "late_w3", "late_w2")[c])
+        for c in range(BLOCKS):
+            squares = sb.tile([P, D], BF16, name="squares%d" % c)
             nc.scalar.activation(squares[:], dw_ps[c][:], ACT.Square, scale=root_inv_d[:],
-                                 accum_out=q_pad[:, COL + c:COL + c + 1])
-            if c < 3:
-                copy_and_turn(c, nc.vector.tensor_copy)
+                                 accum_out=mean_squares[:, STAT + c:STAT + c + 1])
+            copy_and_turn(c)
+
+        window = {}
         for t in (1, 0, 3, 2):
-            win[t] = sb.tile([P, TABLE], F32, name="win%d" % t, tag="late_w%d" % t, align_bytes=64)
-            nc.gpsimd.memset(win[t][:], 0.0)
-        root = sb.tile([P, 4], F32, name="root", tag="raw2")
-        for c in range(4):
-            nc.scalar.activation(root[:, c:c + 1], q_pad[:, COL + c:COL + c + 1], ACT.Sqrt,
-                                 bias=acc_pad[:, COL + c:COL + c + 1])
-        denom = sb.tile([P, 4], F32, name="denom", tag="denom")
+            window[t] = sb.tile([P, TABLE], F32, name="window%d" % t, tag="window%d" % t, align_bytes=64)
+            nc.gpsimd.memset(window[t][:], 0.0)
+
+        root = sb.tile([P, BLOCKS], F32, name="root", tag="raw_half0")
+        for c in range(BLOCKS):
+            nc.scalar.activation(root[:, c:c + 1], mean_squares[:, STAT + c:STAT + c + 1], ACT.Sqrt,
+                                 bias=acc_cols[:, STAT + c:STAT + c + 1])
+        denom = sb.tile([P, BLOCKS], F32, name="denom", tag="raw_lane0")
         nc.scalar.activation(denom[:], root[:], ACT.Identity, bias=EPS)
-        rinv = sb.tile([P, 4], F32, name="rinv")
-        nc.vector.reciprocal(rinv[:], denom[:])
+        factor = sb.tile([P, BLOCKS], F32, name="factor")
+        nc.vector.reciprocal(factor[:], denom[:])
 
-        src = {t: sb.tile([P, SLOTS], F32, name="src%d" % t, tag="src%d" % t) for t in (0, 3)}
-        nc.vector.tensor_copy(src[0][:], lane0_ps[:])
+        raw_lane0 = sb.tile([P, SLOTS], F32, name="raw_lane0", tag="raw_lane0")
+        scaled_lane3 = sb.tile([P, SLOTS], F32, name="scaled_lane3")
+        nc.vector.tensor_copy(raw_lane0[:], lane0_ps[:])
 
-        scaled = {}
-        r_row = sb.tile([P, SLOTS], F32, name="r_row", tag="r_row")
-        r_ps = [bank(5 + h, "r_ps%d" % h) for h in range(2)]
-        for c in range(4):
-            h, k = divmod(c, 2)
-            nc.tensor.transpose(r_ps[h][:, k * P:(k + 1) * P], rinv[:, c:c + 1].to_broadcast([P, P]), ident[:])
-        copy_and_turn(3, nc.vector.tensor_copy)
-        raw_first = sb.tile([P, 2 * HALF], F32, name="raw_first", tag="raw2")
-        nc.scalar.copy(raw_first[:], first_ps[0][:])
+        factor_row = sb.tile([P, SLOTS], F32, name="factor_row", tag="factor_row")
+        factor_ps = [bank(5 + h, "factor_ps%d" % h) for h in range(2)]
+        for c in range(BLOCKS):
+            h, in_half = divmod(c, 2)
+            nc.tensor.transpose(factor_ps[h][:, in_half * P:(in_half + 1) * P],
+                                factor[:, c:c + 1].to_broadcast([P, P]), ident[:])
+        raw_half0 = sb.tile([P, 2 * HALF], F32, name="raw_half0", tag="raw_half0")
+        nc.scalar.copy(raw_half0[:], half_ps[0][:])
+
+        scaled = {(1, h): sb.tile([P, HALF], F32, name="scaled1%d" % h)[:] for h in range(2)}
+        nc.vector.tensor_tensor(scaled[1, 0], factor_ps[0][:, :HALF], raw_half0[:, :HALF], ALU.mult)
+        nc.vector.tensor_copy(factor_row[:, :HALF], factor_ps[0][:, :HALF])
+        nc.scalar.copy(factor_row[:, HALF:], factor_ps[1][:, :HALF])
+        nc.vector.tensor_tensor(scaled[1, 1], turned(1, 1), factor_row[:, HALF:], ALU.mult)
+        nc.vector.tensor_tensor(scaled_lane3[:], lane3_ps[:], factor_row[:], ALU.mult)
         for h in range(2):
-            scaled[1, h] = sb.tile([P, HALF], F32, name="scaled1%d" % h)
-        nc.vector.tensor_tensor(scaled[1, 0][:], r_ps[0][:, :HALF], raw_first[:, :HALF], ALU.mult)
-        nc.vector.tensor_copy(r_row[:, :HALF], r_ps[0][:, :HALF])
-        nc.scalar.copy(r_row[:, HALF:], r_ps[1][:, :HALF])
-        nc.vector.tensor_tensor(scaled[1, 1][:], turned(1, 1), r_row[:, HALF:], ALU.mult)
-        nc.vector.tensor_tensor(src[3][:], lane3_ps[:], r_row[:], ALU.mult)
-        last_ps = bank(5, "last_ps")
+            scaled[3, h] = scaled_lane3[:, h * HALF:(h + 1) * HALF]
+        lane2_late_ps = bank(5, "lane2_late_ps")
         for c in (2, 3):
             turn(2, c)
 
-        out_rows = out_0.rearrange("(m t) c -> m t c", t=LANES)
+        out_rows = out_0.rearrange("(m t) col -> m t col", t=LANES)
 
         def listed(t, h):
-            return win[t][:].indirect(offsets[:, h * HALF // 16:(h + 1) * HALF // 16])
+            return window[t][:].indirect(offsets[:, h * HALF // 16:(h + 1) * HALF // 16])
 
         def scalar_scatter(t, h):
-            values = src[3][:, h * HALF:(h + 1) * HALF] if t == 3 else scaled[t, h][:]
-            nc.scalar.activation(listed(t, h), values, ACT.Copy)
+            nc.scalar.activation(listed(t, h), scaled[t, h], ACT.Copy)
 
-        def store(t):
-            nc.sync.dma_start(out_rows[:, t, :], win[t][:])
+        def store_window(t):
+            nc.sync.dma_start(out_rows[:, t, :], window[t][:])
 
         scalar_scatter(1, 0)
         scalar_scatter(1, 1)
-        store(1)
-        nc.vector.tensor_tensor(win[0][:].indirect(offsets[:]), src[0][:], r_row[:], ALU.mult)
-        store(0)
+        store_window(1)
+        nc.vector.tensor_tensor(window[0][:].indirect(offsets[:]), raw_lane0[:], factor_row[:], ALU.mult)
+        store_window(0)
+
+        na_ps = bank(6, "na_ps")
+        nc.tensor.matmul(na_ps[:, 0:P], mean_squares[:], ident[:], start=True, stop=False, is_transpose=True)
+        nc.tensor.matmul(na_ps[:, 0:P], acc_cols[:], ident[:], start=False, stop=True, is_transpose=True)
+        na_rows = sb.tile([P, P], F32, name="na_rows")
+        nc.scalar.copy(na_rows[:], na_ps[:, 0:P])
+        nc.sync.dma_start(out_1.rearrange("o (c i) -> (o c) i", c=BLOCKS), na_rows[STAT:P, :])
+
         scalar_scatter(3, 0)
         scalar_scatter(3, 1)
-        store(3)
-        nc.vector.tensor_tensor(listed(2, 0), raw_first[:, HALF:], r_row[:, :HALF], ALU.mult)
-        scaled[2, 1] = sb.tile([P, HALF], F32, name="scaled21", tag="src0")
-        nc.vector.tensor_tensor(scaled[2, 1][:], turned(2, 1), r_row[:, HALF:], ALU.mult)
+        store_window(3)
+        scaled[2, 1] = sb.tile([P, HALF], F32, name="scaled21")[:]
+        nc.vector.tensor_tensor(scaled[2, 1], turned(2, 1), factor_row[:, HALF:], ALU.mult)
+        nc.vector.tensor_tensor(listed(2, 0), raw_half0[:, HALF:], factor_row[:, :HALF], ALU.mult)
         scalar_scatter(2, 1)
-        store(2)
-        na_ps = bank(6, "na_ps")
-        nc.tensor.matmul(na_ps[:, 0:P], q_pad[:], ident[:], start=True, stop=False, is_transpose=True)
-        nc.tensor.matmul(na_ps[:, 0:P], acc_pad[:], ident[:], start=False, stop=True, is_transpose=True)
-        na_rows = sb.tile([P, P], F32, name="na_rows", tag="src0")
-        nc.scalar.copy(na_rows[:], na_ps[:, 0:P])
-        nc.sync.dma_start(out_1.rearrange("o (c i) -> (o c) i", c=4), na_rows[COL:P, :])
+        store_window(2)
 
-        scalar_pairs = sb.tile([P, 2, TABLE - VECTOR_COLS, 2], BF16, name="scalar_pairs", tag="raw2")
-        vector_pairs = sb.tile([P, 2, VECTOR_COLS, 2], BF16, name="vector_pairs", tag="r_row")
+        scalar_pairs = sb.tile([P, 2, TABLE - VECTOR_COLS, 2], BF16, name="scalar_pairs", tag="raw_half0")
+        vector_pairs = sb.tile([P, 2, VECTOR_COLS, 2], BF16, name="vector_pairs", tag="factor_row")
         for t in (0, 1):
-            nc.vector.tensor_copy(scalar_pairs[:, 0, :, t], win[t][:, VECTOR_COLS:])
+            nc.vector.tensor_copy(scalar_pairs[:, 0, :, t], window[t][:, VECTOR_COLS:])
         for t in (0, 1):
-            nc.vector.tensor_copy(vector_pairs[:, 0, :, t], win[t][:, :VECTOR_COLS])
+            nc.vector.tensor_copy(vector_pairs[:, 0, :, t], window[t][:, :VECTOR_COLS])
 
-
-        words_out = out_2[0].rearrange("p c l -> p (c l)").bitcast(I32)
+        words_out = out_2[0].rearrange("p col t -> p (col t)").bitcast(I32)
         y_scales = sb.tile([P, TABLE], U8, name="y_scales", align_bytes=64)
-        grouped = {}
+        y_woven = {}
         y_codes = {k: sb.tile([P, CHUNK], U32, name="y_codes%d" % k, align_bytes=64) for k in range(2)}
 
-        def round_lane(engine_copy, pairs, a, b, t):
-            engine_copy(pairs[:, 1, :, t % 2], win[t][:, a:b])
+        def pairs_of(first, end):
+            if first < VECTOR_COLS:
+                return vector_pairs[:, :, first:end, :]
+            return scalar_pairs[:, :, first - VECTOR_COLS:end - VECTOR_COLS, :]
 
-        def weave(engine_copy, pairs, a, b):
-            base, end = [piece for piece in QUANTISED if piece[0] <= a < piece[1]][0]
-            if base not in grouped:
-                grouped[base] = sb.tile([P, (end - base) * LANES], BF16, name="grouped%d" % base, align_bytes=64,
-                                        tag="grouped%d" % base)
-            engine_copy(grouped[base][:, (a - base) * LANES:(b - base) * LANES].bitcast(F32).rearrange("p (c u) -> p c u", u=2),
-                        pairs.bitcast(F32).rearrange("p u c e -> p c (u e)"))
+        def round_lane(engine_copy, t, first, end):
+            engine_copy(pairs_of(first, end)[:, t // 2, :, t % 2], window[t][:, first:end])
 
-        def quantise(a, b):
-            k, first = divmod(a, CHUNK)
-            nc.vector.quantize_mx(out=y_codes[k][:, first:first + b - a].bitcast(E4M3), scales=y_scales[:, a:b],
-                                  in_=grouped[a][:])
+        def weave_pairs(engine_copy, first, end):
+            y_woven[first] = sb.tile([P, (end - first) * LANES], BF16, name="y_woven%d" % first, align_bytes=64,
+                                     tag="y_woven%d" % first)
+            engine_copy(y_woven[first][:].bitcast(F32).rearrange("p (col u) -> p col u", u=2),
+                        pairs_of(first, end).bitcast(F32).rearrange("p u col e -> p col (u e)"))
+
+        def quantise_y(first, end):
+            k, offset = divmod(first, CHUNK)
+            nc.vector.quantize_mx(out=y_codes[k][:, offset:offset + end - first].bitcast(E4M3),
+                                  scales=y_scales[:, first:end], in_=y_woven[first][:])
 
         def store_codes(k):
             nc.sync.dma_start(words_out[:, k * CHUNK:(k + 1) * CHUNK], y_codes[k][:].bitcast(I32))
 
-        for a, b in ((3 * CHUNK, TABLE), (VECTOR_COLS, 3 * CHUNK)):
+        chunk = [(k * CHUNK, (k + 1) * CHUNK) for k in range(TABLE // CHUNK)]
+        for k, pieces in ((3, (chunk[3],)), (2, LAST_PIECES)):
             for t in (3, 2):
-                round_lane(nc.scalar.copy, scalar_pairs[:, :, a - VECTOR_COLS:b - VECTOR_COLS, :], a, b, t)
-            for c, d in SCALAR_PIECES:
-                if a <= c < b:
-                    weave(nc.scalar.copy, scalar_pairs[:, :, c - VECTOR_COLS:d - VECTOR_COLS, :], c, d)
-        first, second = vector_pairs[:, :, :CHUNK, :], vector_pairs[:, :, CHUNK:, :]
-        round_lane(nc.vector.tensor_copy, first, 0, CHUNK, 3)
-        round_lane(nc.vector.tensor_copy, first, 0, CHUNK, 2)
-        round_lane(nc.vector.tensor_copy, second, CHUNK, VECTOR_COLS, 3)
-        weave(nc.vector.tensor_copy, first, 0, CHUNK)
-        round_lane(nc.vector.tensor_copy, second, CHUNK, VECTOR_COLS, 2)
-        quantise(0, CHUNK)
+                round_lane(nc.scalar.copy, t, *chunk[k])
+            for piece in pieces:
+                weave_pairs(nc.scalar.copy, *piece)
+
+        round_lane(nc.vector.tensor_copy, 3, *chunk[0])
+        round_lane(nc.vector.tensor_copy, 2, *chunk[0])
+        round_lane(nc.vector.tensor_copy, 3, *chunk[1])
+        weave_pairs(nc.vector.tensor_copy, *chunk[0])
+        round_lane(nc.vector.tensor_copy, 2, *chunk[1])
+        quantise_y(*chunk[0])
         store_codes(0)
-        weave(nc.vector.tensor_copy, second[:, :, :CHUNK, :], CHUNK, 2 * CHUNK)
-        y_codes[3] = sb.tile([P, CHUNK], U32, name="y_codes3", align_bytes=64, tag="grouped0")
-        quantise(3 * CHUNK, TABLE)
+        weave_pairs(nc.vector.tensor_copy, *chunk[1])
+        y_codes[3] = sb.tile([P, CHUNK], U32, name="y_codes3", align_bytes=64, tag="y_woven%d" % chunk[0][0])
+        quantise_y(*chunk[3])
         store_codes(3)
-        quantise(CHUNK, 2 * CHUNK)
+        quantise_y(*chunk[1])
         store_codes(1)
-        y_codes[2] = sb.tile([P, CHUNK], U32, name="y_codes2", align_bytes=64, tag="grouped%d" % (3 * CHUNK))
-        for a, b in QUANTISED[3:]:
-            quantise(a, b)
+        y_codes[2] = sb.tile([P, CHUNK], U32, name="y_codes2", align_bytes=64, tag="y_woven%d" % chunk[3][0])
+        for piece in LAST_PIECES:
+            quantise_y(*piece)
         store_codes(2)
+
         scales_out = out_3[0].bitcast(I32)
         for q in range(4):
             queue = nc.scalar if q % 2 else nc.sync

@@ -26,7 +26,7 @@ CHUNK = 512
 EPS = 0.001
 BANK = 512
 STAT = P - BLOCKS
-VECTOR_COLS = 2 * CHUNK
+VECTOR_COLS = 1088
 LAST_PIECES = ((1280, 1536), (1152, 1280), (1024, 1152))
 
 FLOPS = 2 * D * R * SLOTS
@@ -267,10 +267,12 @@ def tile_attend_grwada_pl_kernel(tc, xT, G, acc, offs, out_0, out_1, out_2, out_
         def round_lane(engine_copy, t, first, end):
             engine_copy(pairs_of(first, end)[:, t // 2, :, t % 2], window[t][:, first:end])
 
-        def weave_pairs(engine_copy, first, end):
-            y_woven[first] = sb.tile([P, (end - first) * LANES], BF16, name="y_woven%d" % first, align_bytes=64,
-                                     tag="y_woven%d" % first)
-            engine_copy(y_woven[first][:].bitcast(F32).rearrange("p (col u) -> p col u", u=2),
+        def weave_pairs(engine_copy, piece, first, end):
+            start, stop = piece
+            if start not in y_woven:
+                y_woven[start] = sb.tile([P, (stop - start) * LANES], BF16, name="y_woven%d" % start,
+                                         align_bytes=64, tag="y_woven%d" % start)
+            engine_copy(y_woven[start][:, (first - start) * LANES:(end - start) * LANES].bitcast(F32).rearrange("p (col u) -> p col u", u=2),
                         pairs_of(first, end).bitcast(F32).rearrange("p u col e -> p col (u e)"))
 
         def quantise_y(first, end):
@@ -282,20 +284,21 @@ def tile_attend_grwada_pl_kernel(tc, xT, G, acc, offs, out_0, out_1, out_2, out_
             nc.sync.dma_start(words_out[:, k * CHUNK:(k + 1) * CHUNK], y_codes[k][:].bitcast(I32))
 
         chunk = [(k * CHUNK, (k + 1) * CHUNK) for k in range(TABLE // CHUNK)]
-        for k, pieces in ((3, (chunk[3],)), (2, LAST_PIECES)):
+        for (first, end), pieces in ((chunk[3], (chunk[3],)), ((VECTOR_COLS, chunk[2][1]), LAST_PIECES)):
             for t in (3, 2):
-                round_lane(nc.scalar.copy, t, *chunk[k])
+                round_lane(nc.scalar.copy, t, first, end)
             for piece in pieces:
-                weave_pairs(nc.scalar.copy, *piece)
+                weave_pairs(nc.scalar.copy, piece, max(piece[0], first), piece[1])
 
         round_lane(nc.vector.tensor_copy, 3, *chunk[0])
         round_lane(nc.vector.tensor_copy, 2, *chunk[0])
-        round_lane(nc.vector.tensor_copy, 3, *chunk[1])
-        weave_pairs(nc.vector.tensor_copy, *chunk[0])
-        round_lane(nc.vector.tensor_copy, 2, *chunk[1])
+        round_lane(nc.vector.tensor_copy, 3, CHUNK, VECTOR_COLS)
+        weave_pairs(nc.vector.tensor_copy, chunk[0], *chunk[0])
+        round_lane(nc.vector.tensor_copy, 2, CHUNK, VECTOR_COLS)
         quantise_y(*chunk[0])
         store_codes(0)
-        weave_pairs(nc.vector.tensor_copy, *chunk[1])
+        weave_pairs(nc.vector.tensor_copy, chunk[1], *chunk[1])
+        weave_pairs(nc.vector.tensor_copy, LAST_PIECES[-1], chunk[2][0], VECTOR_COLS)
         y_codes[3] = sb.tile([P, CHUNK], U32, name="y_codes3", align_bytes=64, tag="y_woven%d" % chunk[0][0])
         quantise_y(*chunk[3])
         store_codes(3)

@@ -26,8 +26,8 @@ CHUNK = 512
 EPS = 0.001
 BANK = 512
 STAT = P - BLOCKS
-VECTOR_COLS = 1088
-LAST_PIECES = ((1280, 1536), (1152, 1280), (1024, 1152))
+V_END = 768
+GP_END = 1280
 
 FLOPS = 2 * D * R * SLOTS
 BYTES = 4 * (D * R + R * SLOTS + TABLE) + 2 * P * SLOTS // 16 + 4 * (D * TABLE + SLOTS) + D * TABLE + 16 * TABLE
@@ -46,6 +46,8 @@ def tile_attend_grwada_pl_kernel(tc, xT, G, acc, offs, out_0, out_1, out_2, out_
         offsets = sb.tile([P, SLOTS // 16], U16, name="offsets")
         acc_table = sb.tile([P, TABLE], F32, name="acc_table")
         nc.vector.memset(acc_table[0:P - 1, :], 0.0)
+        window = {0: sb.tile([P, TABLE], F32, name="window0", align_bytes=64)}
+        nc.vector.memset(window[0][:, :TABLE // 2], 0.0)
         x_raw = []
         for t in range(LANES):
             x_lane = sb.tile([P, R], F32, name="x_raw%d" % t)
@@ -69,11 +71,14 @@ def tile_attend_grwada_pl_kernel(tc, xT, G, acc, offs, out_0, out_1, out_2, out_
         make_identity(nc, ident[:])
         mean_squares = sb.tile([P, P], F32, name="mean_squares")
         nc.gpsimd.memset(mean_squares[:], 0.0)
+        nc.gpsimd.memset(window[0][:, TABLE // 2:], 0.0)
+        eps_cols = sb.tile([P, 2], F32, name="eps_cols")
+        nc.scalar.activation(eps_cols[:], mean_squares[:, 0:2], ACT.Identity, bias=EPS)
 
         acc_listed = sb.tile([P, SLOTS], F32, name="acc_listed")
         nc.vector.tensor_copy(acc_listed[:], acc_table[:].indirect(offsets[:]))
 
-        x_codes = sb.tile([P, D], U32, name="x_codes", align_bytes=64, tag="window0")
+        x_codes = sb.tile([P, D], U32, name="x_codes", align_bytes=64)
         x_scales = sb.tile([P, D], U8, name="x_scales", align_bytes=64)
         x_cast = {}
         for t in (2, 3, 0, 1):
@@ -135,179 +140,200 @@ def tile_attend_grwada_pl_kernel(tc, xT, G, acc, offs, out_0, out_1, out_2, out_
         product(0, D // 2, D)
         quantise_g(1, g_woven1[:])
         product(1, 0, D)
+
+        def lane0_product(h, b):
+            out = bank(b, "lane0_ps%d" % h)
+            cols = slice(h * HALF, (h + 1) * HALF)
+            nc.tensor.matmul_mx(
+                out=out[:, :HALF], lhsT=x_codes[:, 0:P].bitcast(E4M3), lhsT_scale=x_scales[:, 0:P],
+                rhs=g_codes[:, cols].bitcast(E5M2), rhs_scale=g_scales[:, cols], start=True, stop=True)
+            return out
+
+        lane0_ps = [lane0_product(0, 0)]
         g_woven23 = sb.tile([P, 2 * P * LANES], BF16, name="g_woven23", align_bytes=64, tag="window1")
         for c in (2, 3):
             weave_g(c, nc.vector.tensor_copy, g_woven23[:, (c - 2) * P * LANES:(c - 1) * P * LANES])
-        dw_ps.append(bank(0, "dw_ps3"))
+        dw_ps.append(bank(1, "dw_ps3"))
         for c in (2, 3):
             quantise_g(c, g_woven23[:, (c - 2) * P * LANES:(c - 1) * P * LANES])
             product(c, 0, D)
-        lane0_ps = bank(1, "lane0_ps")
-        nc.tensor.matmul_mx(
-            out=lane0_ps[:], lhsT=x_codes[:, 0:P].bitcast(E4M3), lhsT_scale=x_scales[:, 0:P],
-            rhs=g_codes[:].bitcast(E5M2), rhs_scale=g_scales[:], start=True, stop=True)
 
-        half_ps = [bank(2 + h, "half_ps%d" % h) for h in range(2)]
-        lane3_ps = bank(4, "lane3_ps")
         dw_rows = {}
 
-        def turned(t, h):
-            if t == 3:
-                return lane3_ps[:, h * HALF:(h + 1) * HALF]
-            if (t, h) == (2, 1):
-                return lane2_late_ps[:, :HALF]
-            return half_ps[h][:, (t - 1) * HALF:t * HALF]
-
-        def turn(t, c):
-            h, in_half = divmod(c, 2)
-            nc.tensor.transpose(turned(t, h)[:, in_half * P:(in_half + 1) * P],
-                                dw_rows[c][:, (t - 1) * P:t * P], ident[:])
-
-        def copy_and_turn(c):
-            dw_rows[c] = sb.tile([P, D - P], F32, name="dw_rows%d" % c)
-            nc.vector.tensor_copy(dw_rows[c][:], dw_ps[c][:, P:])
-            for t in (1, 3, 2) if c < 2 else (1, 3):
-                turn(t, c)
-
-        for c in range(BLOCKS):
-            squares = sb.tile([P, D], BF16, name="squares%d" % c)
+        def square(c, tag):
+            squares = sb.tile([P, D], BF16, name="squares%d" % c, tag=tag)
             nc.scalar.activation(squares[:], dw_ps[c][:], ACT.Square, scale=root_inv_d[:],
                                  accum_out=mean_squares[:, STAT + c:STAT + c + 1])
-            copy_and_turn(c)
 
-        window = {}
-        for t in (1, 0, 3, 2):
+        def copy_rows(engine_copy, c):
+            dw_rows[c] = sb.tile([P, D - P], F32, name="dw_rows%d" % c)
+            engine_copy(dw_rows[c][:], dw_ps[c][:, P:])
+
+        def turn(out, t, h):
+            for in_half in range(2):
+                nc.tensor.transpose(out[:, in_half * P:(in_half + 1) * P],
+                                    dw_rows[2 * h + in_half][:, (t - 1) * P:t * P], ident[:])
+
+        def roots(h):
+            root = sb.tile([P, 2], F32, name="root%d" % h)
+            for i in range(2):
+                col = STAT + 2 * h + i
+                nc.scalar.activation(root[:, i:i + 1], mean_squares[:, col:col + 1], ACT.Sqrt, bias=acc_cols[:, col:col + 1])
+            return root
+
+        def add_eps(h, root):
+            denom = sb.tile([P, 2], F32, name="denom%d" % h)
+            nc.vector.tensor_tensor(denom[:], root[:], eps_cols[:], ALU.add)
+            return denom
+
+        def spread_factor(h, denom, b):
+            factor = sb.tile([P, 2], F32, name="factor%d" % h)
+            nc.vector.reciprocal(factor[:], denom[:])
+            out = bank(b, "factor_ps%d" % h)
+            for i in range(2):
+                nc.tensor.transpose(out[:, i * P:(i + 1) * P], factor[:, i:i + 1].to_broadcast([P, P]), ident[:])
+            return out
+
+        for c in (0, 1):
+            square(c, "squares%d" % c)
+            copy_rows(nc.vector.tensor_copy, c)
+        root0 = roots(0)
+        denom0 = add_eps(0, root0)
+        raw00 = sb.tile([P, HALF], F32, name="raw00")
+        nc.vector.tensor_copy(raw00[:], lane0_ps[0][:, :HALF])
+        factor_ps0 = spread_factor(0, denom0, 2)
+        lane10_ps = bank(3, "lane10_ps")
+        turn(lane10_ps, 1, 0)
+        lane0_ps.append(lane0_product(1, 4))
+        for t in (1, 2, 3):
             window[t] = sb.tile([P, TABLE], F32, name="window%d" % t, tag="window%d" % t, align_bytes=64)
             nc.gpsimd.memset(window[t][:], 0.0)
 
-        root = sb.tile([P, BLOCKS], F32, name="root", tag="raw_half0")
-        for c in range(BLOCKS):
-            nc.scalar.activation(root[:, c:c + 1], mean_squares[:, STAT + c:STAT + c + 1], ACT.Sqrt,
-                                 bias=acc_cols[:, STAT + c:STAT + c + 1])
-        denom = sb.tile([P, BLOCKS], F32, name="denom", tag="raw_lane0")
-        nc.scalar.activation(denom[:], root[:], ACT.Identity, bias=EPS)
-        factor = sb.tile([P, BLOCKS], F32, name="factor")
-        nc.vector.reciprocal(factor[:], denom[:])
+        square(2, "squares2")
+        copy_rows(nc.vector.tensor_copy, 2)
+        square(3, "squares3")
+        root1 = roots(1)
+        copy_rows(nc.scalar.copy, 3)
 
-        raw_lane0 = sb.tile([P, SLOTS], F32, name="raw_lane0", tag="raw_lane0")
-        scaled_lane3 = sb.tile([P, SLOTS], F32, name="scaled_lane3")
-        nc.vector.tensor_copy(raw_lane0[:], lane0_ps[:])
+        src00 = sb.tile([P, HALF], F32, name="src00")
+        src01 = sb.tile([P, HALF], F32, name="src01")
+        src1_21 = sb.tile([P, 3 * HALF], F32, name="src1_21")
+        src30_20 = sb.tile([P, 2 * HALF], F32, name="src30_20")
+        src31 = sb.tile([P, HALF], F32, name="src31", tag="src31")
+        row = [sb.tile([P, HALF], F32, name="factor_row%d" % h) for h in range(2)]
 
-        factor_row = sb.tile([P, SLOTS], F32, name="factor_row", tag="factor_row")
-        factor_ps = [bank(5 + h, "factor_ps%d" % h) for h in range(2)]
-        for c in range(BLOCKS):
-            h, in_half = divmod(c, 2)
-            nc.tensor.transpose(factor_ps[h][:, in_half * P:(in_half + 1) * P],
-                                factor[:, c:c + 1].to_broadcast([P, P]), ident[:])
-        raw_half0 = sb.tile([P, 2 * HALF], F32, name="raw_half0", tag="raw_half0")
-        nc.scalar.copy(raw_half0[:], half_ps[0][:])
+        nc.vector.tensor_tensor(src00[:], factor_ps0[:, :HALF], raw00[:], ALU.mult)
+        denom1 = add_eps(1, root1)
+        nc.vector.tensor_copy(row[0][:], factor_ps0[:, :HALF])
+        factor_ps1 = spread_factor(1, denom1, 5)
+        late0_ps = bank(7, "late0_ps")
+        turn(late0_ps[:, :HALF], 3, 0)
+        turn(late0_ps[:, HALF:], 2, 0)
+        late1_ps = bank(6, "late1_ps")
+        turn(late1_ps[:, :HALF], 1, 1)
+        turn(late1_ps[:, HALF:], 2, 1)
+        lane31_ps = bank(1, "lane31_ps")
+        turn(lane31_ps, 3, 1)
 
-        scaled = {(1, h): sb.tile([P, HALF], F32, name="scaled1%d" % h)[:] for h in range(2)}
-        nc.vector.tensor_tensor(scaled[1, 0], factor_ps[0][:, :HALF], raw_half0[:, :HALF], ALU.mult)
-        nc.vector.tensor_copy(factor_row[:, :HALF], factor_ps[0][:, :HALF])
-        nc.scalar.copy(factor_row[:, HALF:], factor_ps[1][:, :HALF])
-        nc.vector.tensor_tensor(scaled[1, 1], turned(1, 1), factor_row[:, HALF:], ALU.mult)
-        nc.vector.tensor_tensor(scaled_lane3[:], lane3_ps[:], factor_row[:], ALU.mult)
-        for h in range(2):
-            scaled[3, h] = scaled_lane3[:, h * HALF:(h + 1) * HALF]
-        lane2_late_ps = bank(5, "lane2_late_ps")
-        for c in (2, 3):
-            turn(2, c)
+        def scale_two(out, ps_tile, h):
+            nc.vector.tensor_tensor(out.rearrange("p (a i) -> p a i", a=2), ps_tile[:].rearrange("p (a i) -> p a i", a=2),
+                                    row[h][:].unsqueeze(1).to_broadcast([P, 2, HALF]), ALU.mult)
+
+        nc.vector.tensor_tensor(src1_21[:, :HALF], lane10_ps[:, :HALF], row[0][:], ALU.mult)
+        nc.vector.tensor_copy(row[1][:], factor_ps1[:, :HALF])
+        scale_two(src30_20[:], late0_ps, 0)
+        nc.vector.tensor_tensor(src01[:], lane0_ps[1][:, :HALF], row[1][:], ALU.mult)
+        scale_two(src1_21[:, HALF:], late1_ps, 1)
 
         out_rows = out_0.rearrange("(m t) col -> m t col", t=LANES)
 
         def listed(t, h):
             return window[t][:].indirect(offsets[:, h * HALF // 16:(h + 1) * HALF // 16])
 
-        def scalar_scatter(t, h):
-            nc.scalar.activation(listed(t, h), scaled[t, h], ACT.Copy)
+        def scalar_scatter(t, h, src):
+            nc.scalar.activation(listed(t, h), src, ACT.Copy)
 
         def store_window(t):
             nc.sync.dma_start(out_rows[:, t, :], window[t][:])
 
-        scalar_scatter(1, 0)
-        scalar_scatter(1, 1)
-        store_window(1)
-        nc.vector.tensor_tensor(window[0][:].indirect(offsets[:]), raw_lane0[:], factor_row[:], ALU.mult)
+        scalar_scatter(0, 0, src00[:])
+        scalar_scatter(0, 1, src01[:])
         store_window(0)
+        nc.vector.tensor_copy(window[1][:].indirect(offsets[:]), src1_21[:, :SLOTS])
+        store_window(1)
+        scalar_scatter(2, 1, src1_21[:, SLOTS:])
 
-        na_ps = bank(6, "na_ps")
+        na_ps = bank(0, "na_ps")
         nc.tensor.matmul(na_ps[:, 0:P], mean_squares[:], ident[:], start=True, stop=False, is_transpose=True)
         nc.tensor.matmul(na_ps[:, 0:P], acc_cols[:], ident[:], start=False, stop=True, is_transpose=True)
         na_rows = sb.tile([P, P], F32, name="na_rows")
         nc.scalar.copy(na_rows[:], na_ps[:, 0:P])
         nc.sync.dma_start(out_1.rearrange("o (c i) -> (o c) i", c=BLOCKS), na_rows[STAT:P, :])
 
-        scalar_scatter(3, 0)
-        scalar_scatter(3, 1)
-        store_window(3)
-        scaled[2, 1] = sb.tile([P, HALF], F32, name="scaled21")[:]
-        nc.vector.tensor_tensor(scaled[2, 1], turned(2, 1), factor_row[:, HALF:], ALU.mult)
-        nc.vector.tensor_tensor(listed(2, 0), raw_half0[:, HALF:], factor_row[:, :HALF], ALU.mult)
-        scalar_scatter(2, 1)
+        nc.vector.tensor_tensor(src31[:], lane31_ps[:, :HALF], row[1][:], ALU.mult)
+        nc.vector.tensor_copy(listed(2, 0), src30_20[:, HALF:])
         store_window(2)
+        scalar_scatter(3, 0, src30_20[:, :HALF])
+        scalar_scatter(3, 1, src31[:])
+        store_window(3)
 
-        scalar_pairs = sb.tile([P, 2, TABLE - VECTOR_COLS, 2], BF16, name="scalar_pairs", tag="raw_half0")
-        vector_pairs = sb.tile([P, 2, VECTOR_COLS, 2], BF16, name="vector_pairs", tag="factor_row")
+        parts = {"v": (0, V_END), "g": (V_END, GP_END), "s": (GP_END, TABLE)}
+        pairs = {}
+        for key, (first, end) in parts.items():
+            pairs[key] = sb.tile([P, 2, end - first, 2], BF16, name="pairs_" + key, tag="src31" if key == "s" else "pairs_" + key)
+
+        def lane_out(key, t):
+            return pairs[key][:, t // 2, :, t % 2]
+
+        def lane_in(key, t):
+            return window[t][:, parts[key][0]:parts[key][1]]
+
         for t in (0, 1):
-            nc.vector.tensor_copy(scalar_pairs[:, 0, :, t], window[t][:, VECTOR_COLS:])
-        for t in (0, 1):
-            nc.vector.tensor_copy(vector_pairs[:, 0, :, t], window[t][:, :VECTOR_COLS])
+            for key in ("v", "g"):
+                nc.gpsimd.tensor_scalar(lane_out(key, t), lane_in(key, t), 1.0, 1.0, ALU.mult, ALU.mult)
 
         words_out = out_2[0].rearrange("p col t -> p (col t)").bitcast(I32)
         y_scales = sb.tile([P, TABLE], U8, name="y_scales", align_bytes=64)
+        y_codes = {key: sb.tile([P, end - first], U32, name="y_codes_" + key, align_bytes=64) for key, (first, end) in parts.items()}
         y_woven = {}
-        y_codes = {k: sb.tile([P, CHUNK], U32, name="y_codes%d" % k, align_bytes=64) for k in range(2)}
 
-        def pairs_of(first, end):
-            if first < VECTOR_COLS:
-                return vector_pairs[:, :, first:end, :]
-            return scalar_pairs[:, :, first - VECTOR_COLS:end - VECTOR_COLS, :]
+        def round_lane(engine_copy, key, t):
+            engine_copy(lane_out(key, t), lane_in(key, t))
 
-        def round_lane(engine_copy, t, first, end):
-            engine_copy(pairs_of(first, end)[:, t // 2, :, t % 2], window[t][:, first:end])
+        def weave(engine_copy, key, first, end):
+            y_woven[key, first] = sb.tile([P, (end - first) * LANES], BF16, name="y_woven_%s%d" % (key, first), align_bytes=64)
+            engine_copy(y_woven[key, first][:].bitcast(F32).rearrange("p (col u) -> p col u", u=2),
+                        pairs[key][:, :, first:end, :].bitcast(F32).rearrange("p u col e -> p col (u e)"))
 
-        def weave_pairs(engine_copy, piece, first, end):
-            start, stop = piece
-            if start not in y_woven:
-                y_woven[start] = sb.tile([P, (stop - start) * LANES], BF16, name="y_woven%d" % start,
-                                         align_bytes=64, tag="y_woven%d" % start)
-            engine_copy(y_woven[start][:, (first - start) * LANES:(end - start) * LANES].bitcast(F32).rearrange("p (col u) -> p col u", u=2),
-                        pairs_of(first, end).bitcast(F32).rearrange("p u col e -> p col (u e)"))
+        def quantise_y(key, piece, first, end):
+            base = parts[key][0]
+            nc.vector.quantize_mx(out=y_codes[key][:, first:end].bitcast(E4M3), scales=y_scales[:, base + first:base + end],
+                                  in_=y_woven[key, piece][:, (first - piece) * LANES:(end - piece) * LANES])
 
-        def quantise_y(first, end):
-            k, offset = divmod(first, CHUNK)
-            nc.vector.quantize_mx(out=y_codes[k][:, offset:offset + end - first].bitcast(E4M3),
-                                  scales=y_scales[:, first:end], in_=y_woven[first][:])
+        def store_codes(key):
+            nc.sync.dma_start(words_out[:, parts[key][0]:parts[key][1]], y_codes[key][:].bitcast(I32))
 
-        def store_codes(k):
-            nc.sync.dma_start(words_out[:, k * CHUNK:(k + 1) * CHUNK], y_codes[k][:].bitcast(I32))
-
-        chunk = [(k * CHUNK, (k + 1) * CHUNK) for k in range(TABLE // CHUNK)]
-        for (first, end), pieces in ((chunk[3], (chunk[3],)), ((VECTOR_COLS, chunk[2][1]), LAST_PIECES)):
-            for t in (3, 2):
-                round_lane(nc.scalar.copy, t, first, end)
-            for piece in pieces:
-                weave_pairs(nc.scalar.copy, piece, max(piece[0], first), piece[1])
-
-        round_lane(nc.vector.tensor_copy, 3, *chunk[0])
-        round_lane(nc.vector.tensor_copy, 2, *chunk[0])
-        round_lane(nc.vector.tensor_copy, 3, CHUNK, VECTOR_COLS)
-        weave_pairs(nc.vector.tensor_copy, chunk[0], *chunk[0])
-        round_lane(nc.vector.tensor_copy, 2, CHUNK, VECTOR_COLS)
-        quantise_y(*chunk[0])
-        store_codes(0)
-        weave_pairs(nc.vector.tensor_copy, chunk[1], *chunk[1])
-        weave_pairs(nc.vector.tensor_copy, LAST_PIECES[-1], chunk[2][0], VECTOR_COLS)
-        y_codes[3] = sb.tile([P, CHUNK], U32, name="y_codes3", align_bytes=64, tag="y_woven%d" % chunk[0][0])
-        quantise_y(*chunk[3])
-        store_codes(3)
-        quantise_y(*chunk[1])
-        store_codes(1)
-        y_codes[2] = sb.tile([P, CHUNK], U32, name="y_codes2", align_bytes=64, tag="y_woven%d" % chunk[3][0])
-        for piece in LAST_PIECES:
-            quantise_y(*piece)
-        store_codes(2)
+        round_lane(nc.vector.tensor_copy, "v", 2)
+        round_lane(nc.vector.tensor_copy, "g", 2)
+        round_lane(nc.scalar.copy, "s", 2)
+        round_lane(nc.scalar.copy, "s", 3)
+        round_lane(nc.vector.tensor_copy, "v", 3)
+        round_lane(nc.vector.tensor_copy, "s", 0)
+        round_lane(nc.vector.tensor_copy, "s", 1)
+        weave(nc.vector.tensor_copy, "v", 0, V_END)
+        round_lane(nc.vector.tensor_copy, "g", 3)
+        quantise_y("v", 0, 0, 512)
+        quantise_y("v", 0, 512, 768)
+        store_codes("v")
+        weave(nc.scalar.copy, "s", 0, 512)
+        weave(nc.scalar.copy, "s", 512, 768)
+        quantise_y("s", 0, 0, 512)
+        quantise_y("s", 512, 512, 768)
+        store_codes("s")
+        for first, end in ((0, 256), (256, 384), (384, 512)):
+            weave(nc.scalar.copy, "g", first, end)
+            quantise_y("g", first, first, end)
+        store_codes("g")
 
         scales_out = out_3[0].bitcast(I32)
         for q in range(4):

@@ -47,7 +47,6 @@ def tile_attend_grwada_pl_kernel(tc, xT, G, acc, offs, out_0, out_1, out_2, out_
         acc_table = sb.tile([P, TABLE], F32, name="acc_table")
         nc.vector.memset(acc_table[0:P - 1, :], 0.0)
         window = {0: sb.tile([P, TABLE], F32, name="window0", align_bytes=64)}
-        nc.vector.memset(window[0][:, :TABLE // 2], 0.0)
         x_raw = []
         for t in range(LANES):
             x_lane = sb.tile([P, R], F32, name="x_raw%d" % t)
@@ -71,7 +70,7 @@ def tile_attend_grwada_pl_kernel(tc, xT, G, acc, offs, out_0, out_1, out_2, out_
         make_identity(nc, ident[:])
         mean_squares = sb.tile([P, P], F32, name="mean_squares")
         nc.gpsimd.memset(mean_squares[:], 0.0)
-        nc.gpsimd.memset(window[0][:, TABLE // 2:], 0.0)
+        nc.gpsimd.memset(window[0][:], 0.0)
         eps_cols = sb.tile([P, 2], F32, name="eps_cols")
         nc.scalar.activation(eps_cols[:], mean_squares[:, 0:2], ACT.Identity, bias=EPS)
 
@@ -111,9 +110,14 @@ def tile_attend_grwada_pl_kernel(tc, xT, G, acc, offs, out_0, out_1, out_2, out_
         nc.scalar.copy(acc_cols[:].rearrange("p (m c) -> p m c", c=BLOCKS),
                        acc_ps[:].rearrange("p (c m) -> p m c", c=BLOCKS)[:, P - P // BLOCKS:P, :])
 
+        acc_first = []
+        for h in range(2):
+            acc_first.append(sb.tile([P, 1], F32, name="acc_first%d" % h, tag="acc_first%d" % h))
+            nc.scalar.copy(acc_first[h][:], acc_ps[:, (2 * h + 1) * P - 1:(2 * h + 1) * P])
+
         g_codes = sb.tile([P, SLOTS], U32, name="g_codes", align_bytes=64, tag="window3")
         g_scales = sb.tile([P, SLOTS], U8, name="g_scales", align_bytes=64, tag="window2")
-        dw_ps = [bank(5 + c, "dw_ps%d" % c) for c in range(BLOCKS - 1)]
+        dw_ps = [bank(4 + c, "dw_ps%d" % c) for c in range(BLOCKS)]
 
         def weave_g(c, engine_copy, woven):
             h, in_half = divmod(c, 2)
@@ -141,44 +145,41 @@ def tile_attend_grwada_pl_kernel(tc, xT, G, acc, offs, out_0, out_1, out_2, out_
         quantise_g(1, g_woven1[:])
         product(1, 0, D)
 
-        def lane0_product(h, b):
-            out = bank(b, "lane0_ps%d" % h)
-            cols = slice(h * HALF, (h + 1) * HALF)
-            nc.tensor.matmul_mx(
-                out=out[:, :HALF], lhsT=x_codes[:, 0:P].bitcast(E4M3), lhsT_scale=x_scales[:, 0:P],
-                rhs=g_codes[:, cols].bitcast(E5M2), rhs_scale=g_scales[:, cols], start=True, stop=True)
-            return out
-
-        lane0_ps = [lane0_product(0, 0)]
         g_woven23 = sb.tile([P, 2 * P * LANES], BF16, name="g_woven23", align_bytes=64, tag="window1")
         for c in (2, 3):
             weave_g(c, nc.vector.tensor_copy, g_woven23[:, (c - 2) * P * LANES:(c - 1) * P * LANES])
-        dw_ps.append(bank(1, "dw_ps3"))
         for c in (2, 3):
             quantise_g(c, g_woven23[:, (c - 2) * P * LANES:(c - 1) * P * LANES])
             product(c, 0, D)
+        lane0_ps = bank(0, "lane0_ps")
+        nc.tensor.matmul_mx(
+            out=lane0_ps[:], lhsT=x_codes[:, 0:P].bitcast(E4M3), lhsT_scale=x_scales[:, 0:P],
+            rhs=g_codes[:].bitcast(E5M2), rhs_scale=g_scales[:], start=True, stop=True)
 
         dw_rows = {}
 
-        def square(c, tag):
-            squares = sb.tile([P, D], BF16, name="squares%d" % c, tag=tag)
-            nc.scalar.activation(squares[:], dw_ps[c][:], ACT.Square, scale=root_inv_d[:],
+        def square(c, squares):
+            nc.scalar.activation(squares, dw_ps[c][:], ACT.Square, scale=root_inv_d[:],
                                  accum_out=mean_squares[:, STAT + c:STAT + c + 1])
 
-        def copy_rows(engine_copy, c):
-            dw_rows[c] = sb.tile([P, D - P], F32, name="dw_rows%d" % c)
+        def copy_rows(engine_copy, c, tag):
+            dw_rows[c] = sb.tile([P, D - P], F32, name="dw_rows%d" % c, tag=tag)
             engine_copy(dw_rows[c][:], dw_ps[c][:, P:])
 
-        def turn(out, t, h):
+        def turn(out, t, c):
+            nc.tensor.transpose(out, dw_rows[c][:, (t - 1) * P:t * P], ident[:])
+
+        def turn_two(ps_tile, first, second):
             for in_half in range(2):
-                nc.tensor.transpose(out[:, in_half * P:(in_half + 1) * P],
-                                    dw_rows[2 * h + in_half][:, (t - 1) * P:t * P], ident[:])
+                for a, (t, h) in enumerate((first, second)):
+                    turn(ps_tile[:, a * HALF + in_half * P:a * HALF + (in_half + 1) * P], t, 2 * h + in_half)
 
         def roots(h):
-            root = sb.tile([P, 2], F32, name="root%d" % h)
+            root = sb.tile([P, 2], F32, name="root%d" % h, tag="root%d" % h)
             for i in range(2):
                 col = STAT + 2 * h + i
-                nc.scalar.activation(root[:, i:i + 1], mean_squares[:, col:col + 1], ACT.Sqrt, bias=acc_cols[:, col:col + 1])
+                nc.scalar.activation(root[:, i:i + 1], mean_squares[:, col:col + 1], ACT.Sqrt,
+                                     bias=acc_first[h][:] if i == 0 else acc_cols[:, col:col + 1])
             return root
 
         def add_eps(h, root):
@@ -187,63 +188,51 @@ def tile_attend_grwada_pl_kernel(tc, xT, G, acc, offs, out_0, out_1, out_2, out_
             return denom
 
         def spread_factor(h, denom, b):
-            factor = sb.tile([P, 2], F32, name="factor%d" % h)
+            factor = sb.tile([P, 2], F32, name="factor%d" % h, tag="factor%d" % h)
             nc.vector.reciprocal(factor[:], denom[:])
             out = bank(b, "factor_ps%d" % h)
             for i in range(2):
                 nc.tensor.transpose(out[:, i * P:(i + 1) * P], factor[:, i:i + 1].to_broadcast([P, P]), ident[:])
             return out
 
+        early_squares = sb.tile([P, 2, D], BF16, name="early_squares")
         for c in (0, 1):
-            square(c, "squares%d" % c)
-            copy_rows(nc.vector.tensor_copy, c)
-        root0 = roots(0)
-        denom0 = add_eps(0, root0)
-        raw00 = sb.tile([P, HALF], F32, name="raw00")
-        nc.vector.tensor_copy(raw00[:], lane0_ps[0][:, :HALF])
-        factor_ps0 = spread_factor(0, denom0, 2)
-        lane10_ps = bank(3, "lane10_ps")
-        turn(lane10_ps, 1, 0)
-        lane0_ps.append(lane0_product(1, 4))
+            square(c, early_squares[:, c, :])
+            copy_rows(nc.vector.tensor_copy, c, "dw_rows%d" % c)
+        factor_ps0 = spread_factor(0, add_eps(0, roots(0)), 2)
         for t in (1, 2, 3):
             window[t] = sb.tile([P, TABLE], F32, name="window%d" % t, tag="window%d" % t, align_bytes=64)
             nc.gpsimd.memset(window[t][:], 0.0)
 
-        square(2, "squares2")
-        copy_rows(nc.vector.tensor_copy, 2)
-        square(3, "squares3")
+        late_squares = sb.tile([P, 2, D], BF16, name="late_squares", tag="acc_first0")
+        square(2, late_squares[:, 0, :])
+        copy_rows(nc.vector.tensor_copy, 2, "dw_rows2")
+        square(3, late_squares[:, 1, :])
         root1 = roots(1)
-        copy_rows(nc.scalar.copy, 3)
+        copy_rows(nc.scalar.copy, 3, "acc_first1")
 
-        src00 = sb.tile([P, HALF], F32, name="src00")
-        src01 = sb.tile([P, HALF], F32, name="src01")
         src1_21 = sb.tile([P, 3 * HALF], F32, name="src1_21")
-        src30_20 = sb.tile([P, 2 * HALF], F32, name="src30_20")
-        src31 = sb.tile([P, HALF], F32, name="src31", tag="src31")
-        row = [sb.tile([P, HALF], F32, name="factor_row%d" % h) for h in range(2)]
+        src20_31 = sb.tile([P, SLOTS], F32, name="src20_31")
+        row = sb.tile([P, SLOTS], F32, name="factor_row", tag="factor_row")
 
-        nc.vector.tensor_tensor(src00[:], factor_ps0[:, :HALF], raw00[:], ALU.mult)
+        nc.vector.tensor_copy(row[:, :HALF], factor_ps0[:, :HALF])
         denom1 = add_eps(1, root1)
-        nc.vector.tensor_copy(row[0][:], factor_ps0[:, :HALF])
-        factor_ps1 = spread_factor(1, denom1, 5)
-        late0_ps = bank(7, "late0_ps")
-        turn(late0_ps[:, :HALF], 3, 0)
-        turn(late0_ps[:, HALF:], 2, 0)
-        late1_ps = bank(6, "late1_ps")
-        turn(late1_ps[:, :HALF], 1, 1)
-        turn(late1_ps[:, HALF:], 2, 1)
-        lane31_ps = bank(1, "lane31_ps")
-        turn(lane31_ps, 3, 1)
-
-        def scale_two(out, ps_tile, h):
-            nc.vector.tensor_tensor(out.rearrange("p (a i) -> p a i", a=2), ps_tile[:].rearrange("p (a i) -> p a i", a=2),
-                                    row[h][:].unsqueeze(1).to_broadcast([P, 2, HALF]), ALU.mult)
-
-        nc.vector.tensor_tensor(src1_21[:, :HALF], lane10_ps[:, :HALF], row[0][:], ALU.mult)
-        nc.vector.tensor_copy(row[1][:], factor_ps1[:, :HALF])
-        scale_two(src30_20[:], late0_ps, 0)
-        nc.vector.tensor_tensor(src01[:], lane0_ps[1][:, :HALF], row[1][:], ALU.mult)
-        scale_two(src1_21[:, HALF:], late1_ps, 1)
+        src0 = [sb.tile([P, HALF], F32, name="src0%d" % h, tag="root1" if h == 0 else "src01") for h in range(2)]
+        nc.vector.tensor_tensor(src0[0][:], lane0_ps[:, :HALF], row[:, :HALF], ALU.mult)
+        factor_ps1 = spread_factor(1, denom1, 3)
+        src30 = sb.tile([P, HALF], F32, name="src30", tag="factor1")
+        ps10_30 = bank(2, "ps10_30")
+        turn_two(ps10_30, (1, 0), (3, 0))
+        ps11_21 = bank(1, "ps11_21")
+        turn_two(ps11_21, (1, 1), (2, 1))
+        nc.vector.tensor_tensor(src1_21[:, :HALF], ps10_30[:, :HALF], row[:, :HALF], ALU.mult)
+        nc.vector.tensor_copy(row[:, HALF:], factor_ps1[:, :HALF])
+        nc.vector.tensor_tensor(src30[:], ps10_30[:, HALF:], row[:, :HALF], ALU.mult)
+        nc.vector.tensor_tensor(src0[1][:], lane0_ps[:, HALF:], row[:, HALF:], ALU.mult)
+        nc.vector.tensor_tensor(src1_21[:, HALF:].rearrange("p (a i) -> p a i", a=2), ps11_21[:].rearrange("p (a i) -> p a i", a=2),
+                                row[:, HALF:].unsqueeze(1).to_broadcast([P, 2, HALF]), ALU.mult)
+        ps20_31 = bank(1, "ps20_31")
+        turn_two(ps20_31, (2, 0), (3, 1))
 
         out_rows = out_0.rearrange("(m t) col -> m t col", t=LANES)
 
@@ -256,8 +245,8 @@ def tile_attend_grwada_pl_kernel(tc, xT, G, acc, offs, out_0, out_1, out_2, out_
         def store_window(t):
             nc.sync.dma_start(out_rows[:, t, :], window[t][:])
 
-        scalar_scatter(0, 0, src00[:])
-        scalar_scatter(0, 1, src01[:])
+        scalar_scatter(0, 0, src0[0][:])
+        scalar_scatter(0, 1, src0[1][:])
         store_window(0)
         nc.vector.tensor_copy(window[1][:].indirect(offsets[:]), src1_21[:, :SLOTS])
         store_window(1)
@@ -270,17 +259,17 @@ def tile_attend_grwada_pl_kernel(tc, xT, G, acc, offs, out_0, out_1, out_2, out_
         nc.scalar.copy(na_rows[:], na_ps[:, 0:P])
         nc.sync.dma_start(out_1.rearrange("o (c i) -> (o c) i", c=BLOCKS), na_rows[STAT:P, :])
 
-        nc.vector.tensor_tensor(src31[:], lane31_ps[:, :HALF], row[1][:], ALU.mult)
-        nc.vector.tensor_copy(listed(2, 0), src30_20[:, HALF:])
+        nc.vector.tensor_tensor(src20_31[:], ps20_31[:], row[:], ALU.mult)
+        nc.vector.tensor_copy(listed(2, 0), src20_31[:, :HALF])
         store_window(2)
-        scalar_scatter(3, 0, src30_20[:, :HALF])
-        scalar_scatter(3, 1, src31[:])
+        scalar_scatter(3, 0, src30[:])
+        scalar_scatter(3, 1, src20_31[:, HALF:])
         store_window(3)
 
         parts = {"v": (0, V_END), "g": (V_END, GP_END), "s": (GP_END, TABLE)}
         pairs = {}
         for key, (first, end) in parts.items():
-            pairs[key] = sb.tile([P, 2, end - first, 2], BF16, name="pairs_" + key, tag="src31" if key == "s" else "pairs_" + key)
+            pairs[key] = sb.tile([P, 2, end - first, 2], BF16, name="pairs_" + key, tag="factor_row" if key == "s" else "pairs_" + key)
 
         def lane_out(key, t):
             return pairs[key][:, t // 2, :, t % 2]

@@ -212,7 +212,8 @@ def tile_attend_grwada_pl_kernel(tc, xT, G, acc, offs, out_0, out_1, out_2, out_
         copy_rows(nc.scalar.copy, 3, "acc_first1")
 
         src1_21 = sb.tile([P, 3 * HALF], F32, name="src1_21")
-        src20_31 = sb.tile([P, SLOTS], F32, name="src20_31")
+        src20 = sb.tile([P, HALF], F32, name="src20", tag="src20")
+        src31 = sb.tile([P, HALF], F32, name="src31", tag="src31")
         row = sb.tile([P, SLOTS], F32, name="factor_row", tag="factor_row")
 
         nc.vector.tensor_copy(row[:, :HALF], factor_ps0[:, :HALF])
@@ -259,17 +260,18 @@ def tile_attend_grwada_pl_kernel(tc, xT, G, acc, offs, out_0, out_1, out_2, out_
         nc.scalar.copy(na_rows[:], na_ps[:, 0:P])
         nc.sync.dma_start(out_1.rearrange("o (c i) -> (o c) i", c=BLOCKS), na_rows[STAT:P, :])
 
-        nc.vector.tensor_tensor(src20_31[:], ps20_31[:], row[:], ALU.mult)
-        nc.vector.tensor_copy(listed(2, 0), src20_31[:, :HALF])
+        nc.vector.tensor_tensor(src20[:], ps20_31[:, :HALF], row[:, :HALF], ALU.mult)
+        nc.vector.tensor_tensor(src31[:], ps20_31[:, HALF:], row[:, HALF:], ALU.mult)
+        nc.vector.tensor_copy(listed(2, 0), src20[:])
         store_window(2)
         scalar_scatter(3, 0, src30[:])
-        scalar_scatter(3, 1, src20_31[:, HALF:])
+        scalar_scatter(3, 1, src31[:])
         store_window(3)
 
         parts = {"v": (0, V_END), "g": (V_END, GP_END), "s": (GP_END, TABLE)}
         pairs = {}
         for key, (first, end) in parts.items():
-            pairs[key] = sb.tile([P, 2, end - first, 2], BF16, name="pairs_" + key, tag="factor_row" if key == "s" else "pairs_" + key)
+            pairs[key] = sb.tile([P, 2, end - first, 2], BF16, name="pairs_" + key, tag={"s": "factor_row", "v": "src20", "g": "src31"}[key])
 
         def lane_out(key, t):
             return pairs[key][:, t // 2, :, t % 2]
@@ -277,9 +279,6 @@ def tile_attend_grwada_pl_kernel(tc, xT, G, acc, offs, out_0, out_1, out_2, out_
         def lane_in(key, t):
             return window[t][:, parts[key][0]:parts[key][1]]
 
-        for t in (0, 1):
-            for key in ("v", "g"):
-                nc.gpsimd.tensor_scalar(lane_out(key, t), lane_in(key, t), 1.0, 1.0, ALU.mult, ALU.mult)
 
         words_out = out_2[0].rearrange("p col t -> p (col t)").bitcast(I32)
         y_scales = sb.tile([P, TABLE], U8, name="y_scales", align_bytes=64)
@@ -302,13 +301,14 @@ def tile_attend_grwada_pl_kernel(tc, xT, G, acc, offs, out_0, out_1, out_2, out_
         def store_codes(key):
             nc.sync.dma_start(words_out[:, parts[key][0]:parts[key][1]], y_codes[key][:].bitcast(I32))
 
-        round_lane(nc.vector.tensor_copy, "v", 2)
-        round_lane(nc.vector.tensor_copy, "g", 2)
+        round_lane(nc.vector.tensor_copy, "s", 0)
+        round_lane(nc.vector.tensor_copy, "s", 1)
+        for key in ("v", "g"):
+            for t in (0, 1, 2):
+                round_lane(nc.vector.tensor_copy, key, t)
         round_lane(nc.scalar.copy, "s", 2)
         round_lane(nc.scalar.copy, "s", 3)
         round_lane(nc.vector.tensor_copy, "v", 3)
-        round_lane(nc.vector.tensor_copy, "s", 0)
-        round_lane(nc.vector.tensor_copy, "s", 1)
         weave(nc.vector.tensor_copy, "v", 0, V_END)
         round_lane(nc.vector.tensor_copy, "g", 3)
         quantise_y("v", 0, 0, 512)

@@ -26,8 +26,7 @@ CHUNK = 512
 EPS = 0.001
 BANK = 512
 STAT = P - BLOCKS
-V_END = 768
-GP_END = 1280
+LAST_PIECES = ((0, 256), (256, 384), (384, 512))
 
 FLOPS = 2 * D * R * SLOTS
 BYTES = 4 * (D * R + R * SLOTS + TABLE) + 2 * P * SLOTS // 16 + 4 * (D * TABLE + SLOTS) + D * TABLE + 16 * TABLE
@@ -211,9 +210,8 @@ def tile_attend_grwada_pl_kernel(tc, xT, G, acc, offs, out_0, out_1, out_2, out_
         root1 = roots(1)
         copy_rows(nc.scalar.copy, 3, "acc_first1")
 
-        src1_21 = sb.tile([P, 3 * HALF], F32, name="src1_21")
-        src20 = sb.tile([P, HALF], F32, name="src20", tag="src20")
-        src31 = sb.tile([P, HALF], F32, name="src31", tag="src31")
+        src20_1 = sb.tile([P, 3, HALF], F32, name="src20_1")
+        src21_31 = sb.tile([P, 2, HALF], F32, name="src21_31", tag="src21_31")
         row = sb.tile([P, SLOTS], F32, name="factor_row", tag="factor_row")
 
         nc.vector.tensor_copy(row[:, :HALF], factor_ps0[:, :HALF])
@@ -224,16 +222,18 @@ def tile_attend_grwada_pl_kernel(tc, xT, G, acc, offs, out_0, out_1, out_2, out_
         src30 = sb.tile([P, HALF], F32, name="src30", tag="factor1")
         ps10_30 = bank(2, "ps10_30")
         turn_two(ps10_30, (1, 0), (3, 0))
-        ps11_21 = bank(1, "ps11_21")
-        turn_two(ps11_21, (1, 1), (2, 1))
-        nc.vector.tensor_tensor(src1_21[:, :HALF], ps10_30[:, :HALF], row[:, :HALF], ALU.mult)
+        ps21_31 = bank(1, "ps21_31")
+        turn_two(ps21_31, (2, 1), (3, 1))
+        nc.vector.tensor_tensor(src20_1[:, 1, :], ps10_30[:, :HALF], row[:, :HALF], ALU.mult)
         nc.vector.tensor_copy(row[:, HALF:], factor_ps1[:, :HALF])
+        ps20_11 = bank(3, "ps20_11")
+        turn_two(ps20_11, (2, 0), (1, 1))
         nc.vector.tensor_tensor(src30[:], ps10_30[:, HALF:], row[:, :HALF], ALU.mult)
         nc.vector.tensor_tensor(src0[1][:], lane0_ps[:, HALF:], row[:, HALF:], ALU.mult)
-        nc.vector.tensor_tensor(src1_21[:, HALF:].rearrange("p (a i) -> p a i", a=2), ps11_21[:].rearrange("p (a i) -> p a i", a=2),
+        nc.vector.tensor_tensor(src21_31[:], ps21_31[:].rearrange("p (a i) -> p a i", a=2),
                                 row[:, HALF:].unsqueeze(1).to_broadcast([P, 2, HALF]), ALU.mult)
-        ps20_31 = bank(1, "ps20_31")
-        turn_two(ps20_31, (2, 0), (3, 1))
+        nc.vector.tensor_tensor(src20_1[:, 0:3:2, :], ps20_11[:].rearrange("p (a i) -> p a i", a=2),
+                                row[:].rearrange("p (a i) -> p a i", a=2), ALU.mult)
 
         out_rows = out_0.rearrange("(m t) col -> m t col", t=LANES)
 
@@ -249,80 +249,74 @@ def tile_attend_grwada_pl_kernel(tc, xT, G, acc, offs, out_0, out_1, out_2, out_
         scalar_scatter(0, 0, src0[0][:])
         scalar_scatter(0, 1, src0[1][:])
         store_window(0)
-        nc.vector.tensor_copy(window[1][:].indirect(offsets[:]), src1_21[:, :SLOTS])
+        nc.vector.tensor_copy(window[1][:].indirect(offsets[:]), src20_1[:, 1:3, :].rearrange("p a i -> p (a i)"))
         store_window(1)
-        scalar_scatter(2, 1, src1_21[:, SLOTS:])
+        scalar_scatter(2, 1, src21_31[:, 0, :])
 
-        na_ps = bank(0, "na_ps")
+        na_ps = bank(2, "na_ps")
         nc.tensor.matmul(na_ps[:, 0:P], mean_squares[:], ident[:], start=True, stop=False, is_transpose=True)
         nc.tensor.matmul(na_ps[:, 0:P], acc_cols[:], ident[:], start=False, stop=True, is_transpose=True)
         na_rows = sb.tile([P, P], F32, name="na_rows")
         nc.scalar.copy(na_rows[:], na_ps[:, 0:P])
         nc.sync.dma_start(out_1.rearrange("o (c i) -> (o c) i", c=BLOCKS), na_rows[STAT:P, :])
 
-        nc.vector.tensor_tensor(src20[:], ps20_31[:, :HALF], row[:, :HALF], ALU.mult)
-        nc.vector.tensor_tensor(src31[:], ps20_31[:, HALF:], row[:, HALF:], ALU.mult)
-        nc.vector.tensor_copy(listed(2, 0), src20[:])
+        nc.vector.tensor_copy(listed(2, 0), src20_1[:, 0, :])
         store_window(2)
         scalar_scatter(3, 0, src30[:])
-        scalar_scatter(3, 1, src31[:])
+        scalar_scatter(3, 1, src21_31[:, 1, :])
         store_window(3)
 
-        parts = {"v": (0, V_END), "g": (V_END, GP_END), "s": (GP_END, TABLE)}
-        pairs = {}
-        for key, (first, end) in parts.items():
-            pairs[key] = sb.tile([P, 2, end - first, 2], BF16, name="pairs_" + key, tag={"s": "factor_row", "v": "src20", "g": "src31"}[key])
+        pairs = [sb.tile([P, 2, CHUNK, 2], BF16, name="pairs%d" % k, tag=tag)
+                 for k, tag in enumerate(("pairs0", "pairs1", "factor1", "src21_31"))]
+        chunk = [slice(k * CHUNK, (k + 1) * CHUNK) for k in range(4)]
 
-        def lane_out(key, t):
-            return pairs[key][:, t // 2, :, t % 2]
+        def lane_out(k, t):
+            return pairs[k][:, t // 2, :, t % 2]
 
-        def lane_in(key, t):
-            return window[t][:, parts[key][0]:parts[key][1]]
-
+        for t in (0, 1):
+            for k in (0, 1):
+                nc.gpsimd.tensor_scalar(lane_out(k, t), window[t][:, chunk[k]], 1.0, 1.0, ALU.mult, ALU.mult)
 
         words_out = out_2[0].rearrange("p col t -> p (col t)").bitcast(I32)
         y_scales = sb.tile([P, TABLE], U8, name="y_scales", align_bytes=64)
-        y_codes = {key: sb.tile([P, end - first], U32, name="y_codes_" + key, align_bytes=64) for key, (first, end) in parts.items()}
         y_woven = {}
+        y_codes = {}
 
-        def round_lane(engine_copy, key, t):
-            engine_copy(lane_out(key, t), lane_in(key, t))
+        def round_lane(engine_copy, k, t):
+            engine_copy(lane_out(k, t), window[t][:, chunk[k]])
 
-        def weave(engine_copy, key, first, end):
-            y_woven[key, first] = sb.tile([P, (end - first) * LANES], BF16, name="y_woven_%s%d" % (key, first), align_bytes=64)
-            engine_copy(y_woven[key, first][:].bitcast(F32).rearrange("p (col u) -> p col u", u=2),
-                        pairs[key][:, :, first:end, :].bitcast(F32).rearrange("p u col e -> p col (u e)"))
+        def weave(engine_copy, k, first, end):
+            y_woven[k, first] = sb.tile([P, (end - first) * LANES], BF16, name="y_woven%d_%d" % (k, first), align_bytes=64)
+            engine_copy(y_woven[k, first][:].bitcast(F32).rearrange("p (col u) -> p col u", u=2),
+                        pairs[k][:, :, first:end, :].bitcast(F32).rearrange("p u col e -> p col (u e)"))
 
-        def quantise_y(key, piece, first, end):
-            base = parts[key][0]
-            nc.vector.quantize_mx(out=y_codes[key][:, first:end].bitcast(E4M3), scales=y_scales[:, base + first:base + end],
-                                  in_=y_woven[key, piece][:, (first - piece) * LANES:(end - piece) * LANES])
+        def quantise_y(k, first, end, store_first, store_end):
+            if store_first not in y_codes:
+                y_codes[store_first] = sb.tile([P, store_end - store_first], U32, name="y_codes%d" % store_first, align_bytes=64)
+            lo, hi = k * CHUNK + first, k * CHUNK + end
+            nc.vector.quantize_mx(out=y_codes[store_first][:, lo - store_first:hi - store_first].bitcast(E4M3),
+                                  scales=y_scales[:, lo:hi], in_=y_woven[k, first][:])
+            if hi == store_end:
+                nc.sync.dma_start(words_out[:, store_first:store_end], y_codes[store_first][:].bitcast(I32))
 
-        def store_codes(key):
-            nc.sync.dma_start(words_out[:, parts[key][0]:parts[key][1]], y_codes[key][:].bitcast(I32))
-
-        round_lane(nc.vector.tensor_copy, "s", 0)
-        round_lane(nc.vector.tensor_copy, "s", 1)
-        for key in ("v", "g"):
-            for t in (0, 1, 2):
-                round_lane(nc.vector.tensor_copy, key, t)
-        round_lane(nc.scalar.copy, "s", 2)
-        round_lane(nc.scalar.copy, "s", 3)
-        round_lane(nc.vector.tensor_copy, "v", 3)
-        weave(nc.vector.tensor_copy, "v", 0, V_END)
-        round_lane(nc.vector.tensor_copy, "g", 3)
-        quantise_y("v", 0, 0, 512)
-        quantise_y("v", 0, 512, 768)
-        store_codes("v")
-        weave(nc.scalar.copy, "s", 0, 512)
-        weave(nc.scalar.copy, "s", 512, 768)
-        quantise_y("s", 0, 0, 512)
-        quantise_y("s", 512, 512, 768)
-        store_codes("s")
-        for first, end in ((0, 256), (256, 384), (384, 512)):
-            weave(nc.scalar.copy, "g", first, end)
-            quantise_y("g", first, first, end)
-        store_codes("g")
+        for k, t in ((2, 0), (2, 1), (0, 2), (1, 2), (3, 0), (3, 1)):
+            round_lane(nc.vector.tensor_copy, k, t)
+        for k in (2, 3):
+            for t in (2, 3):
+                round_lane(nc.scalar.copy, k, t)
+            if k == 2:
+                weave(nc.scalar.copy, k, 0, CHUNK)
+        for first, end in LAST_PIECES:
+            weave(nc.scalar.copy, 3, first, end)
+        round_lane(nc.vector.tensor_copy, 0, 3)
+        round_lane(nc.vector.tensor_copy, 1, 3)
+        weave(nc.vector.tensor_copy, 0, 0, CHUNK)
+        weave(nc.vector.tensor_copy, 1, 0, CHUNK)
+        quantise_y(0, 0, CHUNK, 0, 2 * CHUNK)
+        quantise_y(1, 0, CHUNK, 0, 2 * CHUNK)
+        quantise_y(2, 0, CHUNK, 2 * CHUNK, 3 * CHUNK)
+        for first, end in LAST_PIECES:
+            quantise_y(3, first, end, 3 * CHUNK, TABLE)
 
         scales_out = out_3[0].bitcast(I32)
         for q in range(4):

@@ -26,7 +26,8 @@ CHUNK = 512
 EPS = 0.001
 BANK = 512
 STAT = P - BLOCKS
-LAST_PIECES = ((0, 256), (256, 384), (384, 512))
+GP_FIRST = 896
+V_END = 1792
 
 FLOPS = 2 * D * R * SLOTS
 BYTES = 4 * (D * R + R * SLOTS + TABLE) + 2 * P * SLOTS // 16 + 4 * (D * TABLE + SLOTS) + D * TABLE + 16 * TABLE
@@ -70,7 +71,7 @@ def tile_attend_grwada_pl_kernel(tc, xT, G, acc, offs, out_0, out_1, out_2, out_
         mean_squares = sb.tile([P, P], F32, name="mean_squares")
         nc.gpsimd.memset(mean_squares[:], 0.0)
         nc.gpsimd.memset(window[0][:], 0.0)
-        eps_cols = sb.tile([P, 2], F32, name="eps_cols")
+        eps_cols = sb.tile([P, 2], F32, name="eps_cols", tag="eps_cols")
         nc.scalar.activation(eps_cols[:], mean_squares[:, 0:2], ACT.Identity, bias=EPS)
 
         acc_listed = sb.tile([P, SLOTS], F32, name="acc_listed")
@@ -173,6 +174,10 @@ def tile_attend_grwada_pl_kernel(tc, xT, G, acc, offs, out_0, out_1, out_2, out_
                 for a, (t, h) in enumerate((first, second)):
                     turn(ps_tile[:, a * HALF + in_half * P:a * HALF + (in_half + 1) * P], t, 2 * h + in_half)
 
+        def turn_half(ps_tile, t, h):
+            for in_half in range(2):
+                turn(ps_tile[:, in_half * P:(in_half + 1) * P], t, 2 * h + in_half)
+
         def roots(h):
             root = sb.tile([P, 2], F32, name="root%d" % h, tag="root%d" % h)
             for i in range(2):
@@ -210,30 +215,36 @@ def tile_attend_grwada_pl_kernel(tc, xT, G, acc, offs, out_0, out_1, out_2, out_
         root1 = roots(1)
         copy_rows(nc.scalar.copy, 3, "acc_first1")
 
-        src20_1 = sb.tile([P, 3, HALF], F32, name="src20_1")
-        src21_31 = sb.tile([P, 2, HALF], F32, name="src21_31", tag="src21_31")
+        src3 = [sb.tile([P, HALF], F32, name="src3%d" % h, tag="src3%d" % h) for h in range(2)]
         row = sb.tile([P, SLOTS], F32, name="factor_row", tag="factor_row")
+
+        def scale(out, ps_half, h):
+            nc.vector.tensor_tensor(out, ps_half, row[:, h * HALF:(h + 1) * HALF], ALU.mult)
 
         nc.vector.tensor_copy(row[:, :HALF], factor_ps0[:, :HALF])
         denom1 = add_eps(1, root1)
         src0 = [sb.tile([P, HALF], F32, name="src0%d" % h, tag="root1" if h == 0 else "src01") for h in range(2)]
-        nc.vector.tensor_tensor(src0[0][:], lane0_ps[:, :HALF], row[:, :HALF], ALU.mult)
+        scale(src0[0][:], lane0_ps[:, :HALF], 0)
         factor_ps1 = spread_factor(1, denom1, 3)
-        src30 = sb.tile([P, HALF], F32, name="src30", tag="factor1")
-        ps10_30 = bank(2, "ps10_30")
-        turn_two(ps10_30, (1, 0), (3, 0))
-        ps21_31 = bank(1, "ps21_31")
-        turn_two(ps21_31, (2, 1), (3, 1))
-        nc.vector.tensor_tensor(src20_1[:, 1, :], ps10_30[:, :HALF], row[:, :HALF], ALU.mult)
+        src1 = [sb.tile([P, HALF], F32, name="src1%d" % h, tag="eps_cols" if h == 0 else "src11") for h in range(2)]
+        src2 = sb.tile([P, SLOTS], F32, name="src2", tag="factor1")
+        ps10_20 = bank(6, "ps10_20")
+        turn_two(ps10_20, (1, 0), (2, 0))
+        ps11 = bank(1, "ps11")
+        turn_half(ps11, 1, 1)
+        scale(src1[0][:], ps10_20[:, :HALF], 0)
         nc.vector.tensor_copy(row[:, HALF:], factor_ps1[:, :HALF])
-        ps20_11 = bank(3, "ps20_11")
-        turn_two(ps20_11, (2, 0), (1, 1))
-        nc.vector.tensor_tensor(src30[:], ps10_30[:, HALF:], row[:, :HALF], ALU.mult)
-        nc.vector.tensor_tensor(src0[1][:], lane0_ps[:, HALF:], row[:, HALF:], ALU.mult)
-        nc.vector.tensor_tensor(src21_31[:], ps21_31[:].rearrange("p (a i) -> p a i", a=2),
-                                row[:, HALF:].unsqueeze(1).to_broadcast([P, 2, HALF]), ALU.mult)
-        nc.vector.tensor_tensor(src20_1[:, 0:3:2, :], ps20_11[:].rearrange("p (a i) -> p a i", a=2),
-                                row[:].rearrange("p (a i) -> p a i", a=2), ALU.mult)
+        scale(src2[:, :HALF], ps10_20[:, HALF:], 0)
+        scale(src1[1][:], ps11[:, :HALF], 1)
+        scale(src0[1][:], lane0_ps[:, HALF:], 1)
+
+        na_ps = bank(3, "na_ps")
+        nc.tensor.matmul(na_ps[:, 0:P], mean_squares[:], ident[:], start=True, stop=False, is_transpose=True)
+        nc.tensor.matmul(na_ps[:, 0:P], acc_cols[:], ident[:], start=False, stop=True, is_transpose=True)
+        ps3 = bank(1, "ps3")
+        ps21 = bank(0, "ps21")
+        turn_half(ps21, 2, 1)
+        turn_two(ps3, (3, 0), (3, 1))
 
         out_rows = out_0.rearrange("(m t) col -> m t col", t=LANES)
 
@@ -247,76 +258,90 @@ def tile_attend_grwada_pl_kernel(tc, xT, G, acc, offs, out_0, out_1, out_2, out_
             nc.sync.dma_start(out_rows[:, t, :], window[t][:])
 
         scalar_scatter(0, 0, src0[0][:])
-        scalar_scatter(0, 1, src0[1][:])
-        store_window(0)
-        nc.vector.tensor_copy(window[1][:].indirect(offsets[:]), src20_1[:, 1:3, :].rearrange("p a i -> p (a i)"))
-        store_window(1)
-        scalar_scatter(2, 1, src21_31[:, 0, :])
-
-        na_ps = bank(2, "na_ps")
-        nc.tensor.matmul(na_ps[:, 0:P], mean_squares[:], ident[:], start=True, stop=False, is_transpose=True)
-        nc.tensor.matmul(na_ps[:, 0:P], acc_cols[:], ident[:], start=False, stop=True, is_transpose=True)
         na_rows = sb.tile([P, P], F32, name="na_rows")
         nc.scalar.copy(na_rows[:], na_ps[:, 0:P])
         nc.sync.dma_start(out_1.rearrange("o (c i) -> (o c) i", c=BLOCKS), na_rows[STAT:P, :])
-
-        nc.vector.tensor_copy(listed(2, 0), src20_1[:, 0, :])
+        scalar_scatter(0, 1, src0[1][:])
+        store_window(0)
+        nc.vector.tensor_copy(listed(1, 1), src1[1][:])
+        scalar_scatter(1, 0, src1[0][:])
+        store_window(1)
+        scale(src2[:, HALF:], ps21[:, :HALF], 1)
+        for h in range(2):
+            scale(src3[h][:], ps3[:, h * HALF:(h + 1) * HALF], h)
+        nc.vector.tensor_copy(window[2][:].indirect(offsets[:]), src2[:])
         store_window(2)
-        scalar_scatter(3, 0, src30[:])
-        scalar_scatter(3, 1, src21_31[:, 1, :])
+        for h in range(2):
+            scalar_scatter(3, h, src3[h][:])
         store_window(3)
 
-        pairs = [sb.tile([P, 2, CHUNK, 2], BF16, name="pairs%d" % k, tag=tag)
-                 for k, tag in enumerate(("pairs0", "pairs1", "factor1", "src21_31"))]
-        chunk = [slice(k * CHUNK, (k + 1) * CHUNK) for k in range(4)]
+        parts = {"s": (0, CHUNK), "v": (CHUNK, GP_FIRST), "g": (GP_FIRST, V_END), "z": (V_END, TABLE)}
+        pairs = {}
 
-        def lane_out(k, t):
-            return pairs[k][:, t // 2, :, t % 2]
+        def new_pairs(key, tag):
+            pairs[key] = sb.tile([P, 2, parts[key][1] - parts[key][0], 2], BF16, name="pairs_" + key, tag=tag)
+
+        for key, tag in (("g", "factor_row"), ("v", "factor1"), ("s", "src30")):
+            new_pairs(key, tag)
+
+        def lane_out(key, t):
+            return pairs[key][:, t // 2, :, t % 2]
+
+        def lane_in(key, t):
+            return window[t][:, parts[key][0]:parts[key][1]]
 
         for t in (0, 1):
-            for k in (0, 1):
-                nc.gpsimd.tensor_scalar(lane_out(k, t), window[t][:, chunk[k]], 1.0, 1.0, ALU.mult, ALU.mult)
+            nc.gpsimd.tensor_scalar(lane_out("g", t), lane_in("g", t), 1.0, 1.0, ALU.mult, ALU.mult)
 
         words_out = out_2[0].rearrange("p col t -> p (col t)").bitcast(I32)
         y_scales = sb.tile([P, TABLE], U8, name="y_scales", align_bytes=64)
         y_woven = {}
         y_codes = {}
+        done = {}
+        stores = ((0, 2 * CHUNK), (2 * CHUNK, 3 * CHUNK), (3 * CHUNK, TABLE))
 
-        def round_lane(engine_copy, k, t):
-            engine_copy(lane_out(k, t), window[t][:, chunk[k]])
+        def round_lane(engine_copy, key, t):
+            engine_copy(lane_out(key, t), lane_in(key, t))
 
-        def weave(engine_copy, k, first, end):
-            y_woven[k, first] = sb.tile([P, (end - first) * LANES], BF16, name="y_woven%d_%d" % (k, first), align_bytes=64)
-            engine_copy(y_woven[k, first][:].bitcast(F32).rearrange("p (col u) -> p col u", u=2),
-                        pairs[k][:, :, first:end, :].bitcast(F32).rearrange("p u col e -> p col (u e)"))
+        def weave(engine_copy, key, first, end, tile_first, tile_end):
+            base = parts[key][0]
+            if tile_first not in y_woven:
+                y_woven[tile_first] = sb.tile([P, (tile_end - tile_first) * LANES], BF16, name="y_woven%d" % tile_first, align_bytes=64)
+            engine_copy(y_woven[tile_first][:, (first - tile_first) * LANES:(end - tile_first) * LANES].bitcast(F32).rearrange("p (col u) -> p col u", u=2),
+                        pairs[key][:, :, first - base:end - base, :].bitcast(F32).rearrange("p u col e -> p col (u e)"))
 
-        def quantise_y(k, first, end, store_first, store_end):
+        def quantise_y(first, end, tile_first):
+            store_first, store_end = [store for store in stores if store[0] <= first < store[1]][0]
             if store_first not in y_codes:
                 y_codes[store_first] = sb.tile([P, store_end - store_first], U32, name="y_codes%d" % store_first, align_bytes=64)
-            lo, hi = k * CHUNK + first, k * CHUNK + end
-            nc.vector.quantize_mx(out=y_codes[store_first][:, lo - store_first:hi - store_first].bitcast(E4M3),
-                                  scales=y_scales[:, lo:hi], in_=y_woven[k, first][:])
-            if hi == store_end:
+            nc.vector.quantize_mx(out=y_codes[store_first][:, first - store_first:end - store_first].bitcast(E4M3),
+                                  scales=y_scales[:, first:end],
+                                  in_=y_woven[tile_first][:, (first - tile_first) * LANES:(end - tile_first) * LANES])
+            done.setdefault(store_first, []).append(end - first)
+            if sum(done[store_first]) == store_end - store_first:
                 nc.sync.dma_start(words_out[:, store_first:store_end], y_codes[store_first][:].bitcast(I32))
 
-        for k, t in ((2, 0), (2, 1), (0, 2), (1, 2), (3, 0), (3, 1)):
-            round_lane(nc.vector.tensor_copy, k, t)
-        for k in (2, 3):
-            for t in (2, 3):
-                round_lane(nc.scalar.copy, k, t)
-            if k == 2:
-                weave(nc.scalar.copy, k, 0, CHUNK)
-        for first, end in LAST_PIECES:
-            weave(nc.scalar.copy, 3, first, end)
-        round_lane(nc.vector.tensor_copy, 0, 3)
-        round_lane(nc.vector.tensor_copy, 1, 3)
-        weave(nc.vector.tensor_copy, 0, 0, CHUNK)
-        weave(nc.vector.tensor_copy, 1, 0, CHUNK)
-        quantise_y(0, 0, CHUNK, 0, 2 * CHUNK)
-        quantise_y(1, 0, CHUNK, 0, 2 * CHUNK)
-        quantise_y(2, 0, CHUNK, 2 * CHUNK, 3 * CHUNK)
-        for first, end in LAST_PIECES:
-            quantise_y(3, first, end, 3 * CHUNK, TABLE)
+        for key, t in (("s", 0), ("s", 1), ("g", 2), ("v", 0), ("v", 1), ("v", 2)):
+            round_lane(nc.vector.tensor_copy, key, t)
+        for t in (3, 2):
+            round_lane(nc.scalar.copy, "s", t)
+        weave(nc.scalar.copy, "s", *parts["s"], *parts["s"])
+        new_pairs("z", "src31")
+        for t in range(LANES):
+            round_lane(nc.scalar.copy, "z", t)
+        last_pieces = ((V_END, V_END + P), (V_END + P, TABLE))
+        for piece in last_pieces:
+            weave(nc.scalar.copy, "z", *piece, *piece)
+        round_lane(nc.vector.tensor_copy, "v", 3)
+        round_lane(nc.vector.tensor_copy, "g", 3)
+        weave(nc.vector.tensor_copy, "v", CHUNK, GP_FIRST, CHUNK, 2 * CHUNK)
+        weave(nc.vector.tensor_copy, "g", GP_FIRST, 2 * CHUNK, CHUNK, 2 * CHUNK)
+        quantise_y(*parts["s"], 0)
+        quantise_y(CHUNK, 2 * CHUNK, CHUNK)
+        for first, end in ((2 * CHUNK, 3 * CHUNK), (3 * CHUNK, V_END)):
+            weave(nc.vector.tensor_copy, "g", first, end, first, end)
+        for piece in ((2 * CHUNK, 3 * CHUNK), (3 * CHUNK, V_END)) + last_pieces:
+            quantise_y(*piece, piece[0])
 
         scales_out = out_3[0].bitcast(I32)
         for q in range(4):

@@ -294,7 +294,7 @@ def tile_attend_grwada_pl_kernel(tc, xT, G, acc, offs, out_0, out_1, out_2, out_
             nc.gpsimd.tensor_scalar(lane_out("g", t), lane_in("g", t), 1.0, 1.0, ALU.mult, ALU.mult)
 
         words_out = out_2[0].rearrange("p col t -> p (col t)").bitcast(I32)
-        y_scales = sb.tile([P, TABLE], U8, name="y_scales", align_bytes=64)
+        y_scales = sb.tile([P, CHUNK], U8, name="y_scales", align_bytes=64)
         y_woven = {}
         y_codes = {}
         done = {}
@@ -315,7 +315,7 @@ def tile_attend_grwada_pl_kernel(tc, xT, G, acc, offs, out_0, out_1, out_2, out_
             if store_first not in y_codes:
                 y_codes[store_first] = sb.tile([P, store_end - store_first], U32, name="y_codes%d" % store_first, align_bytes=64)
             nc.vector.quantize_mx(out=y_codes[store_first][:, first - store_first:end - store_first].bitcast(E4M3),
-                                  scales=y_scales[:, first:end],
+                                  scales=y_scales[4 * (first // CHUNK):, first % CHUNK:first % CHUNK + end - first],
                                   in_=y_woven[tile_first][:, (first - tile_first) * LANES:(end - tile_first) * LANES])
             done.setdefault(store_first, []).append(end - first)
             if sum(done[store_first]) == store_end - store_first:
@@ -337,13 +337,15 @@ def tile_attend_grwada_pl_kernel(tc, xT, G, acc, offs, out_0, out_1, out_2, out_
         weave(nc.vector.tensor_copy, "v", CHUNK, GP_FIRST, CHUNK, 2 * CHUNK)
         weave(nc.vector.tensor_copy, "g", GP_FIRST, 2 * CHUNK, CHUNK, 2 * CHUNK)
         quantise_y(*parts["s"], 0)
+        weave(nc.vector.tensor_copy, "g", 2 * CHUNK, 3 * CHUNK, 2 * CHUNK, 3 * CHUNK)
         quantise_y(CHUNK, 2 * CHUNK, CHUNK)
-        for first, end in ((2 * CHUNK, 3 * CHUNK), (3 * CHUNK, V_END)):
-            weave(nc.vector.tensor_copy, "g", first, end, first, end)
-        for piece in ((2 * CHUNK, 3 * CHUNK), (3 * CHUNK, V_END)) + last_pieces:
+        weave(nc.vector.tensor_copy, "g", 3 * CHUNK, V_END, 3 * CHUNK, V_END)
+        quantise_y(2 * CHUNK, 2 * CHUNK + HALF, 2 * CHUNK)
+        quantise_y(2 * CHUNK + HALF, 3 * CHUNK, 2 * CHUNK)
+        for piece in ((3 * CHUNK, V_END),) + last_pieces:
             quantise_y(*piece, piece[0])
 
-        scales_out = out_3[0].bitcast(I32)
+        scales_out = out_3[0].bitcast(I32).rearrange("(q r) (k c) -> q k r c", r=4, k=TABLE // CHUNK)
         for q in range(4):
             queue = nc.scalar if q % 2 else nc.sync
-            queue.dma_start(scales_out[4 * q:4 * q + 4, :], y_scales[32 * q:32 * q + 4, :].bitcast(I32))
+            queue.dma_start(scales_out[q], y_scales[32 * q:32 * q + 16, :].bitcast(I32))

@@ -26,8 +26,9 @@ CHUNK = 512
 EPS = 0.001
 BANK = 512
 STAT = P - BLOCKS
-GP_FIRST = 896
-V_END = 1792
+GP_END = 896
+V_END = 1280
+GROUPS = ((1280, 1536), (1536, 1792), (1792, 2048))
 
 FLOPS = 2 * D * R * SLOTS
 BYTES = 4 * (D * R + R * SLOTS + TABLE) + 2 * P * SLOTS // 16 + 4 * (D * TABLE + SLOTS) + D * TABLE + 16 * TABLE
@@ -37,6 +38,7 @@ def tile_attend_grwada_pl_kernel(tc, xT, G, acc, offs, out_0, out_1, out_2, out_
     nc = tc.nc
     with ExitStack() as ctx:
         sb = ctx.enter_context(tc.tile_pool(name="sb", bufs=1))
+        shared = ctx.enter_context(tc.tile_pool(name="shared", bufs=1))
         ps = ctx.enter_context(tc.psum_pool(name="ps", bufs=1))
 
         def bank(b, name):
@@ -215,7 +217,7 @@ def tile_attend_grwada_pl_kernel(tc, xT, G, acc, offs, out_0, out_1, out_2, out_
         root1 = roots(1)
         copy_rows(nc.scalar.copy, 3, "acc_first1")
 
-        src3 = [sb.tile([P, HALF], F32, name="src3%d" % h, tag="src3%d" % h) for h in range(2)]
+        src3 = [sb.tile([P, HALF], F32, name="src30", tag="src30"), shared.tile([P, HALF], F32, name="src31", offset=2 * HALF)]
         row = sb.tile([P, SLOTS], F32, name="factor_row", tag="factor_row")
 
         def scale(out, ps_half, h):
@@ -271,17 +273,13 @@ def tile_attend_grwada_pl_kernel(tc, xT, G, acc, offs, out_0, out_1, out_2, out_
             scale(src3[h][:], ps3[:, h * HALF:(h + 1) * HALF], h)
         nc.vector.tensor_copy(window[2][:].indirect(offsets[:]), src2[:])
         store_window(2)
-        for h in range(2):
-            scalar_scatter(3, h, src3[h][:])
-        store_window(3)
-
-        parts = {"s": (0, CHUNK), "v": (CHUNK, GP_FIRST), "g": (GP_FIRST, V_END), "z": (V_END, TABLE)}
+        parts = {"g": (0, GP_END), "v": (GP_END, V_END)}
         pairs = {}
 
         def new_pairs(key, tag):
             pairs[key] = sb.tile([P, 2, parts[key][1] - parts[key][0], 2], BF16, name="pairs_" + key, tag=tag)
 
-        for key, tag in (("g", "factor_row"), ("v", "factor1"), ("s", "src30")):
+        for key, tag in (("g", "factor_row"), ("v", "factor1")):
             new_pairs(key, tag)
 
         def lane_out(key, t):
@@ -298,7 +296,7 @@ def tile_attend_grwada_pl_kernel(tc, xT, G, acc, offs, out_0, out_1, out_2, out_
         y_woven = {}
         y_codes = {}
         done = {}
-        stores = ((0, 2 * CHUNK), (2 * CHUNK, 3 * CHUNK), (3 * CHUNK, TABLE))
+        stores = ((0, CHUNK + HALF), (CHUNK + HALF, 3 * CHUNK), (3 * CHUNK, TABLE))
 
         def round_lane(engine_copy, key, t):
             engine_copy(lane_out(key, t), lane_in(key, t))
@@ -321,29 +319,65 @@ def tile_attend_grwada_pl_kernel(tc, xT, G, acc, offs, out_0, out_1, out_2, out_
             if sum(done[store_first]) == store_end - store_first:
                 nc.sync.dma_start(words_out[:, store_first:store_end], y_codes[store_first][:].bitcast(I32))
 
-        for key, t in (("s", 0), ("s", 1), ("g", 2), ("v", 0), ("v", 1), ("v", 2)):
+        turned_pairs = {}
+
+        def blocks(j):
+            return (GROUPS[j][1] - GROUPS[j][0]) // P
+
+        def turn_lanes(u, j, b):
+            out = bank(b, "lanes_ps%d%d" % (u, j))
+            for e in range(2):
+                for blk in range(blocks(j)):
+                    first = GROUPS[j][0] + blk * P
+                    nc.tensor.transpose(out[:, (2 * blk + e) * P:(2 * blk + e + 1) * P], window[2 * u + e][:, first:first + P], ident[:])
+            return out
+
+        def round_turned(u, j, lanes_ps, pool, **place):
+            turned_pairs[u, j] = pool.tile([P, blocks(j), P, 2], BF16, name="turned_pairs%d%d" % (u, j), **place)
+            nc.scalar.copy(turned_pairs[u, j][:], lanes_ps[:, :2 * blocks(j) * P].rearrange("p (blk e m) -> p blk m e", e=2, m=P))
+
+        def turn_back(u, j, out):
+            words = turned_pairs[u, j][:].rearrange("p blk m e -> p (blk m e)").bitcast(F32)
+            for blk in range(blocks(j)):
+                first = (u * blocks(j) + blk) * P
+                nc.tensor.transpose(out[:, first:first + P], words[:, blk * P:(blk + 1) * P], ident[:])
+
+        def weave_turned(j, first, end):
+            y_woven[first] = sb.tile([P, (end - first) * LANES], BF16, name="y_woven%d" % first, align_bytes=64)
+            nc.scalar.copy(y_woven[first][:].bitcast(F32).rearrange("p (col u) -> p col u", u=2),
+                           words_ps[j][:].rearrange("p (u col) -> p col u", u=2)[:, first - GROUPS[j][0]:end - GROUPS[j][0], :])
+
+        early_ps = [turn_lanes(0, j, 2 + j) for j in range(len(GROUPS))]
+        scalar_scatter(3, 0, src3[0][:])
+        round_turned(0, 0, early_ps[0], sb, tag="src30")
+        scalar_scatter(3, 1, src3[1][:])
+        store_window(3)
+        words_ps = [bank(b, "words_ps%d" % b) for b in range(len(GROUPS))]
+        turn_back(0, 0, words_ps[0])
+        late_ps = [turn_lanes(1, j, 5 + j) for j in range(len(GROUPS))]
+        for j in (1, 2):
+            round_turned(0, j, early_ps[j], shared, offset=(j - 1) * 4 * HALF)
+        for j in range(len(GROUPS)):
+            round_turned(1, j, late_ps[j], sb)
+            if j > 0:
+                turn_back(0, j, words_ps[j])
+            turn_back(1, j, words_ps[j])
+        scalar_pieces = ((0,) + GROUPS[0], (1,) + GROUPS[1], (2, TABLE - 2 * P, TABLE - P), (2, TABLE - P, TABLE))
+        for piece in scalar_pieces:
+            weave_turned(*piece)
+
+        for key, t in (("v", 0), ("v", 1), ("g", 2), ("v", 2), ("g", 3), ("v", 3)):
             round_lane(nc.vector.tensor_copy, key, t)
-        for t in (3, 2):
-            round_lane(nc.scalar.copy, "s", t)
-        weave(nc.scalar.copy, "s", *parts["s"], *parts["s"])
-        new_pairs("z", "src31")
-        for t in range(LANES):
-            round_lane(nc.scalar.copy, "z", t)
-        last_pieces = ((V_END, V_END + P), (V_END + P, TABLE))
-        for piece in last_pieces:
-            weave(nc.scalar.copy, "z", *piece, *piece)
-        round_lane(nc.vector.tensor_copy, "v", 3)
-        round_lane(nc.vector.tensor_copy, "g", 3)
-        weave(nc.vector.tensor_copy, "v", CHUNK, GP_FIRST, CHUNK, 2 * CHUNK)
-        weave(nc.vector.tensor_copy, "g", GP_FIRST, 2 * CHUNK, CHUNK, 2 * CHUNK)
-        quantise_y(*parts["s"], 0)
-        weave(nc.vector.tensor_copy, "g", 2 * CHUNK, 3 * CHUNK, 2 * CHUNK, 3 * CHUNK)
-        quantise_y(CHUNK, 2 * CHUNK, CHUNK)
-        weave(nc.vector.tensor_copy, "g", 3 * CHUNK, V_END, 3 * CHUNK, V_END)
-        quantise_y(2 * CHUNK, 2 * CHUNK + HALF, 2 * CHUNK)
-        quantise_y(2 * CHUNK + HALF, 3 * CHUNK, 2 * CHUNK)
-        for piece in ((3 * CHUNK, V_END),) + last_pieces:
-            quantise_y(*piece, piece[0])
+        weave(nc.vector.tensor_copy, "g", 0, CHUNK, 0, CHUNK)
+        weave(nc.vector.tensor_copy, "g", CHUNK, GP_END, CHUNK, 2 * CHUNK)
+        quantise_y(0, CHUNK, 0)
+        weave(nc.vector.tensor_copy, "v", GP_END, 2 * CHUNK, CHUNK, 2 * CHUNK)
+        quantise_y(CHUNK, CHUNK + HALF, CHUNK)
+        weave(nc.vector.tensor_copy, "v", 2 * CHUNK, V_END, 2 * CHUNK, V_END)
+        quantise_y(CHUNK + HALF, 2 * CHUNK, CHUNK)
+        quantise_y(2 * CHUNK, V_END, 2 * CHUNK)
+        for j, first, end in scalar_pieces:
+            quantise_y(first, end, first)
 
         scales_out = out_3[0].bitcast(I32).rearrange("(q r) (k c) -> q k r c", r=4, k=TABLE // CHUNK)
         for q in range(4):

@@ -27,8 +27,8 @@ EPS = 0.001
 BANK = 512
 STAT = P - BLOCKS
 GP_END = 896
-V_END = 1280
-GROUPS = ((1280, 1536), (1536, 1792), (1792, 2048))
+V_END = 1408
+GROUPS = ((1408, 1664), (1664, 1920), (1920, 2048))
 
 FLOPS = 2 * D * R * SLOTS
 BYTES = 4 * (D * R + R * SLOTS + TABLE) + 2 * P * SLOTS // 16 + 4 * (D * TABLE + SLOTS) + D * TABLE + 16 * TABLE
@@ -112,10 +112,10 @@ def tile_attend_grwada_pl_kernel(tc, xT, G, acc, offs, out_0, out_1, out_2, out_
         nc.scalar.copy(acc_cols[:].rearrange("p (m c) -> p m c", c=BLOCKS),
                        acc_ps[:].rearrange("p (c m) -> p m c", c=BLOCKS)[:, P - P // BLOCKS:P, :])
 
-        acc_first = []
-        for h in range(2):
-            acc_first.append(sb.tile([P, 1], F32, name="acc_first%d" % h, tag="acc_first%d" % h))
-            nc.scalar.copy(acc_first[h][:], acc_ps[:, (2 * h + 1) * P - 1:(2 * h + 1) * P])
+        acc_first = {}
+        for c in (0, 2, 3):
+            acc_first[c] = sb.tile([P, 1], F32, name="acc_col%d" % c, tag="acc_col%d" % c)
+            nc.scalar.copy(acc_first[c][:], acc_ps[:, (c + 1) * P - 1:(c + 1) * P])
 
         g_codes = sb.tile([P, SLOTS], U32, name="g_codes", align_bytes=64, tag="window3")
         g_scales = sb.tile([P, SLOTS], U8, name="g_scales", align_bytes=64, tag="window2")
@@ -147,16 +147,23 @@ def tile_attend_grwada_pl_kernel(tc, xT, G, acc, offs, out_0, out_1, out_2, out_
         quantise_g(1, g_woven1[:])
         product(1, 0, D)
 
+
+        def lane0_product(h):
+            out = bank(h, "lane0_ps%d" % h)
+            cols = slice(h * HALF, (h + 1) * HALF)
+            nc.tensor.matmul_mx(
+                out=out[:, :HALF], lhsT=x_codes[:, 0:P].bitcast(E4M3), lhsT_scale=x_scales[:, 0:P],
+                rhs=g_codes[:, cols].bitcast(E5M2), rhs_scale=g_scales[:, cols], start=True, stop=True)
+            return out
+
+        lane0_ps = [lane0_product(0)]
         g_woven23 = sb.tile([P, 2 * P * LANES], BF16, name="g_woven23", align_bytes=64, tag="window1")
         for c in (2, 3):
             weave_g(c, nc.vector.tensor_copy, g_woven23[:, (c - 2) * P * LANES:(c - 1) * P * LANES])
         for c in (2, 3):
             quantise_g(c, g_woven23[:, (c - 2) * P * LANES:(c - 1) * P * LANES])
             product(c, 0, D)
-        lane0_ps = bank(0, "lane0_ps")
-        nc.tensor.matmul_mx(
-            out=lane0_ps[:], lhsT=x_codes[:, 0:P].bitcast(E4M3), lhsT_scale=x_scales[:, 0:P],
-            rhs=g_codes[:].bitcast(E5M2), rhs_scale=g_scales[:], start=True, stop=True)
+        lane0_ps.append(lane0_product(1))
 
         dw_rows = {}
 
@@ -185,11 +192,11 @@ def tile_attend_grwada_pl_kernel(tc, xT, G, acc, offs, out_0, out_1, out_2, out_
             for i in range(2):
                 col = STAT + 2 * h + i
                 nc.scalar.activation(root[:, i:i + 1], mean_squares[:, col:col + 1], ACT.Sqrt,
-                                     bias=acc_first[h][:] if i == 0 else acc_cols[:, col:col + 1])
+                                     bias=acc_first[2 * h + i][:] if 2 * h + i in acc_first else acc_cols[:, col:col + 1])
             return root
 
         def add_eps(h, root):
-            denom = sb.tile([P, 2], F32, name="denom%d" % h)
+            denom = sb.tile([P, 2], F32, name="denom%d" % h, tag="denom%d" % h)
             nc.vector.tensor_tensor(denom[:], root[:], eps_cols[:], ALU.add)
             return denom
 
@@ -201,6 +208,8 @@ def tile_attend_grwada_pl_kernel(tc, xT, G, acc, offs, out_0, out_1, out_2, out_
                 nc.tensor.transpose(out[:, i * P:(i + 1) * P], factor[:, i:i + 1].to_broadcast([P, P]), ident[:])
             return out
 
+        raw00 = sb.tile([P, HALF], F32, name="raw00", tag="raw00")
+        nc.vector.tensor_copy(raw00[:], lane0_ps[0][:, :HALF])
         early_squares = sb.tile([P, 2, D], BF16, name="early_squares")
         for c in (0, 1):
             square(c, early_squares[:, c, :])
@@ -210,43 +219,17 @@ def tile_attend_grwada_pl_kernel(tc, xT, G, acc, offs, out_0, out_1, out_2, out_
             window[t] = sb.tile([P, TABLE], F32, name="window%d" % t, tag="window%d" % t, align_bytes=64)
             nc.gpsimd.memset(window[t][:], 0.0)
 
-        late_squares = sb.tile([P, 2, D], BF16, name="late_squares", tag="acc_first0")
+        late_squares = sb.tile([P, 2, D], BF16, name="late_squares", tag="acc_col0")
         square(2, late_squares[:, 0, :])
         copy_rows(nc.vector.tensor_copy, 2, "dw_rows2")
         square(3, late_squares[:, 1, :])
         root1 = roots(1)
-        copy_rows(nc.scalar.copy, 3, "acc_first1")
+        copy_rows(nc.scalar.copy, 3, "acc_col3")
 
-        src3 = [sb.tile([P, HALF], F32, name="src30", tag="src30"), shared.tile([P, HALF], F32, name="src31", offset=2 * HALF)]
         row = sb.tile([P, SLOTS], F32, name="factor_row", tag="factor_row")
 
         def scale(out, ps_half, h):
             nc.vector.tensor_tensor(out, ps_half, row[:, h * HALF:(h + 1) * HALF], ALU.mult)
-
-        nc.vector.tensor_copy(row[:, :HALF], factor_ps0[:, :HALF])
-        denom1 = add_eps(1, root1)
-        src0 = [sb.tile([P, HALF], F32, name="src0%d" % h, tag="root1" if h == 0 else "src01") for h in range(2)]
-        scale(src0[0][:], lane0_ps[:, :HALF], 0)
-        factor_ps1 = spread_factor(1, denom1, 3)
-        src1 = [sb.tile([P, HALF], F32, name="src1%d" % h, tag="eps_cols" if h == 0 else "src11") for h in range(2)]
-        src2 = sb.tile([P, SLOTS], F32, name="src2", tag="factor1")
-        ps10_20 = bank(6, "ps10_20")
-        turn_two(ps10_20, (1, 0), (2, 0))
-        ps11 = bank(1, "ps11")
-        turn_half(ps11, 1, 1)
-        scale(src1[0][:], ps10_20[:, :HALF], 0)
-        nc.vector.tensor_copy(row[:, HALF:], factor_ps1[:, :HALF])
-        scale(src2[:, :HALF], ps10_20[:, HALF:], 0)
-        scale(src1[1][:], ps11[:, :HALF], 1)
-        scale(src0[1][:], lane0_ps[:, HALF:], 1)
-
-        na_ps = bank(3, "na_ps")
-        nc.tensor.matmul(na_ps[:, 0:P], mean_squares[:], ident[:], start=True, stop=False, is_transpose=True)
-        nc.tensor.matmul(na_ps[:, 0:P], acc_cols[:], ident[:], start=False, stop=True, is_transpose=True)
-        ps3 = bank(1, "ps3")
-        ps21 = bank(0, "ps21")
-        turn_half(ps21, 2, 1)
-        turn_two(ps3, (3, 0), (3, 1))
 
         out_rows = out_0.rearrange("(m t) col -> m t col", t=LANES)
 
@@ -259,27 +242,53 @@ def tile_attend_grwada_pl_kernel(tc, xT, G, acc, offs, out_0, out_1, out_2, out_
         def store_window(t):
             nc.sync.dma_start(out_rows[:, t, :], window[t][:])
 
+        nc.vector.tensor_copy(row[:, :HALF], factor_ps0[:, :HALF])
+        src0 = [sb.tile([P, HALF], F32, name="src0%d" % h, tag="acc_col2" if h == 0 else "src01") for h in range(2)]
+        nc.vector.tensor_tensor(src0[0][:], factor_ps0[:, :HALF], raw00[:], ALU.mult)
         scalar_scatter(0, 0, src0[0][:])
+        denom1 = add_eps(1, root1)
+        src2 = sb.tile([P, SLOTS], F32, name="src2", tag="eps_cols")
+        ps20_30 = bank(6, "ps20_30")
+        turn_two(ps20_30, (2, 0), (3, 0))
+        ps10 = bank(2, "ps10")
+        turn_half(ps10, 1, 0)
+        scale(src2[:, :HALF], ps20_30[:, :HALF], 0)
+        factor_ps1 = spread_factor(1, denom1, 3)
+        src3 = [sb.tile([P, HALF], F32, name="src30", tag="denom1"), shared.tile([P, HALF], F32, name="src31", offset=2 * HALF)]
+        scale(src3[0][:], ps20_30[:, HALF:], 0)
+        nc.vector.tensor_copy(row[:, HALF:], factor_ps1[:, :HALF])
+        src1 = [sb.tile([P, HALF], F32, name="src1%d" % h, tag="factor1" if h == 0 else "src11") for h in range(2)]
+        na_ps = bank(3, "na_ps")
+        nc.tensor.matmul(na_ps[:, 0:P], mean_squares[:], ident[:], start=True, stop=False, is_transpose=True)
+        nc.tensor.matmul(na_ps[:, 0:P], acc_cols[:], ident[:], start=False, stop=True, is_transpose=True)
         na_rows = sb.tile([P, P], F32, name="na_rows")
         nc.scalar.copy(na_rows[:], na_ps[:, 0:P])
         nc.sync.dma_start(out_1.rearrange("o (c i) -> (o c) i", c=BLOCKS), na_rows[STAT:P, :])
+        scale(src1[0][:], ps10[:, :HALF], 0)
+        scale(src0[1][:], lane0_ps[1][:, :HALF], 1)
         scalar_scatter(0, 1, src0[1][:])
         store_window(0)
-        nc.vector.tensor_copy(listed(1, 1), src1[1][:])
-        scalar_scatter(1, 0, src1[0][:])
+        nc.vector.tensor_copy(listed(1, 0), src1[0][:])
+
+        ps11_21 = bank(6, "ps11_21")
+        turn_two(ps11_21, (1, 1), (2, 1))
+        ps31 = bank(1, "ps31")
+        turn_half(ps31, 3, 1)
+        scale(src1[1][:], ps11_21[:, :HALF], 1)
+        scalar_scatter(1, 1, src1[1][:])
         store_window(1)
-        scale(src2[:, HALF:], ps21[:, :HALF], 1)
-        for h in range(2):
-            scale(src3[h][:], ps3[:, h * HALF:(h + 1) * HALF], h)
+        scale(src2[:, HALF:], ps11_21[:, HALF:], 1)
+        scale(src3[1][:], ps31[:, :HALF], 1)
         nc.vector.tensor_copy(window[2][:].indirect(offsets[:]), src2[:])
         store_window(2)
+
         parts = {"g": (0, GP_END), "v": (GP_END, V_END)}
         pairs = {}
 
         def new_pairs(key, tag):
             pairs[key] = sb.tile([P, 2, parts[key][1] - parts[key][0], 2], BF16, name="pairs_" + key, tag=tag)
 
-        for key, tag in (("g", "factor_row"), ("v", "factor1")):
+        for key, tag in (("g", "factor_row"), ("v", "eps_cols")):
             new_pairs(key, tag)
 
         def lane_out(key, t):
@@ -345,11 +354,11 @@ def tile_attend_grwada_pl_kernel(tc, xT, G, acc, offs, out_0, out_1, out_2, out_
         def weave_turned(j, first, end):
             y_woven[first] = sb.tile([P, (end - first) * LANES], BF16, name="y_woven%d" % first, align_bytes=64)
             nc.scalar.copy(y_woven[first][:].bitcast(F32).rearrange("p (col u) -> p col u", u=2),
-                           words_ps[j][:].rearrange("p (u col) -> p col u", u=2)[:, first - GROUPS[j][0]:end - GROUPS[j][0], :])
+                           words_ps[j][:, :2 * (end - first)].rearrange("p (u col) -> p col u", u=2))
 
         early_ps = [turn_lanes(0, j, 2 + j) for j in range(len(GROUPS))]
         scalar_scatter(3, 0, src3[0][:])
-        round_turned(0, 0, early_ps[0], sb, tag="src30")
+        round_turned(0, 0, early_ps[0], sb, tag="denom1")
         scalar_scatter(3, 1, src3[1][:])
         store_window(3)
         words_ps = [bank(b, "words_ps%d" % b) for b in range(len(GROUPS))]
@@ -362,21 +371,22 @@ def tile_attend_grwada_pl_kernel(tc, xT, G, acc, offs, out_0, out_1, out_2, out_
             if j > 0:
                 turn_back(0, j, words_ps[j])
             turn_back(1, j, words_ps[j])
-        scalar_pieces = ((0,) + GROUPS[0], (1,) + GROUPS[1], (2, TABLE - 2 * P, TABLE - P), (2, TABLE - P, TABLE))
-        for piece in scalar_pieces:
-            weave_turned(*piece)
-
         for key, t in (("v", 0), ("v", 1), ("g", 2), ("v", 2), ("g", 3), ("v", 3)):
             round_lane(nc.vector.tensor_copy, key, t)
+        weave(nc.scalar.copy, "v", 2 * CHUNK, V_END, 2 * CHUNK, V_END)
+        for j, group in enumerate(GROUPS):
+            weave_turned(j, *group)
         weave(nc.vector.tensor_copy, "g", 0, CHUNK, 0, CHUNK)
         weave(nc.vector.tensor_copy, "g", CHUNK, GP_END, CHUNK, 2 * CHUNK)
         quantise_y(0, CHUNK, 0)
         weave(nc.vector.tensor_copy, "v", GP_END, 2 * CHUNK, CHUNK, 2 * CHUNK)
         quantise_y(CHUNK, CHUNK + HALF, CHUNK)
-        weave(nc.vector.tensor_copy, "v", 2 * CHUNK, V_END, 2 * CHUNK, V_END)
         quantise_y(CHUNK + HALF, 2 * CHUNK, CHUNK)
-        quantise_y(2 * CHUNK, V_END, 2 * CHUNK)
-        for j, first, end in scalar_pieces:
+        quantise_y(2 * CHUNK, 2 * CHUNK + HALF, 2 * CHUNK)
+        quantise_y(2 * CHUNK + HALF, V_END, 2 * CHUNK)
+        quantise_y(V_END, 3 * CHUNK, V_END)
+        quantise_y(3 * CHUNK, GROUPS[0][1], V_END)
+        for first, end in GROUPS[1:]:
             quantise_y(first, end, first)
 
         scales_out = out_3[0].bitcast(I32).rearrange("(q r) (k c) -> q k r c", r=4, k=TABLE // CHUNK)

@@ -27,8 +27,8 @@ EPS = 0.001
 BANK = 512
 STAT = P - BLOCKS
 GP_END = 896
-V_END = 1408
-GROUPS = ((1408, 1664), (1664, 1920), (1920, 2048))
+V_END = 1280
+GROUPS = ((1280, 1536), (1536, 1792), (1792, 2048))
 
 FLOPS = 2 * D * R * SLOTS
 BYTES = 4 * (D * R + R * SLOTS + TABLE) + 2 * P * SLOTS // 16 + 4 * (D * TABLE + SLOTS) + D * TABLE + 16 * TABLE
@@ -224,9 +224,15 @@ def tile_attend_grwada_pl_kernel(tc, xT, G, acc, offs, out_0, out_1, out_2, out_
         copy_rows(nc.vector.tensor_copy, 2, "dw_rows2")
         square(3, late_squares[:, 1, :])
         root1 = roots(1)
+        na_ps = bank(0, "na_ps")
+        nc.tensor.matmul(na_ps[:, 0:P], mean_squares[:], ident[:], start=True, stop=False, is_transpose=True)
+        nc.tensor.matmul(na_ps[:, 0:P], acc_cols[:], ident[:], start=False, stop=True, is_transpose=True)
+        na_rows = sb.tile([P, P], F32, name="na_rows")
+        nc.scalar.copy(na_rows[:], na_ps[:, 0:P])
+        nc.sync.dma_start(out_1.rearrange("o (c i) -> (o c) i", c=BLOCKS), na_rows[STAT:P, :])
         copy_rows(nc.scalar.copy, 3, "acc_col3")
 
-        row = sb.tile([P, SLOTS], F32, name="factor_row", tag="factor_row")
+        row = shared.tile([P, SLOTS], F32, name="factor_row", offset=8 * GP_END - 2 * SLOTS)
 
         def scale(out, ps_half, h):
             nc.vector.tensor_tensor(out, ps_half, row[:, h * HALF:(h + 1) * HALF], ALU.mult)
@@ -254,16 +260,10 @@ def tile_attend_grwada_pl_kernel(tc, xT, G, acc, offs, out_0, out_1, out_2, out_
         turn_half(ps10, 1, 0)
         scale(src2[:, :HALF], ps20_30[:, :HALF], 0)
         factor_ps1 = spread_factor(1, denom1, 3)
-        src3 = [sb.tile([P, HALF], F32, name="src30", tag="denom1"), shared.tile([P, HALF], F32, name="src31", offset=2 * HALF)]
+        src3 = [sb.tile([P, HALF], F32, name="src30", tag="denom1"), sb.tile([P, HALF], F32, name="src31", tag="src31")]
         scale(src3[0][:], ps20_30[:, HALF:], 0)
         nc.vector.tensor_copy(row[:, HALF:], factor_ps1[:, :HALF])
         src1 = [sb.tile([P, HALF], F32, name="src1%d" % h, tag="factor1" if h == 0 else "src11") for h in range(2)]
-        na_ps = bank(3, "na_ps")
-        nc.tensor.matmul(na_ps[:, 0:P], mean_squares[:], ident[:], start=True, stop=False, is_transpose=True)
-        nc.tensor.matmul(na_ps[:, 0:P], acc_cols[:], ident[:], start=False, stop=True, is_transpose=True)
-        na_rows = sb.tile([P, P], F32, name="na_rows")
-        nc.scalar.copy(na_rows[:], na_ps[:, 0:P])
-        nc.sync.dma_start(out_1.rearrange("o (c i) -> (o c) i", c=BLOCKS), na_rows[STAT:P, :])
         scale(src1[0][:], ps10[:, :HALF], 0)
         scale(src0[1][:], lane0_ps[1][:, :HALF], 1)
         scalar_scatter(0, 1, src0[1][:])
@@ -288,8 +288,8 @@ def tile_attend_grwada_pl_kernel(tc, xT, G, acc, offs, out_0, out_1, out_2, out_
         def new_pairs(key, tag):
             pairs[key] = sb.tile([P, 2, parts[key][1] - parts[key][0], 2], BF16, name="pairs_" + key, tag=tag)
 
-        for key, tag in (("g", "factor_row"), ("v", "eps_cols")):
-            new_pairs(key, tag)
+        pairs["g"] = shared.tile([P, 2, GP_END, 2], BF16, name="pairs_g", offset=0)
+        new_pairs("v", "eps_cols")
 
         def lane_out(key, t):
             return pairs[key][:, t // 2, :, t % 2]
@@ -341,9 +341,9 @@ def tile_attend_grwada_pl_kernel(tc, xT, G, acc, offs, out_0, out_1, out_2, out_
                     nc.tensor.transpose(out[:, (2 * blk + e) * P:(2 * blk + e + 1) * P], window[2 * u + e][:, first:first + P], ident[:])
             return out
 
-        def round_turned(u, j, lanes_ps, pool, **place):
+        def round_turned(u, j, lanes_ps, engine_copy, pool, **place):
             turned_pairs[u, j] = pool.tile([P, blocks(j), P, 2], BF16, name="turned_pairs%d%d" % (u, j), **place)
-            nc.scalar.copy(turned_pairs[u, j][:], lanes_ps[:, :2 * blocks(j) * P].rearrange("p (blk e m) -> p blk m e", e=2, m=P))
+            engine_copy(turned_pairs[u, j][:], lanes_ps[:, :2 * blocks(j) * P].rearrange("p (blk e m) -> p blk m e", e=2, m=P))
 
         def turn_back(u, j, out):
             words = turned_pairs[u, j][:].rearrange("p blk m e -> p (blk m e)").bitcast(F32)
@@ -354,39 +354,37 @@ def tile_attend_grwada_pl_kernel(tc, xT, G, acc, offs, out_0, out_1, out_2, out_
         def weave_turned(j, first, end):
             y_woven[first] = sb.tile([P, (end - first) * LANES], BF16, name="y_woven%d" % first, align_bytes=64)
             nc.scalar.copy(y_woven[first][:].bitcast(F32).rearrange("p (col u) -> p col u", u=2),
-                           words_ps[j][:, :2 * (end - first)].rearrange("p (u col) -> p col u", u=2))
+                           words_ps[j][:].rearrange("p (u col) -> p col u", u=2)[:, first - GROUPS[j][0]:end - GROUPS[j][0], :])
 
         early_ps = [turn_lanes(0, j, 2 + j) for j in range(len(GROUPS))]
         scalar_scatter(3, 0, src3[0][:])
-        round_turned(0, 0, early_ps[0], sb, tag="denom1")
+        round_turned(0, 0, early_ps[0], nc.scalar.copy, sb, tag="denom1")
         scalar_scatter(3, 1, src3[1][:])
         store_window(3)
         words_ps = [bank(b, "words_ps%d" % b) for b in range(len(GROUPS))]
         turn_back(0, 0, words_ps[0])
         late_ps = [turn_lanes(1, j, 5 + j) for j in range(len(GROUPS))]
-        for j in (1, 2):
-            round_turned(0, j, early_ps[j], shared, offset=(j - 1) * 4 * HALF)
+        round_turned(0, 1, early_ps[1], nc.vector.tensor_copy, shared, offset=8 * GP_END)
+        round_turned(0, 2, early_ps[2], nc.scalar.copy, sb, tag="src31")
         for j in range(len(GROUPS)):
-            round_turned(1, j, late_ps[j], sb)
+            round_turned(1, j, late_ps[j], nc.scalar.copy, sb)
             if j > 0:
                 turn_back(0, j, words_ps[j])
             turn_back(1, j, words_ps[j])
         for key, t in (("v", 0), ("v", 1), ("g", 2), ("v", 2), ("g", 3), ("v", 3)):
             round_lane(nc.vector.tensor_copy, key, t)
         weave(nc.scalar.copy, "v", 2 * CHUNK, V_END, 2 * CHUNK, V_END)
-        for j, group in enumerate(GROUPS):
-            weave_turned(j, *group)
+        scalar_pieces = ((0,) + GROUPS[0], (1,) + GROUPS[1], (2, TABLE - 2 * P, TABLE - P), (2, TABLE - P, TABLE))
+        for piece in scalar_pieces:
+            weave_turned(*piece)
         weave(nc.vector.tensor_copy, "g", 0, CHUNK, 0, CHUNK)
         weave(nc.vector.tensor_copy, "g", CHUNK, GP_END, CHUNK, 2 * CHUNK)
         quantise_y(0, CHUNK, 0)
         weave(nc.vector.tensor_copy, "v", GP_END, 2 * CHUNK, CHUNK, 2 * CHUNK)
         quantise_y(CHUNK, CHUNK + HALF, CHUNK)
         quantise_y(CHUNK + HALF, 2 * CHUNK, CHUNK)
-        quantise_y(2 * CHUNK, 2 * CHUNK + HALF, 2 * CHUNK)
-        quantise_y(2 * CHUNK + HALF, V_END, 2 * CHUNK)
-        quantise_y(V_END, 3 * CHUNK, V_END)
-        quantise_y(3 * CHUNK, GROUPS[0][1], V_END)
-        for first, end in GROUPS[1:]:
+        quantise_y(2 * CHUNK, V_END, 2 * CHUNK)
+        for j, first, end in scalar_pieces:
             quantise_y(first, end, first)
 
         scales_out = out_3[0].bitcast(I32).rearrange("(q r) (k c) -> q k r c", r=4, k=TABLE // CHUNK)

@@ -58,11 +58,12 @@ def tile_attend_grwada_pl_kernel(tc, xT, G, acc, offs, out_0, out_1, out_2, out_
                 nc.sync.dma_start(acc_table[P - 1:P, :], acc[0:1, :])
                 nc.sync.dma_start(offsets[:], offs)
         g_rows = G.rearrange("(p j) i -> p j i", j=LANES)
-        g_raw = []
-        for h in range(2):
-            g_half = sb.tile([P, LANES, HALF], F32, name="g_raw%d" % h)
-            nc.sync.dma_start(g_half[:], g_rows[:, :, h * HALF:(h + 1) * HALF])
-            g_raw.append(g_half)
+        g_raw = {}
+        for first, end in ((0, 2), (2, 3), (3, 4)):
+            g_part = sb.tile([P, LANES, (end - first) * P], F32, name="g_raw%d" % first, tag="g_raw%d" % first, align_bytes=64)
+            nc.sync.dma_start(g_part[:], g_rows[:, :, first * P:end * P])
+            for c in range(first, end):
+                g_raw[c] = g_part[:, :, (c - first) * P:(c - first + 1) * P]
 
         inv_d = sb.tile([P, 1], F32, name="inv_d")
         nc.gpsimd.memset(inv_d[:], 1.0 / D)
@@ -122,9 +123,8 @@ def tile_attend_grwada_pl_kernel(tc, xT, G, acc, offs, out_0, out_1, out_2, out_
         dw_ps = [bank(4 + c, "dw_ps%d" % c) for c in range(BLOCKS)]
 
         def weave_g(c, engine_copy, woven):
-            h, in_half = divmod(c, 2)
             engine_copy(woven.rearrange("p (g i j) -> p g j i", i=4, j=LANES),
-                        g_raw[h][:, :, in_half * P:(in_half + 1) * P].rearrange("p j (g i) -> p g j i", i=4))
+                        g_raw[c].rearrange("p j (g i) -> p g j i", i=4))
 
         def quantise_g(c, woven):
             cols = slice(c * P, (c + 1) * P)
@@ -157,11 +157,10 @@ def tile_attend_grwada_pl_kernel(tc, xT, G, acc, offs, out_0, out_1, out_2, out_
             return out
 
         lane0_ps = [lane0_product(0)]
-        g_woven23 = sb.tile([P, 2 * P * LANES], BF16, name="g_woven23", align_bytes=64, tag="window1")
-        for c in (2, 3):
-            weave_g(c, nc.vector.tensor_copy, g_woven23[:, (c - 2) * P * LANES:(c - 1) * P * LANES])
-        for c in (2, 3):
-            quantise_g(c, g_woven23[:, (c - 2) * P * LANES:(c - 1) * P * LANES])
+        for c, tag in ((2, "g_raw0"), (3, "window1")):
+            g_woven = sb.tile([P, P * LANES], BF16, name="g_woven%d" % c, align_bytes=64, tag=tag)
+            weave_g(c, nc.vector.tensor_copy, g_woven[:])
+            quantise_g(c, g_woven[:])
             product(c, 0, D)
         lane0_ps.append(lane0_product(1))
 

from contextlib import ExitStack

import concourse.mybir as mybir
from concourse.masks import make_identity

F32 = mybir.dt.float32
BF16 = mybir.dt.bfloat16
I32 = mybir.dt.int32
U32 = mybir.dt.uint32
U16 = mybir.dt.uint16
U8 = mybir.dt.uint8
E4M3 = mybir.dt.float8_e4m3fn_x4
E5M2 = mybir.dt.float8_e5m2_x4
ACT = mybir.ActivationFunctionType
ALU = mybir.AluOpType

P = 128
LANES = 4
D = 512
R = 512
SLOTS = 512
BLOCKS = SLOTS // P
HALF = SLOTS // 2
TABLE = 2048
CHUNK = 512
EPS = 0.001
BANK = 512
STAT = P - BLOCKS
GP_END = 896
V_END = 1280
GROUPS = ((1280, 1536), (1536, 1792), (1792, 2048))

FLOPS = 2 * D * R * SLOTS
BYTES = 4 * (D * R + R * SLOTS + TABLE) + 2 * P * SLOTS // 16 + 4 * (D * TABLE + SLOTS) + D * TABLE + 16 * TABLE


def tile_attend_grwada_pl_kernel(tc, xT, G, acc, offs, out_0, out_1, out_2, out_3):
    nc = tc.nc
    with ExitStack() as ctx:
        sb = ctx.enter_context(tc.tile_pool(name="sb", bufs=1))
        shared = ctx.enter_context(tc.tile_pool(name="shared", bufs=1))
        ps = ctx.enter_context(tc.psum_pool(name="ps", bufs=1))

        def bank(b, name):
            return ps.tile([P, BANK], F32, name=name, tag="bank%d" % b)

        x_rows = xT.rearrange("(m t) r -> m t r", t=LANES)
        offsets = sb.tile([P, SLOTS // 16], U16, name="offsets")
        acc_table = sb.tile([P, TABLE], F32, name="acc_table")
        nc.vector.memset(acc_table[0:P - 1, :], 0.0)
        window = {0: sb.tile([P, TABLE], F32, name="window0", align_bytes=64)}
        x_raw = []
        for t in range(LANES):
            x_lane = sb.tile([P, R], F32, name="x_raw%d" % t)
            nc.sync.dma_start(x_lane[:], x_rows[:, t, :])
            x_raw.append(x_lane)
            if t == 0:
                nc.sync.dma_start(acc_table[P - 1:P, :], acc[0:1, :])
                nc.sync.dma_start(offsets[:], offs)
        g_rows = G.rearrange("(p j) i -> p j i", j=LANES)
        g_raw = {}
        for first, end in ((0, 2), (2, 3), (3, 4)):
            g_part = sb.tile([P, LANES, (end - first) * P], F32, name="g_raw%d" % first, tag="g_raw%d" % first, align_bytes=64)
            nc.sync.dma_start(g_part[:], g_rows[:, :, first * P:end * P])
            for c in range(first, end):
                g_raw[c] = g_part[:, :, (c - first) * P:(c - first + 1) * P]

        inv_d = sb.tile([P, 1], F32, name="inv_d")
        nc.gpsimd.memset(inv_d[:], 1.0 / D)
        root_inv_d = sb.tile([P, 1], F32, name="root_inv_d")
        nc.scalar.activation(root_inv_d[:], inv_d[:], ACT.Sqrt)
        ident = sb.tile([P, P], F32, name="ident")
        make_identity(nc, ident[:])
        mean_squares = sb.tile([P, P], F32, name="mean_squares")
        nc.gpsimd.memset(mean_squares[:], 0.0)
        nc.gpsimd.memset(window[0][:], 0.0)
        eps_cols = sb.tile([P, 2], F32, name="eps_cols", tag="eps_cols")
        nc.scalar.activation(eps_cols[:], mean_squares[:, 0:2], ACT.Identity, bias=EPS)

        acc_listed = sb.tile([P, SLOTS], F32, name="acc_listed")
        nc.vector.tensor_copy(acc_listed[:], acc_table[:].indirect(offsets[:]))

        x_codes = sb.tile([P, D], U32, name="x_codes", align_bytes=64)
        x_scales = sb.tile([P, D], U8, name="x_scales", align_bytes=64)
        x_cast = {}
        for t in (2, 3, 0, 1):
            x_cast[t] = sb.tile([P, 2, P, 2], BF16, name="x_cast%d" % t, tag="x_cast%d" % t, align_bytes=64)
            engine_copy = nc.vector.tensor_copy if t >= 2 else nc.scalar.copy
            engine_copy(x_cast[t][:], x_raw[t][:].rearrange("m (p u e) -> m u p e", u=2, e=2))
        x_woven = []

        def quantise_x(t):
            cols = slice(t * P, (t + 1) * P)
            nc.vector.quantize_mx(out=x_codes[:, cols].bitcast(E4M3), scales=x_scales[:, cols], in_=x_woven[t][:])

        for t in range(LANES):
            x_words = x_cast[t][:].rearrange("m u p e -> m (u p e)").bitcast(F32)
            x_ps = bank(t, "x_ps%d" % t)
            for u in range(2):
                nc.tensor.transpose(x_ps[:, u * P:(u + 1) * P], x_words[:, u * P:(u + 1) * P], ident[:])
            x_woven.append(sb.tile([P, LANES * P], BF16, name="x_woven%d" % t, align_bytes=64,
                                   tag="window1" if t == LANES - 1 else "x_woven%d" % t))
            nc.scalar.copy(
                x_woven[t][:].bitcast(F32).rearrange("p (m u) -> p m u", u=2),
                x_ps[:, 0:2 * P].rearrange("p (u m) -> p m u", u=2))
            if t < LANES - 1:
                quantise_x(t)

        acc_ps = bank(2, "acc_ps")
        for c in range(BLOCKS):
            nc.tensor.transpose(acc_ps[:, c * P:(c + 1) * P], acc_listed[:, c * P:(c + 1) * P], ident[:])
        acc_cols = sb.tile([P, P], F32, name="acc_cols")
        nc.scalar.copy(acc_cols[:].rearrange("p (m c) -> p m c", c=BLOCKS),
                       acc_ps[:].rearrange("p (c m) -> p m c", c=BLOCKS)[:, P - P // BLOCKS:P, :])

        acc_first = {}
        for c in (0, 2, 3):
            acc_first[c] = sb.tile([P, 1], F32, name="acc_col%d" % c, tag="acc_col%d" % c)
            nc.scalar.copy(acc_first[c][:], acc_ps[:, (c + 1) * P - 1:(c + 1) * P])

        g_codes = sb.tile([P, SLOTS], U32, name="g_codes", align_bytes=64, tag="window3")
        g_scales = sb.tile([P, SLOTS], U8, name="g_scales", align_bytes=64, tag="window2")
        dw_ps = [bank(4 + c, "dw_ps%d" % c) for c in range(BLOCKS)]

        def weave_g(c, engine_copy, woven):
            engine_copy(woven.rearrange("p (g i j) -> p g j i", i=4, j=LANES),
                        g_raw[c].rearrange("p j (g i) -> p g j i", i=4))

        def quantise_g(c, woven):
            cols = slice(c * P, (c + 1) * P)
            nc.vector.quantize_mx(out=g_codes[:, cols].bitcast(E5M2), scales=g_scales[:, cols], in_=woven)

        def product(c, first, end):
            cols = slice(c * P, (c + 1) * P)
            nc.tensor.matmul_mx(
                out=dw_ps[c][:, first:end], lhsT=g_codes[:, cols].bitcast(E5M2), lhsT_scale=g_scales[:, cols],
                rhs=x_codes[:, first:end].bitcast(E4M3), rhs_scale=x_scales[:, first:end], start=True, stop=True)

        g_woven0 = sb.tile([P, P * LANES], BF16, name="g_woven0", align_bytes=64, tag="x_woven2")
        weave_g(0, nc.vector.tensor_copy, g_woven0[:])
        g_woven1 = sb.tile([P, P * LANES], BF16, name="g_woven1", align_bytes=64, tag="x_cast3")
        weave_g(1, nc.scalar.copy, g_woven1[:])
        quantise_g(0, g_woven0[:])
        product(0, 0, D // 2)
        quantise_x(LANES - 1)
        product(0, D // 2, D)
        quantise_g(1, g_woven1[:])
        product(1, 0, D)


        def lane0_product(h):
            out = bank(h, "lane0_ps%d" % h)
            cols = slice(h * HALF, (h + 1) * HALF)
            nc.tensor.matmul_mx(
                out=out[:, :HALF], lhsT=x_codes[:, 0:P].bitcast(E4M3), lhsT_scale=x_scales[:, 0:P],
                rhs=g_codes[:, cols].bitcast(E5M2), rhs_scale=g_scales[:, cols], start=True, stop=True)
            return out

        lane0_ps = [lane0_product(0)]
        for c, tag in ((2, "g_raw0"), (3, "window1")):
            g_woven = sb.tile([P, P * LANES], BF16, name="g_woven%d" % c, align_bytes=64, tag=tag)
            weave_g(c, nc.vector.tensor_copy, g_woven[:])
            quantise_g(c, g_woven[:])
            product(c, 0, D)
        lane0_ps.append(lane0_product(1))

        dw_rows = {}

        def square(c, squares):
            nc.scalar.activation(squares, dw_ps[c][:], ACT.Square, scale=root_inv_d[:],
                                 accum_out=mean_squares[:, STAT + c:STAT + c + 1])

        def copy_rows(engine_copy, c, tag):
            dw_rows[c] = sb.tile([P, D - P], F32, name="dw_rows%d" % c, tag=tag)
            engine_copy(dw_rows[c][:], dw_ps[c][:, P:])

        def turn(out, t, c):
            nc.tensor.transpose(out, dw_rows[c][:, (t - 1) * P:t * P], ident[:])

        def turn_two(ps_tile, first, second):
            for in_half in range(2):
                for a, (t, h) in enumerate((first, second)):
                    turn(ps_tile[:, a * HALF + in_half * P:a * HALF + (in_half + 1) * P], t, 2 * h + in_half)

        def turn_half(ps_tile, t, h):
            for in_half in range(2):
                turn(ps_tile[:, in_half * P:(in_half + 1) * P], t, 2 * h + in_half)

        def roots(h):
            root = sb.tile([P, 2], F32, name="root%d" % h, tag="root%d" % h)
            for i in range(2):
                col = STAT + 2 * h + i
                nc.scalar.activation(root[:, i:i + 1], mean_squares[:, col:col + 1], ACT.Sqrt,
                                     bias=acc_first[2 * h + i][:] if 2 * h + i in acc_first else acc_cols[:, col:col + 1])
            return root

        def add_eps(h, root):
            denom = sb.tile([P, 2], F32, name="denom%d" % h, tag="denom%d" % h)
            nc.vector.tensor_tensor(denom[:], root[:], eps_cols[:], ALU.add)
            return denom

        def spread_factor(h, denom, b):
            factor = sb.tile([P, 2], F32, name="factor%d" % h, tag="factor%d" % h)
            nc.vector.reciprocal(factor[:], denom[:])
            out = bank(b, "factor_ps%d" % h)
            for i in range(2):
                nc.tensor.transpose(out[:, i * P:(i + 1) * P], factor[:, i:i + 1].to_broadcast([P, P]), ident[:])
            return out

        raw00 = sb.tile([P, HALF], F32, name="raw00", tag="raw00")
        nc.vector.tensor_copy(raw00[:], lane0_ps[0][:, :HALF])
        early_squares = sb.tile([P, 2, D], BF16, name="early_squares")
        for c in (0, 1):
            square(c, early_squares[:, c, :])
            copy_rows(nc.vector.tensor_copy, c, "dw_rows%d" % c)
        factor_ps0 = spread_factor(0, add_eps(0, roots(0)), 2)
        for t in (1, 2, 3):
            window[t] = sb.tile([P, TABLE], F32, name="window%d" % t, tag="window%d" % t, align_bytes=64)
            nc.gpsimd.memset(window[t][:], 0.0)

        late_squares = sb.tile([P, 2, D], BF16, name="late_squares", tag="acc_col0")
        square(2, late_squares[:, 0, :])
        copy_rows(nc.vector.tensor_copy, 2, "dw_rows2")
        square(3, late_squares[:, 1, :])
        root1 = roots(1)
        na_ps = bank(0, "na_ps")
        nc.tensor.matmul(na_ps[:, 0:P], mean_squares[:], ident[:], start=True, stop=False, is_transpose=True)
        nc.tensor.matmul(na_ps[:, 0:P], acc_cols[:], ident[:], start=False, stop=True, is_transpose=True)
        na_rows = sb.tile([P, P], F32, name="na_rows")
        nc.scalar.copy(na_rows[:], na_ps[:, 0:P])
        nc.sync.dma_start(out_1.rearrange("o (c i) -> (o c) i", c=BLOCKS), na_rows[STAT:P, :])
        copy_rows(nc.scalar.copy, 3, "acc_col3")

        row = shared.tile([P, SLOTS], F32, name="factor_row", offset=8 * GP_END - 2 * SLOTS)

        def scale(out, ps_half, h):
            nc.vector.tensor_tensor(out, ps_half, row[:, h * HALF:(h + 1) * HALF], ALU.mult)

        out_rows = out_0.rearrange("(m t) col -> m t col", t=LANES)

        def listed(t, h):
            return window[t][:].indirect(offsets[:, h * HALF // 16:(h + 1) * HALF // 16])

        def scalar_scatter(t, h, src):
            nc.scalar.activation(listed(t, h), src, ACT.Copy)

        def store_window(t):
            nc.sync.dma_start(out_rows[:, t, :], window[t][:])

        nc.vector.tensor_copy(row[:, :HALF], factor_ps0[:, :HALF])
        src0 = [sb.tile([P, HALF], F32, name="src0%d" % h, tag="acc_col2" if h == 0 else "src01") for h in range(2)]
        nc.vector.tensor_tensor(src0[0][:], factor_ps0[:, :HALF], raw00[:], ALU.mult)
        scalar_scatter(0, 0, src0[0][:])
        denom1 = add_eps(1, root1)
        src2 = sb.tile([P, SLOTS], F32, name="src2", tag="eps_cols")
        ps20_30 = bank(6, "ps20_30")
        turn_two(ps20_30, (2, 0), (3, 0))
        ps10 = bank(2, "ps10")
        turn_half(ps10, 1, 0)
        scale(src2[:, :HALF], ps20_30[:, :HALF], 0)
        factor_ps1 = spread_factor(1, denom1, 3)
        src3 = [sb.tile([P, HALF], F32, name="src30", tag="denom1"), sb.tile([P, HALF], F32, name="src31", tag="src31")]
        scale(src3[0][:], ps20_30[:, HALF:], 0)
        nc.vector.tensor_copy(row[:, HALF:], factor_ps1[:, :HALF])
        src1 = [sb.tile([P, HALF], F32, name="src1%d" % h, tag="factor1" if h == 0 else "src11") for h in range(2)]
        scale(src1[0][:], ps10[:, :HALF], 0)
        scale(src0[1][:], lane0_ps[1][:, :HALF], 1)
        scalar_scatter(0, 1, src0[1][:])
        store_window(0)
        nc.vector.tensor_copy(listed(1, 0), src1[0][:])

        ps11_21 = bank(6, "ps11_21")
        turn_two(ps11_21, (1, 1), (2, 1))
        ps31 = bank(1, "ps31")
        turn_half(ps31, 3, 1)
        scale(src1[1][:], ps11_21[:, :HALF], 1)
        scalar_scatter(1, 1, src1[1][:])
        store_window(1)
        scale(src2[:, HALF:], ps11_21[:, HALF:], 1)
        scale(src3[1][:], ps31[:, :HALF], 1)
        nc.vector.tensor_copy(window[2][:].indirect(offsets[:]), src2[:])
        store_window(2)

        parts = {"g": (0, GP_END), "v": (GP_END, V_END)}
        pairs = {}

        def new_pairs(key, tag):
            pairs[key] = sb.tile([P, 2, parts[key][1] - parts[key][0], 2], BF16, name="pairs_" + key, tag=tag)

        pairs["g"] = shared.tile([P, 2, GP_END, 2], BF16, name="pairs_g", offset=0)
        new_pairs("v", "eps_cols")

        def lane_out(key, t):
            return pairs[key][:, t // 2, :, t % 2]

        def lane_in(key, t):
            return window[t][:, parts[key][0]:parts[key][1]]

        for t in (0, 1):
            nc.gpsimd.tensor_scalar(lane_out("g", t), lane_in("g", t), 1.0, 1.0, ALU.mult, ALU.mult)

        words_out = out_2[0].rearrange("p col t -> p (col t)").bitcast(I32)
        y_scales = sb.tile([P, CHUNK], U8, name="y_scales", align_bytes=64)
        y_woven = {}
        y_codes = {}
        done = {}
        stores = ((0, CHUNK + HALF), (CHUNK + HALF, 3 * CHUNK), (3 * CHUNK, TABLE))

        def round_lane(engine_copy, key, t):
            engine_copy(lane_out(key, t), lane_in(key, t))

        def weave(engine_copy, key, first, end, tile_first, tile_end):
            base = parts[key][0]
            if tile_first not in y_woven:
                y_woven[tile_first] = sb.tile([P, (tile_end - tile_first) * LANES], BF16, name="y_woven%d" % tile_first, align_bytes=64)
            engine_copy(y_woven[tile_first][:, (first - tile_first) * LANES:(end - tile_first) * LANES].bitcast(F32).rearrange("p (col u) -> p col u", u=2),
                        pairs[key][:, :, first - base:end - base, :].bitcast(F32).rearrange("p u col e -> p col (u e)"))

        def quantise_y(first, end, tile_first):
            store_first, store_end = [store for store in stores if store[0] <= first < store[1]][0]
            if store_first not in y_codes:
                y_codes[store_first] = sb.tile([P, store_end - store_first], U32, name="y_codes%d" % store_first, align_bytes=64)
            nc.vector.quantize_mx(out=y_codes[store_first][:, first - store_first:end - store_first].bitcast(E4M3),
                                  scales=y_scales[4 * (first // CHUNK):, first % CHUNK:first % CHUNK + end - first],
                                  in_=y_woven[tile_first][:, (first - tile_first) * LANES:(end - tile_first) * LANES])
            done.setdefault(store_first, []).append(end - first)
            if sum(done[store_first]) == store_end - store_first:
                nc.sync.dma_start(words_out[:, store_first:store_end], y_codes[store_first][:].bitcast(I32))

        turned_pairs = {}

        def blocks(j):
            return (GROUPS[j][1] - GROUPS[j][0]) // P

        def turn_lanes(u, j, b):
            out = bank(b, "lanes_ps%d%d" % (u, j))
            for e in range(2):
                for blk in range(blocks(j)):
                    first = GROUPS[j][0] + blk * P
                    nc.tensor.transpose(out[:, (2 * blk + e) * P:(2 * blk + e + 1) * P], window[2 * u + e][:, first:first + P], ident[:])
            return out

        def round_turned(u, j, lanes_ps, engine_copy, pool, **place):
            turned_pairs[u, j] = pool.tile([P, blocks(j), P, 2], BF16, name="turned_pairs%d%d" % (u, j), **place)
            engine_copy(turned_pairs[u, j][:], lanes_ps[:, :2 * blocks(j) * P].rearrange("p (blk e m) -> p blk m e", e=2, m=P))

        def turn_back(u, j, out):
            words = turned_pairs[u, j][:].rearrange("p blk m e -> p (blk m e)").bitcast(F32)
            for blk in range(blocks(j)):
                first = (u * blocks(j) + blk) * P
                nc.tensor.transpose(out[:, first:first + P], words[:, blk * P:(blk + 1) * P], ident[:])

        def weave_turned(j, first, end):
            y_woven[first] = sb.tile([P, (end - first) * LANES], BF16, name="y_woven%d" % first, align_bytes=64)
            nc.scalar.copy(y_woven[first][:].bitcast(F32).rearrange("p (col u) -> p col u", u=2),
                           words_ps[j][:].rearrange("p (u col) -> p col u", u=2)[:, first - GROUPS[j][0]:end - GROUPS[j][0], :])

        early_ps = [turn_lanes(0, j, 2 + j) for j in range(len(GROUPS))]
        scalar_scatter(3, 0, src3[0][:])
        round_turned(0, 0, early_ps[0], nc.scalar.copy, sb, tag="denom1")
        scalar_scatter(3, 1, src3[1][:])
        store_window(3)
        words_ps = [bank(b, "words_ps%d" % b) for b in range(len(GROUPS))]
        turn_back(0, 0, words_ps[0])
        late_ps = [turn_lanes(1, j, 5 + j) for j in range(len(GROUPS))]
        round_turned(0, 1, early_ps[1], nc.vector.tensor_copy, shared, offset=8 * GP_END)
        round_turned(0, 2, early_ps[2], nc.scalar.copy, sb, tag="src31")
        for j in range(len(GROUPS)):
            round_turned(1, j, late_ps[j], nc.scalar.copy, sb)
            if j > 0:
                turn_back(0, j, words_ps[j])
            turn_back(1, j, words_ps[j])
        for key, t in (("v", 0), ("v", 1), ("g", 2), ("v", 2), ("g", 3), ("v", 3)):
            round_lane(nc.vector.tensor_copy, key, t)
        weave(nc.scalar.copy, "v", 2 * CHUNK, V_END, 2 * CHUNK, V_END)
        scalar_pieces = ((0,) + GROUPS[0], (1,) + GROUPS[1], (2, TABLE - 2 * P, TABLE - P), (2, TABLE - P, TABLE))
        for piece in scalar_pieces:
            weave_turned(*piece)
        weave(nc.vector.tensor_copy, "g", 0, CHUNK, 0, CHUNK)
        weave(nc.vector.tensor_copy, "g", CHUNK, GP_END, CHUNK, 2 * CHUNK)
        quantise_y(0, CHUNK, 0)
        weave(nc.vector.tensor_copy, "v", GP_END, 2 * CHUNK, CHUNK, 2 * CHUNK)
        quantise_y(CHUNK, CHUNK + HALF, CHUNK)
        quantise_y(CHUNK + HALF, 2 * CHUNK, CHUNK)
        quantise_y(2 * CHUNK, V_END, 2 * CHUNK)
        for j, first, end in scalar_pieces:
            quantise_y(first, end, first)

        scales_out = out_3[0].bitcast(I32).rearrange("(q r) (k c) -> q k r c", r=4, k=TABLE // CHUNK)
        for q in range(4):
            queue = nc.scalar if q % 2 else nc.sync
            queue.dma_start(scales_out[q], y_scales[32 * q:32 * q + 16, :].bitcast(I32))
